import numpy as np, ml_dtypes
CORES = [48,51,52,55]
N = 4
BF = ml_dtypes.bfloat16
def gentries(a):
    return np.ascontiguousarray(a.reshape(8, 16, -1).transpose(0, 2, 1)).reshape(8, -1)
def gtable(e):
    e = np.asarray(e); return np.ascontiguousarray(e.reshape(8, -1, 16).transpose(0, 2, 1)).reshape(128, -1).astype(np.int32)
V, C, S, L = 3072, 2048, 64, 256
RS, RP, Q, F = 4, 4, 2, 640
H = V - (N - 1) * S
I, J = np.arange(N)[:, None, None], np.arange(8)[None, :, None]
def mixed(rng, a):
    return np.take_along_axis(a, np.argsort(rng.random(a.shape), axis=-1), axis=-1)
def make(rng, npl=0, nq=0, own=None, power=1, tip=False):
    po = rng.random((N, 8, H))
    if tip: po[..., 0] = 2
    po = np.argsort(po, axis=-1)
    key = rng.random((N, 8, V)); key[I, J, po[..., :npl + nq]] = 9
    if own is not None: key[..., H:] += 5 * own[..., None]
    if tip: key[..., V - 1] = -2; key[..., 0] = -1
    U = H - npl - nq if npl + nq else V
    pool = np.argsort(key, axis=-1)[..., :U]
    m = rng.random((N, 8, C))
    if tip: m[..., 0] = -2; m[..., C - 1] = -1
    cp = np.argsort(m, axis=-1)
    mv = np.zeros((N, 8, C), np.int64); mv[I, J, cp[..., :npl]] = po[..., :npl]; mv[I, J, cp[..., npl:]] = pool[..., :C - npl][..., ::-1]
    u = np.sort((rng.random((N, 8, C, 16)) ** power * (U - 15)).astype(np.int64), axis=-1) + np.arange(16)
    va = np.take_along_axis(pool, u.reshape(N, 8, -1), axis=-1).reshape(N, 8, C, 16)
    eq = va == mv[..., None]; j = np.where(np.any(eq, axis=-1), np.argmax(eq, axis=-1), rng.integers(0, 16, (N, 8, C)))
    np.put_along_axis(va, j[..., None], mv[..., None], axis=-1)
    if tip:
        m = (rng.random((N, 8, C)) < 0.5) & ~np.any((va == 0) | (va == V - 1), axis=-1)
        for i, z in ((1, 0), (2, V - 1)):
            q = ((j + i) & 15)[..., None]
            np.put_along_axis(va, q, np.where(m[..., None], z, np.take_along_axis(va, q, axis=-1)), axis=-1)
    va = mixed(rng, va)
    p = rng.random((N, 8, L)); p[..., 0] = -1; p[..., 1] = 2
    nl = np.take_along_axis(cp[..., :L], np.argsort(p, axis=-1), axis=-1)
    o = mv.copy(); o[I, J, cp[..., :L + C // 16]] = V
    det = np.zeros((N, 8, V + 1), bool); det[I, J, o] = True
    w = rng.integers(0, 256, (N, 8, V)); w = np.where(det[..., :V], w, np.maximum(w, rng.integers(0, 256, (N, 8, V))))
    return {"x": rng.integers(0, 256, (N, 8, 16, V)), "w": w, "va": va, "k": rng.integers(0, 256, (N, 8, 16, C)), "s": rng.integers(0, 256, (N, 8, C)), "o": o, "nl": nl,
            "cp": cp, "mv": mv, "priv": po[..., :npl], "quiet": po[..., npl:npl + nq], "det": det[..., :V]}
def pack(a):
    return {"xv": np.ascontiguousarray(a["x"].reshape(N, 128, V)).astype(np.float32).astype(BF), "wv": a["w"].astype(np.int32), "va": np.stack([gtable(q.reshape(8, -1)) for q in a["va"]]),
            "kc": np.ascontiguousarray(a["k"].reshape(N, 128, C)).astype(np.float32).astype(BF), "sc": a["s"].astype(np.int32), "ov": a["o"].astype(np.int32), "nl": np.stack([gtable(q) for q in a["nl"]])}
def setup_inputs(rng):
    a = make(rng); a["nl"] = np.where(rng.random((N, 8, L)) < 0.03, C, a["nl"])
    return pack(a)
def setup_inputs_spread(rng):
    a = make(rng, power=2)
    a["x"] = (np.exp2(8 * rng.random((N, 8, 1, V))) * rng.random((N, 8, 16, V)) * (rng.random((N, 8, 1, V)) > 0.0625)).astype(np.int64)
    b = (np.exp2(8 * rng.random((N, 8, V)))).astype(np.int64) - 1; e = rng.integers(0, 256, (N, 8, V))
    a["w"] = np.where(a["det"], b, np.maximum(b, e))
    a["s"] = 256 - np.minimum(np.exp2(8 * rng.random((N, 8, C))).astype(np.int64), 256)
    a["k"] = (np.exp2(8 * rng.random((N, 8, 1, C))) * rng.random((N, 8, 16, C))).astype(np.int64)
    a["nl"] = np.where(rng.random((N, 8, L)) < rng.choice(np.array([0.0, 0.1, 0.5]), (N, 8, 1)), C, a["nl"])
    return pack(a)
def setup_inputs_ends(rng):
    n = 24; a = make(rng, n, 64, tip=True); qv, pv, c = a["quiet"], a["priv"], a["cp"][..., :n]
    a["x"] = 255 * rng.integers(0, 2, (N, 8, 16, V)); a["k"] = 255 * rng.integers(0, 2, (N, 8, 16, C))
    share = np.array([0.06, 0.12, 0.5])[(np.arange(N)[:, None] + np.arange(8)[None, :]) % 3][..., None]
    a["w"] = 255 * (rng.random((N, 8, V)) >= share).astype(np.int64); a["s"] = 255 * (rng.random((N, 8, C)) < 0.75).astype(np.int64)
    a["x"][I, J, :, qv[..., :32]] = 255; a["x"][I, J, :, qv[..., 32:]] = 0
    a["w"][I, J, qv] = 255; a["w"][I, J, pv] = 0; a["s"][I, J, c] = 255
    z = np.argsort(rng.random((N, 8, n, 32)), axis=-1)
    hi = np.take_along_axis(np.broadcast_to(qv[..., None, :32], z.shape), z, axis=-1)[..., :15]; lo = np.take_along_axis(np.broadcast_to(qv[..., None, 32:], z.shape), z, axis=-1)[..., :15]
    sel = (np.arange(n) % 3)[:, None]
    row = np.where(sel == 0, lo, np.where(sel == 1, hi, np.where(np.arange(15) < 8, hi, lo)))
    a["va"][I, J, c] = mixed(rng, np.concatenate([pv[..., None], row], axis=-1))
    kept = np.any(a["nl"][..., None] == c[..., None, :], axis=-1)
    void = np.where((np.arange(8) & 3) == 2, 0.5, 0.06)[None, :, None]
    a["nl"] = np.where((rng.random((N, 8, L)) < void) & ~kept, C, a["nl"])
    return pack(a)
def marked(rng, a, g):
    va = a["va"][N - 1, g]; a["o"][N - 1, g] = V; sp = H + rng.permutation(S); cl = rng.permutation(C); n = C // 16
    va[cl[2 * n:], rng.integers(0, 16, C - 2 * n)] = sp[0]
    va[cl[:n]] = sp[17:][np.argsort(rng.random((n, S - 17)), axis=1)[:, :16]]
    row = np.where(np.arange(16)[None, :] < rng.integers(1, 17, n)[:, None], sp[1:17][np.argsort(rng.random((n, 16)), axis=1)], va[cl[n:2 * n]])
    va[cl[n:2 * n]] = mixed(rng, row)
    xg = a["x"][N - 1, g]; q = sp[1:17]
    xg[:, q] = a["x"][N - 2, (1 - g) & 7][:, q]; xg[15, q] = (xg[15, q] + rng.integers(1, 256, 16)) & 255
def setup_inputs_corners(rng):
    ty = (np.arange(8)[None, :] + 3 * np.arange(N)[:, None]) & 7
    a = make(rng, L, 32, own=(((ty >= 1) & (ty <= 3)) | ((ty == 0) & (np.arange(N)[:, None] >= N - 2))).astype(np.int64)); va, w, s, o, nl = a["va"], a["w"], a["s"], a["o"], a["nl"]
    cls = np.arange(L) & 15; half = cls >= 8
    for r in range(N):
        for g in range(8):
            t = int(ty[r, g]); c = a["cp"][r, g]; pv = a["priv"][r, g]; qv = a["quiet"][r, g]
            if t == 0:
                nl[r, g] = C
                if r == N - 2: o[r, g] = a["mv"][r, g]
                if r == N - 1: marked(rng, a, g)
            elif t <= 3:
                oth = np.argsort(rng.random((L, L)) + 2 * (half[:, None] != half[None, :]) + 4 * np.eye(L), axis=1)[:, :15]
                q = np.argsort(rng.random((L, 31)), axis=1)[:, :15]
                row = np.where(np.arange(15)[None, :] < cls[:, None], pv[oth], qv[q])
                xg = a["x"][r, g]; kg = a["k"][r, g]; dead = pv[8:8 + Q]
                xg[:, qv[:16]] = 255
                row[16] = np.concatenate([dead, qv[:15 - Q]]); row[32] = np.concatenate([dead[:1], qv[:14]])
                old = np.zeros(16, np.int64)
                for i in range(RP):
                    z = 48 + 16 * i; still = rng.permutation(qv[:31])[:(14 - Q if i else 15)]
                    row[z] = np.concatenate([dead, pv[z - 16:z - 15], still]) if i else still
                    new = rng.integers(0, 256, 16)
                    if i == RP - 2: new[:15] = 0; new[15] = rng.integers(1, 256)
                    if i == RP - 1: new[:] = 0
                    kg[:, c[z]] = (new + old + np.add.reduce(xg[:, still], axis=1)) & 255
                    old = new
                z = 48 + 16 * (RP - 2); row[112] = np.concatenate([pv[z:z + 1], rng.permutation(qv[:31])[:14]])
                row = mixed(rng, row)
                va[r, g, c[:L]] = np.concatenate([pv[:, None], row], axis=1)
                w[r, g] = np.maximum(w[r, g], 1); w[r, g, pv] = 0; w[r, g, qv] = 255; s[r, g, c[:L]] = rng.integers(128, 256, L)
                if t == 2:
                    e = int(c[C - 1]); i = int(np.argmax(va[r, g, e] == o[r, g, e]))
                    va[r, g, e, i] = pv[0]; va[r, g, e, (i + 1) & 15] = qv[31]; o[r, g, e] = pv[0]; w[r, g, qv[31]] = 0; s[r, g, e] = 255
                if t == 3: nl[r, g, int(rng.integers(0, L))] = C
            elif t == 4:
                if r & 1: nl[r, g, :L - 1] = C
                else: nl[r, g, 1:] = C
            elif t == 5: o[r, g] = V
            elif t == 6: s[r, g, c[:L]] = 255 * rng.integers(0, 2, L)
    return pack(a)
def counted(rng, a, r, g):
    b = r & 3; z = (r + 1 + (r >> 2)) & 3; last = (RP - 1) * F
    va = a["va"][r, g]; o = a["o"][r, g]; a["nl"][r, g] = C; o[:] = V
    p = rng.permutation(F); m = np.concatenate([p[:L + b], np.arange(F, last), last + rng.permutation(C - last)[:z]])
    va[m, rng.integers(0, 16, len(m))] = H + 1 - (r & 1)
    if r & 1: va[p[F - 1], 0] = H + 1; o[p[F - 1]] = H + 1
def crossed(rng, a, r, g):
    va = a["va"][r, g]; w = a["w"][r, g]; s = a["s"][r, g]; o = a["o"][r, g]; nl = a["nl"][r, g]; c = a["cp"][r, g]; d = N - 1 - r
    w[:] = np.maximum(w, 1); s[c[:L]] = np.maximum(s[c[:L]], 1)
    if d:
        v = H + (d - 1) * S + np.arange(S); va[c[:S], 0] = v; w[v] = 0
        nl[np.isin(nl, c[S:L])] = C
        if r & 1:
            e = int(c[C - 1]); va[e, int(np.argmax(va[e] == o[e]))] = H + 1; o[e] = H + 1
        return
    v = a["mv"][r, g, c[:L]]; u = a["quiet"][r, g]; ok = np.ones(H, bool); ok[v] = False; ok[u] = False
    rest = np.nonzero(ok)[0]
    va[c[:L]] = np.concatenate([v[:, None], rest[np.argsort(rng.random((L, len(rest))), axis=1)[:, :15]]], axis=1)
    w[v] = 0; nl[np.isin(nl, c[L - 4:L])] = C
    e = c[C - 4:]; u = u[8:22]; xg = a["x"][r, g]
    a["k"][r, g][:, e] = (xg[:, o[e]] + np.add.reduce(xg[:, u], axis=1)[:, None]) & 255
    va[e] = mixed(rng, np.concatenate([o[e][:, None], (V - 1 - np.arange(4))[:, None], np.broadcast_to(u, (4, 14))], axis=1))
def setup_inputs_crowd(rng):
    ty = (np.arange(8)[None, :] + np.arange(N)[:, None]) & 3
    a = make(rng, 0, 24, own=(ty == 3).astype(np.int64)); va, w, s, o = a["va"], a["w"], a["s"], a["o"]
    for r in range(N):
        for g in range(8):
            t = int(ty[r, g])
            if t == 3:
                if ((r + g) & 7) == N - 1: crossed(rng, a, r, g)
                else: counted(rng, a, r, g)
                continue
            c = a["nl"][r, g]; qv = a["quiet"][r, g]; i = np.arange(L)
            n = rng.integers(0, 4, L) if t == 2 else np.zeros(L, np.int64)
            p = rng.integers(0, 15, L); q = p + 1 + (rng.random(L) * (15 - p)).astype(np.int64)
            row = va[r, g, c]; keep = row.copy(); row[i, p] = qv[2 * n]; row[i, q] = qv[2 * n + 1]
            if t == 1: z = 0 if r & 1 else L - 1; row[z] = keep[z]
            va[r, g, c] = row; w[r, g] = np.maximum(w[r, g], 1); w[r, g, qv] = 0; s[r, g, c] = np.maximum(s[r, g, c], 1)
            e = int(a["cp"][r, g, C - 1]); h = int(np.argmax(va[r, g, e] == o[r, g, e]))
            va[r, g, e, h] = qv[0]
            if h == 15: h = 14; va[r, g, e, h] = qv[0]
            va[r, g, e, h + 1] = qv[1]; o[r, g, e] = qv[0]; s[r, g, e] = max(int(s[r, g, e]), 1)
    return pack(a)
def setup_inputs_calm(rng):
    a = make(rng); base = np.array([0, 1, 100, 215])[(np.arange(N)[:, None] + np.arange(8)[None, :]) & 3][..., None]
    a["w"] = base + ((a["w"] * 41) >> 8)
    low = np.min(np.take_along_axis(a["w"], a["va"].reshape(N, 8, -1), axis=-1).reshape(N, 8, C, 16), axis=-1)
    a["s"] = np.minimum(low + rng.integers(0, 4, (N, 8, C)), 255)
    return pack(a)
def check_inputs(d):
    bad = []; u = {}
    for k, lo, hi in (("xv", 0, 255), ("wv", 0, 255), ("va", 0, V - 1), ("kc", 0, 255), ("sc", 0, 255), ("ov", 0, V), ("nl", 0, C)):
        v = np.nan_to_num(np.asarray(d[k]).astype(np.float64), nan=-1.0, posinf=1e9, neginf=-1e9)
        if not np.all((v >= lo) & (v <= hi) & (v == np.floor(v))): bad.append("range of " + k)
        u[k] = np.clip(v, lo, hi).astype(np.int64)
    a = np.stack([gentries(q) for q in u["va"]]).reshape(N, 8, C, 16); n = np.stack([gentries(q) for q in u["nl"]]); o = u["ov"]
    if np.any(np.diff(np.sort(a, axis=-1), axis=-1) == 0): bad.append("va: the variables of a constraint differ")
    if np.any((o < V) & ~np.any(a == o[..., None], axis=-1)): bad.append("ov: an output is a variable of its constraint")
    for k, v, top in (("ov: outputs differ", o, V), ("nl: constraints in lanes differ", n, C)):
        z = np.sort(v, axis=-1)
        if np.any((z[..., 1:] == z[..., :-1]) & (z[..., 1:] < top)): bad.append(k)
    if np.any((n < C) & (np.take_along_axis(o, np.minimum(n, C - 1), axis=-1) < V)): bad.append("nl: constraints in lanes have no output")
    return bad
def meet(x, w, de, o, ch):
    me = np.arange(N)
    for d in range(1, N):
        pr = me ^ d; pg = (d - np.arange(8)) & 7; at = H + (d - 1) * S; cs = slice(at, at + S)
        mx, mw, md = x[..., cs].copy(), w[..., cs].copy(), de[..., cs] < C
        px, pw, pd = mx[pr][:, pg], mw[pr][:, pg], md[pr][:, pg]
        high = (me > pr)[:, None, None]
        lose = np.where(md & pd, np.where(mw == pw, high, mw < pw), np.where(md | pd, pd, high))
        r, g, i = np.nonzero(lose & md); o[r, g, de[r, g, at + i]] = V; de[r, g, at + i] = C
        ch[..., cs] |= lose & np.any(mx != px, axis=2)
        x[..., cs] = np.where(lose[:, :, None, :], px, mx); w[..., cs] = np.where(lose, pw, mw)
def raised(ch, a):
    return np.any(np.take_along_axis(ch, a.reshape(N, 8, -1), axis=-1).reshape(N, 8, C, 16), axis=-1)
def reference(xv, wv, va, kc, sc, ov, nl):
    x = xv.astype(np.float32).astype(np.int64).reshape(N, 8, 16, V); k = kc.astype(np.float32).astype(np.int64).reshape(N, 8, 16, C)
    w = wv.astype(np.int64); s = sc.astype(np.int64); o = ov.astype(np.int64)
    a = np.stack([gentries(q) for q in va]).astype(np.int64).reshape(N, 8, C, 16); ln = np.stack([gentries(q) for q in nl]).astype(np.int64)
    de = np.full((N, 8, V + 1), C, np.int64); de[I, J, o] = np.arange(C); de[..., V] = C
    fl = np.zeros((N, 8, C), bool)
    for step in range(RS):
        c = np.minimum(ln, C - 1); rows = a[I, J, c]; ww = w[I[..., None], J[..., None], rows]
        kk = np.argmin(ww, axis=-1); oo = np.take_along_axis(rows, kk[..., None], axis=-1)[..., 0]
        srt = np.sort(ww, axis=-1); st = s[I, J, c]
        live = (ln < C) & (srt[..., 0] < st); ln = np.where(live, ln, C)
        first = np.full((N, 8, V), L, np.int64); np.minimum.at(first, (I, J, oo), np.where(live, np.arange(L), L))
        act = live & (first[I, J, oo] == np.arange(L)); nw = np.minimum(st, srt[..., 1])
        r, g, j = np.nonzero(act); cc = c[r, g, j]; v = oo[r, g, j]; e = de[r, g, v]
        de[r, g, v] = cc; o[r, g, cc] = v; w[r, g, v] = nw[r, g, j]; x[r, g, :, v] = 256; fl[r, g, cc] = True
        q = e < C; o[r[q], g[q], e[q]] = V
        ln[r, g, j] = e
        ch = np.zeros((N, 8, V), bool); meet(x, w, de, o, ch); fl |= raised(ch, a)
    for t in range(RP):
        order = np.roll(np.arange(C), -t * F); ff = fl[:, :, order]
        r, g, i = np.nonzero(ff & (np.add.accumulate(ff.astype(np.int64), axis=-1) <= L)); c = order[i]
        has = o[r, g, c] < V
        fl[r[~has], g[~has], c[~has]] = False
        r, g, c = r[has], g[has], c[has]; v = o[r, g, c]; rows = a[r, g, c]; own = rows == v[:, None]
        stale = np.add.reduce(((x[r[:, None], g[:, None], 0, rows] == 256) & ~own).astype(np.int64), axis=1)
        go = stale <= Q; r, g, c, v, rows, own = r[go], g[go], c[go], v[go], rows[go], own[go]
        xs = x[r[:, None], g[:, None], :, rows]
        nx = (k[r, g, :, c] - np.add.reduce(np.where(own[:, :, None], 0, xs), axis=1)) & 255
        nw = np.minimum(s[r, g, c], np.min(np.where(own, 256, w[r[:, None], g[:, None], rows]), axis=1))
        ch = np.zeros((N, 8, V), bool); ch[r, g, v] = np.any(x[r, g, :, v] != nx, axis=1)
        x[r, g, :, v] = nx; w[r, g, v] = nw; fl[r, g, c] = False
        meet(x, w, de, o, ch); fl |= raised(ch, a)
    return {"y": x.reshape(N, 128, V).astype(np.float32).astype(BF), "yw": w.astype(np.float32), "yo": o.astype(np.float32), "yf": fl.astype(np.float32)}

@@ -1,0 +1,813 @@
+from concourse.bass import DstId, RemoteDMATransfer
+from concourse.mybir import AluOpType as AL, AxisListType as AX, ActivationFunctionType as AF
+
+V, C, S, N = 3072, 2048, 64, 4
+H = V - 3 * S
+NV, DV0, VW, CWD = 3072, 3088, 3344, 2304
+STALE = 4096.0
+BIG = 3.0e7
+B16, F32, I32, U16 = "bfloat16", "float32", "int32", "uint16"
+_sb = {
+    "VA": (CWD, I32), "VAP": (C, U16), "A": (VW, B16), "X": (VW, B16), "KK": (CWD, B16), "CW": (CWD, B16), "CW2": (CWD, B16), "OW": (CWD, B16),
+    "BITS": (DV0, B16), "GR": (32768, B16), "CODE": (V, B16), "MK": (C, F32), "MB": (C, B16), "MT": (1024, I32), "EQ": (256, B16),
+    "IO": (256, F32), "ZERO": (256, B16), "GI": (128, F32), "JI": (256, B16), "J1": (256, F32), "II": (128, I32), "CF": (160, F32), "IC": (16, F32),
+    "JW": (128, F32), "TMP": (256, F32), "TMP2": (256, F32), "MAT": (60 * 128, B16), "SM": (256, B16), "ZW": (4 * 160, B16), "IDF": (128, F32), "G8": (8, F32),
+    "MASKR": (512, F32), "RSB": (256, F32), "RS1": (128, B16), "ELX": (48, U16), "BASEW": (64, F32), "JT": (32, F32),
+    "OVI": (128, I32), "OV2": (384, I32), "OVL": (128, U16), "OVB": (256, B16), "WI": (192, I32), "WB": (192, B16), "SI": (128, I32), "SBF": (128, B16), "NLI": (16, I32),
+    "LN": (32 * 5, U16), "VARS": (256, U16), "SR": (256, B16), "M1": (256, F32), "YY": (256, F32), "M2": (256, F32),
+    "TI": (64, I32), "OI": (16, I32), "TF": (256, F32), "SCT": (48, F32), "ACT": (16, F32), "NM": (32, F32), "DO": (16, F32), "EXP": (512, F32), "DOX": (256, F32),
+    "L1": (16, U16), "L2": (64, U16), "BE": (256, B16), "BO": (256, B16), "GO": (256, B16), "WL": (32, B16), "VT": (256, B16), "VAL": (1024, B16), "C4K": (256, B16),
+    "ONES": (256, B16), "LA": (192 * 5, B16), "LS": (192, B16), "TT": (192 * 4, B16), "SQ": (192 * 4, B16), "XR0": (192, B16), "DX": (192, B16), "NE": (192, B16), "GM": (192, B16),
+    "T192": (384, F32), "U12": (32, F32), "LO128": (128, U16),
+    "F": (128, B16), "FF": (128, F32), "IP": (128, B16), "CR": (128, B16), "CMP": (2048, B16), "POS": (144, F32), "LB": (16, U16), "BC": (16, B16), "OH": (256, B16), "CL": (16, U16),
+    "ORG": (256, F32), "CG": (256, B16), "KR": (256, B16), "XO": (256, B16), "AO": (256, B16), "LO": (16, U16), "MI": (512, I32), "GG": (256, B16), "WT": (256, B16),
+    "NEQ": (256, B16), "T1": (256, B16), "NXG": (256, B16), "XW": (256, B16), "RH": (128, B16),
+}
+SCRATCH = {k: ("sbuf", [128, w], d) for k, (w, d) in _sb.items()}
+SCRATCH["SB"] = ("sbuf", [128, 3, 128], B16)
+for _i in range(4):
+    SCRATCH["LP%d" % _i] = ("sbuf", [128, 384], B16)
+for _i in range(8):
+    SCRATCH["P%d" % _i] = ("psum", [128, 512], F32)
+SEMAPHORES = ["cv", "cs", "cp", "cg"] + ["d%d" % i for i in range(40)] + ["ar%d" % i for i in range(9)] + ["ls%d" % i for i in range(9)]
+ALIAS = {"TH": ("GR", 4096, 3072), "DEW": ("GR", 8192, DV0 + C), "DVAL": ("GR", 13568, C), "AB": ("GR", 0, C), "GV": ("GR", C, C), "YB": ("BITS", 0, V)}
+SAMEQ = True
+
+
+def rank_program(g, core, T, topo):
+    rank = T.rank_of(core)
+    if rank is None:
+        return
+    Q = {"v": g.vector, "s": g.scalar, "p": g.tensor, "g": g, "y": g.sync}
+    CS = {"v": "cv", "s": "cs", "p": "cp", "g": "cg"}
+    cnt, waited, rec, nd = {}, {}, {}, [0]
+
+    def wait(q, sem, val):
+        if waited.get((q, sem), 0) < val:
+            Q[q].wait_ge(T.sem[sem], val)
+            waited[(q, sem)] = val
+
+    def note(regs, sem, val, wr, beside=None):
+        for (b, lo, hi) in regs:
+            d = rec.setdefault(b, {})
+            if wr and beside is None:
+                for k in [k for k in d if lo <= k[0] and k[1] <= hi]:
+                    del d[k]
+            d[(lo, hi, sem, wr)] = val
+
+    def op(q, fn, outs, ins, sem=None, inc=1, beside=None):
+        own = sem or CS[q]
+        wr = [r for o in outs for r in o[1]]
+        rd = [r for o in outs for r in o[2]] + [r for o in ins if isinstance(o, tuple) for r in o[1] + o[2]]
+        need = {}
+        for regs, w in ((wr, True), (rd, False)):
+            for (b, lo, hi) in regs:
+                ps = b[0] == "P" and b[1:].isdigit()
+                for (l2, h2, s2, w2), val in rec.get(b, {}).items():
+                    if s2 == own:
+                        hit = q != "p" and l2 < hi and lo < h2 and ((w2 and not w) or (SAMEQ and (w or w2)))
+                    else:
+                        hit = ps or (l2 < hi and lo < h2 and (w or w2))
+                    if hit and s2 != beside and val > need.get(s2, 0):
+                        need[s2] = val
+        for s2, val in need.items():
+            wait(q, s2, val)
+        cnt[own] = cnt.get(own, 0) + inc
+        ins_ = fn()
+        if ins_ is not None:
+            ins_.then_inc(T.sem[own], inc)
+        note(rd, own, cnt[own], False)
+        note(wr, own, cnt[own], True, beside)
+
+    def s(name, lo=0, hi=None, step=1, p=None):
+        if name in ALIAS:
+            b, o, w = ALIAS[name]
+            name, lo, hi = b, o + lo, o + (w if hi is None else hi)
+        t = T[name]
+        hi = t.shape[1] if hi is None else hi
+        ps = slice(0, 128) if p is None else p
+        return (t[ps, lo:hi:step] if step > 1 else t[ps, lo:hi], [(name, lo, hi)], [])
+
+    def w_(name, lo, n):
+        return s(name, lo, lo + n)
+
+    def ind(win, off):
+        return (win[0].indirect(off[0]), win[1], off[1])
+
+    def a(x):
+        return x[0] if isinstance(x, tuple) else x
+
+    def cp(o, i):
+        op("v", lambda: g.vector.tensor_copy(o[0], i[0]), [o], [i])
+
+    def tt(o, x, y, f):
+        op("v", lambda: g.vector.tensor_tensor(o[0], x[0], y[0], f), [o], [x, y])
+
+    def ts(o, x, s1, f0, s2=None, f1=None):
+        if f1 is None:
+            op("v", lambda: g.vector.tensor_scalar(o[0], x[0], a(s1), None, f0), [o], [x, s1])
+        else:
+            op("v", lambda: g.vector.tensor_scalar(o[0], x[0], a(s1), a(s2), f0, f1), [o], [x, s1, s2])
+
+    def ms(o, c):
+        op("v", lambda: g.vector.memset(o[0], c), [o], [])
+
+    def scan(o, d0, d1, init, f0, f1):
+        op("v", lambda: g.vector.tensor_tensor_scan(o[0], d0[0], d1[0], a(init), f0, f1), [o], [d0, d1, init])
+
+    def red(o, i):
+        op("v", lambda: g.vector.tensor_reduce(o[0], i[0], AX.X, AL.add), [o], [i])
+
+    def act(o, i, f=AF.Copy, bias=0.0, scale=1.0):
+        op("s", lambda: g.scalar.activation(o[0], i[0], f, bias=a(bias), scale=a(scale)), [o], [i, bias, scale])
+
+    def gat(e, o, i):
+        cp(o, i) if e == "v" else act(o, i)
+
+    tiles = {}
+
+    def mm(o, l, r, st=True, sp=True, tile=None):
+        bank = o[1][0][0]
+        if bank in tiles and tiles[bank][0] != tile:
+            wait("p", "cp", tiles[bank][1])
+        op("p", lambda: g.tensor.matmul(o[0], l[0], r[0], st, sp), [o], [l, r])
+        tiles[bank] = (tile, cnt["cp"])
+
+    def mms(lst, st=True, sp=True):
+        for n, (o, l, r) in enumerate(lst):
+            mm(o, l, r, st and n == 0, sp and n == len(lst) - 1)
+
+    def iota(o, pat, base, cm, flt=True):
+        if flt:
+            op("g", lambda: g.iota(o[0], pat, base, cm, allow_small_or_imprecise_dtypes=True), [o], [])
+        else:
+            op("g", lambda: g.iota(o[0], pat, base, cm), [o], [])
+
+    def dma(q, o, i, beside=False):
+        sem = "d%d" % nd[0]
+        nd[0] += 1
+        op(q, lambda: Q[q].dma_start(o[0], i[0]), [o], [i], sem=sem, inc=16, beside="d%d" % (nd[0] - 2) if beside else None)
+
+    def ext(ap):
+        return (ap, [], [])
+
+    def send(m, srcs, land, base, w):
+        trs, tot = [], 0
+        for d in (1, 2, 3):
+            dst = T.cores[rank ^ d]
+            rid, pid, _ = topo.addr(dst)
+            en = topo.engines(core, dst)
+            k = len(en) // 4
+            mask = sum(1 << e for e in en[k * (d - 1):k * d])
+            tot += k
+            trs.append(RemoteDMATransfer(dst_ids=[DstId(rid=rid, pnc=pid)], dma_engine_mask=mask, remote_sem=T.sem["ar%d" % m],
+                                         src=srcs[d - 1][0], dst=T[land][:, base + (d - 1) * w:base + d * w]))
+
+        def go():
+            g.remote_dma_fused(trs, local_sem=T.sem["ls%d" % m])
+        op("g", go, [], srcs, sem="ls%d" % m, inc=tot)
+        cnt["ar%d" % m] = tot
+        note([(land, base, base + 3 * w)], "ar%d" % m, tot, True)
+
+    high = [rank > (rank ^ d) for d in (1, 2, 3)]
+    cols, mats, sms = {}, {}, {}
+
+    def col(n):
+        if n not in cols:
+            cols[n] = len(cols)
+        return w_("CF", cols[n], 1)
+
+    def ic(i):
+        return w_("IC", i, 1)
+
+    def M(n):
+        if n not in mats:
+            mats[n] = len(mats)
+        return w_("MAT", mats[n] * 128, 128)
+
+    def sm(n, w=8):
+        if n not in sms:
+            sms[n] = (sum(x[1] for x in sms.values()), w)
+        return w_("SM", sms[n][0], sms[n][1])
+
+    def shift(k):
+        return s("ZW", 16 - k, 144 - k)
+
+    def slide(z, r):
+        return w_("ZW", 160 * z + 15 - r, 128)
+
+    def lin(n, terms, e="s"):
+        for k, (i, w) in enumerate(terms):
+            o = col(n if k == len(terms) - 1 else n + str(k))
+            if e == "s":
+                act(o, ic(i), AF.Identity, bias=col(n + str(k - 1)) if k else 0.0, scale=float(w))
+            else:
+                ts(o, ic(i), float(w), AL.mult, col(n + str(k - 1)) if k else 0.0, AL.add)
+
+    def sel(o, i, pat, cmp, fill, base, cm=1):
+        op("g", lambda: g.affine_select(o[0], i[0], pat, cmp, fill, base, cm), [o], [i])
+
+    def terms(o, lst, first=True):
+        n = o[1][0][2] - o[1][0][1]
+        for (i, j, w) in lst:
+            pat = [[-16, 8]] if n == 8 else [[-16, n // 16], [0 if j is None else 256, 16]]
+            sel(o, s("ZERO", 0, n) if first else o, pat, AL.not_equal, float(w), -i - 256 * (j or 0))
+            first = False
+
+    row = lambda i: slice(i, 128, 16)
+    AREP, XREP = s("A", H, V), s("X", H, V)
+    AW, XW_ = s("A"), s("X")
+    IO128, ID, G8, BD = s("IO", 0, 128), shift(0), s("G8"), M("BD")
+
+    dma("y", s("OVI"), ext(T.ov[:]))
+    dma("s", s("VA", 0, C), ext(T.va[:]))
+    dma("y", s("NLI"), ext(T.nl[:]))
+    dma("y", s("WI"), ext(T.wv[:]))
+    dma("y", s("SI"), ext(T.sc[:]))
+    dma("y", XREP, ext(T.xv[:, H:V]))
+    iota(s("II", 0, 1), [[0, 1]], 0, 1, False)
+    iota(s("IO"), [[1, 256]], 0, 0)
+    iota(s("JW"), [[16, 128]], 0, 1)
+    iota(s("II", 16, 48), [[16, 2], [1, 2], [2, 8]], 0, 0, False)
+    iota(s("II", 48, 56), [[16, 8]], 15, 0, False)
+    iota(s("DEW", V, DV0 + C), [[0, DV0 + C - V]], 0, 0)
+    iota(s("ONES"), [[0, 256]], 1, 0)
+    iota(s("ZERO"), [[0, 256]], 0, 0)
+    sel(s("ZW", 0, 160), s("ZERO", 0, 160), [[-1, 160]], AL.not_equal, 1.0, 16)
+    iota(M("SELK"), [[0, 8], [4096, 16]], 2048, 0)
+    sel(M("SELK"), M("SELK"), [[-16, 8], [0, 16]], AL.is_equal, 0.0, -6)
+    terms(M("SELK"), [(0, None, 65536), (4, None, 256), (5, None, 1)], False)
+    sel(s("RSB"), s("ZERO"), [[0, 16], [1, 16]], AL.not_equal, BIG, 0, 0)
+    sel(G8, s("ONES", 0, 8), [[-16, 8]], AL.is_ge, 0.0, 0)
+    sel(G8, G8, [[16, 8]], AL.is_ge, 0.0, 15, -1)
+    SELC = sm("SELC", 24)
+    SELW = w_("SM", 8, 8)
+    terms(w_("SM", 0, 8), [(0, None, 65536)])
+    terms(SELW, [(0, None, 1)])
+    terms(w_("SM", 16, 8), [(4, None, 256), (5, None, 1)])
+    sel(s("IDF"), s("ZERO", 0, 128), [[-1, 128]], AL.not_equal, 1.0, 0)
+    ms(s("DEW", 0, V), 0.0)
+    act(s("CODE", 0, H), s("DEW", 0, H))
+    ms(s("TMP", 0, 8), 2.0)
+    ms(s("TMP", 8, 136), 0.0)
+    ts(s("II", 1, 2), s("II", 0, 1), 15, AL.bitwise_and)
+    ts(s("II", 2, 3), s("II", 0, 1), 112, AL.bitwise_and)
+    ts(s("II", 3, 4), s("II", 0, 1), 16, AL.bitwise_and)
+    for n in ("p", "i", "g16", "odd"):
+        col(n)
+    cp(s("CF", 0, 4), s("II", 0, 4))
+    ms(s("VA", C, CWD), NV)
+    ts(s("IC"), s("IO", 0, 16), col("i"), AL.is_equal)
+    ts(s("BITS", 0, 1), col("i"), 12.0, AL.is_lt)
+    for n in range(8):
+        col("w5_%d" % n)
+    for n in range(4):
+        col("w4_%d" % n)
+    lin("h5", [(5, 0.5)], "v")
+    lin("h4", [(4, 0.5)], "v")
+    ts(s("TF", 0, 16), s("IC"), -2.0, AL.mult, 1.0, AL.add)
+    lin("ca", [(0, 255), (4, -8), (6, 1), (7, 1)], "v")
+    scan(w_("CF", cols["w5_0"], 8), s("TMP", 0, 8), s("TMP", 8, 16), col("h5"), AL.mult, AL.add)
+    scan(w_("CF", cols["w4_0"], 4), s("TMP", 0, 4), s("TMP", 8, 12), col("h4"), AL.mult, AL.add)
+    ts(s("A", 0, 256), s("IO"), ic(5), AL.mult, col("ca"), AL.add)
+    ts(col("n0"), ic(0), -1.0, AL.mult, 1.0, AL.add)
+
+    def bits(bs):
+        for b in bs:
+            n = 1 << b
+            w = min(n, DV0 - n)
+            act(w_("BITS", n, w), s("BITS", 0, w), scale=w_("TF", b, 1))
+    bits(range(10))
+    for k in range(4):
+        n = 256 << k
+        w = min(n, VW - n)
+        ts(w_("A", n, w), s("A", 0, w), col("w4_%d" % k), AL.add)
+    act(s("CW"), s("A", 0, CWD), scale=col("n0"))
+    cp(s("WB"), s("WI"))
+    cp(s("DVAL", 0, 16), s("A", 0, C, 128))
+    ts(s("JW"), s("JW"), col("g16"), AL.subtract)
+    dma("y", s("A", 0, V, p=row(0)), s("WB"))
+    bits(range(10, 12))
+    act(s("MASKR", 0, 16), s("IC"))
+    for k in range(5):
+        act(w_("MASKR", 16 << k, 16 << k), s("MASKR", 0, 16 << k))
+    for k in range(7):
+        ts(s("DVAL", 16 << k, 32 << k), s("DVAL", 0, 16 << k), col("w5_%d" % k), AL.add)
+    ts(s("TMP", 128, 256), s("OVI"), float(V), AL.is_ge)
+    ts(s("TMP2", 128, 256), s("JW"), 16.0, AL.add)
+    cp(s("SBF"), s("SI"))
+    tt(s("TMP", 128, 256), s("TMP", 128, 256), s("TMP2", 128, 256), AL.mult)
+    cp(s("LN", 0, 16), s("NLI"))
+    tt(s("OV2", 0, 128), s("TMP", 128, 256), s("OVI"), AL.add)
+    dma("y", s("CW", 0, C, p=row(0)), s("SBF"))
+    cp(s("OVL"), s("OV2", 0, 128))
+    ms(s("U12", 16, 28), 4.0)
+    scan(s("U12", 0, 12), s("U12", 16, 28), s("TMP", 16, 28), 0.25, AL.mult, AL.add)
+    cp(s("VARS"), ind(s("VA"), s("LN", 0, 16)))
+    cp(ind(s("DEW"), s("OVL")), s("DVAL"))
+    dma("y", s("X", 0, H), ext(T.xv[:, 0:H]))
+    dma("y", s("KK", 0, C), ext(T.kc[:]))
+    send(0, [w_("X", H + S * d, S) for d in range(3)], "LA", 0, S)
+    iota(s("JT", 0, 16), [[0, 8], [128, 2]], 0, 1)
+    iota(s("JT", 16, 32), [[0, 8], [128, 2]], DV0, 1)
+    iota(s("VT"), [[0, 256]], 0, 0)
+    sel(BD, s("ONES", 0, 128), [[-16, 8], [0, 16]], AL.is_ge, 0.0, 0)
+    sel(BD, BD, [[16, 8], [0, 16]], AL.is_ge, 0.0, 15, -1)
+    terms(sm("SELE"), [(2, None, 256), (3, None, 1)])
+    terms(M("SV1"), [(4, 4, 1), (5, 5, 1), (6, 6, 1)])
+    terms(M("SV2"), [(4, 2, 1), (5, 3, 1)])
+    for d in range(3):
+        sel(M("PI%d" % d), s("ZERO", 0, 128), [[16, 8], [-1, 16]], AL.not_equal, 1.0, -16 * (d + 1))
+        sel(M("PI%d" % d), M("PI%d" % d), [[16, 8], [-1, 16]], AL.not_equal, 1.0, -16 * (d + 1) - 128)
+    sel(M("B7"), BD, [[0, 8], [1, 16]], AL.is_equal, 0.0, -7, 0)
+    terms(M("K1"), [(0, 1, 1), (6, 1, 1), (6, 7, 1)])
+    terms(M("K3"), [(2, 1, -1)])
+    iota(s("II", 12, 15), [[16, 3]], 143 + 16, -1, False)
+    iota(s("GI"), [[16, 8], [0, 16]], 0, 0)
+    terms(M("SK"), [(1, None, -1)])
+    terms(M("SD"), [(i, i, -1) for i in (0, 1, 2, 3, 7)])
+
+    def steal_consts():
+        cp(s("ELX", 0, 40), s("II", 16, 56))
+        ts(col("od"), col("odd"), 1.0 / 16, AL.mult)
+        ts(col("ev"), col("odd"), 1.0, AL.is_lt)
+        ms(s("TMP2", 0, 128), 0.5)
+        ms(s("YY", 0, 1), 0.0)
+        scan(s("TMP2", 128, 256), s("TMP2", 0, 128), s("ZERO", 0, 128), 2.0 ** 61, AL.mult, AL.add)
+        ts(s("BASEW", 0, 16), s("JW", 0, 16), float(DV0), AL.add)
+        tt(s("TMP2", 128, 256), s("TMP2", 128, 256), s("IDF"), AL.mult)
+        red(col("pow"), s("TMP2", 128, 256))
+        ts(col("thr"), col("pow"), 2.5, AL.mult)
+
+    def meet_consts():
+        lin("kh", [(1, 1), (6, 0.5)])
+        lin("kl", [(1, 1), (6, -0.5)])
+        lin("r07", [(0, 1), (7, 1)])
+        ts(s("II", 12, 15), s("II", 12, 15), 112, AL.bitwise_and)
+        for n in range(3):
+            col("pg%d" % n)
+        cp(w_("CF", cols["pg0"], 3), s("II", 12, 15))
+        act(s("BASEW", 32, 48), s("JW", 0, 16), AF.Identity, bias=float(C))
+        act(s("BASEW", 16, 32), s("JW", 0, 16), AF.Identity, bias=float(C), scale=0.0)
+        for d in range(3):
+            act(M("PD%d" % d), M("PI%d" % d), scale=col("r07"))
+            ts(M("PK%d" % d), s("GI"), col("pg%d" % d), AL.is_equal, col("kh" if high[d] else "kl"), AL.mult)
+
+    def out_rows():
+        ts(s("OV2", 128, 256), s("OVI"), 8, AL.arith_shift_right)
+        ts(s("OV2", 256, 384), s("OVI"), 255, AL.bitwise_and)
+        ts(s("OVB", 0, 128), s("OV2", 128, 256), -8.0, AL.add)
+        cp(s("OVB", 128, 256), s("OV2", 256, 384))
+        dma("y", s("OW", 0, C, p=row(4)), s("OVB", 0, 128))
+        dma("y", s("OW", 0, C, p=row(5)), s("OVB", 128, 256), True)
+
+    def first_replicas():
+        for d in range(3):
+            mm(w_("P7", S * d, S), M("PI%d" % d), w_("LA", S * d, S))
+        tt(s("NE"), s("P7", 0, 192), XREP, AL.not_equal)
+        tt(s("DX"), s("P7", 0, 192), XREP, AL.subtract)
+        cp(s("XR0"), XREP)
+        mm(s("P7", 0, 192), M("K1"), AREP)
+        mms([(s("P7", 256, 448), M("K3"), AREP)] + [(w_("P7", 256 + S * d, S), M("B7"), w_("NE", S * d, S)) for d in range(3) if high[d]])
+        ts(s("LS"), s("P7", 256, 448), 0.0, AL.is_gt)
+        tt(s("LS"), s("P7", 0, 192), s("LS"), AL.mult)
+        tt(AREP, AREP, s("LS"), AL.add)
+
+    CR = [13, 14, 15, 7]
+
+    def plan_consts(part):
+        Z128, O128 = s("ZERO", 0, 128), s("ONES", 0, 128)
+        if part == 0:
+            iota(s("OW"), [[0, CWD]], 0, 0)
+            iota(s("X", V, VW), [[0, VW - V]], 0, 0)
+            iota(s("C4K"), [[0, 256]], int(STALE), 0)
+            terms(s("ZW", 160, 320), [(4, 15, 256), (5, 15, 1)])
+            terms(M("BU22"), [(7, None, 2 ** 22)])
+            terms(M("BU"), [(7, None, 1)])
+            terms(M("BDE"), [(2, 1, 256), (3, 1, 1)])
+            terms(M("NBO"), [(4, 1, -256), (5, 1, -1), (0, 0, 1), (6, 6, 1)])
+            terms(M("BO"), [(4, None, -256), (5, None, 1)])
+            terms(sm("SF"), [(6, None, 1)])
+            terms(sm("S8"), [(8, None, 1)])
+            terms(M("SU"), [(7, 8, 1)])
+        if part == 1:
+            terms(M("MO"), [(4, 4, -1), (5, 5, 1)])
+            terms(M("MAB"), [(0, 0, 1), (6, 6, 1), (6, 4, 4), (1, 4, -4096), (1, 5, -4096), (1, 6, -4096), (1, 7, 4096)])
+            terms(M("BNH"), [(7, None, 32)])
+            terms(s("ZW", 480, 640), [(4, 15, -256), (5, 15, 1), (6, 15, -4096)])
+            for n, w in (("NID", -1.0), ("ID16", 16.0), ("ID256", 256.0)):
+                sel(M(n), Z128, [[-1, 128]], AL.not_equal, w, 0)
+            sel(sm("G8B"), G8, [[0, 8]], AL.is_ge, 0.0, 0)
+            sel(s("RS1"), O128, [[0, 8], [1, 16]], AL.not_equal, 0.0, 0, 0)
+            iota(s("JI"), [[1, 16], [16, 16]], 0, 0)
+            iota(s("J1"), [[1, 256]], 1, 0)
+            iota(s("KK", C, CWD), [[0, CWD - C]], 0, 0)
+            iota(s("CW2", C, CWD), [[0, CWD - C]], 0, 0)
+            act(s("POS", 128, 144), s("JW", 0, 16), AF.Identity, bias=1.0)
+            act(s("BASEW", 48, 64), s("JW", 0, 16), AF.Identity, bias=float(DV0 - 7168))
+            ts(col("g15"), col("g16"), 15.0, AL.add)
+            ts(s("ZW", 320, 480), s("IO", 0, 160), col("g15"), AL.is_equal, col("i"), AL.mult)
+        if part >= 2:
+            t = part - 2
+            r = 40 * t
+            for n, cmp in (("TRI", AL.is_ge), ("TRS", AL.is_gt)):
+                o = M("%s%d" % (n, t))
+                sel(o, O128, [[1, 128]], cmp, 0.0, r, -1)
+                if t:
+                    c0 = o[1][0][1]
+                    sel(s("MAT", c0, c0 + 128, p=slice(0, r)), s("ONES", 0, 128, p=slice(0, r)), [[1, 128]], cmp, 0.0, r - 128, -1)
+            for n, w in (("PM", 1.0), ("PM4", 4096.0)):
+                o = M("%s%d" % (n, t))
+                sel(o, Z128, [[1, 128]], AL.not_equal, w, r, -1)
+                if t:
+                    sel(o, o, [[1, 128]], AL.not_equal, w, r - 128, -1)
+            sel(M("SCH%d" % t), BD, [[0, 8], [1, 16]], AL.is_equal, 0.0, -9 - t, 0)
+            terms(M("SCL%d" % t), [(0, CR[t], 1)])
+            terms(M("BCH%d" % t), [(9 + t, None, 2 ** 22)])
+            terms(sm("SN%d" % t), [(CR[t], None, -1)])
+            terms(sm("SR%d" % t), [(9 + t, None, 1)])
+            for h, last in ((0, 1), (1, 128 - (127 + r) % 128)):
+                o = w_("RH", 32 * t + 16 * h, 16)
+                iota(o, [[1, 16]], last, 0)
+                sel(o, o, [[0, 16]], AL.is_equal, 1.0, -127)
+                if h and t:
+                    sel(o, o, [[0, 16]], AL.not_equal, -127.0, r - 127)
+
+    def permute(qs):
+        for q in qs:
+            cp(w_("VAP", 128 * q, 128), s("VA", q, C, 16))
+
+    def new_outputs(m):
+        cp(ind(s("OW"), w_("LN", 32 * (m + 1) + 16, 16)), w_("VAL", 256 * m, 256))
+
+    def stale_marks(m):
+        cp(ind(XW_, w_("L2", 16 * m, 16)), s("C4K"))
+
+    bg = [0, 0, 0]
+
+    def mask_gather(n, e="s"):
+        for _ in range(n):
+            if bg[0] < 32:
+                h = bg[0]
+                gat(e, w_("GR", 16384 + 1024 * (h % 16), 1024), ind(s("CODE"), w_("VAP", 64 * h, 64)))
+                bg[0] += 1
+
+    def mask_fold(n):
+        for _ in range(n):
+            if bg[1] < min(bg[0], bg[2] + 8):
+                h = bg[1]
+                b0 = 16384 + 1024 * (h % 16)
+                mms([(w_("P7", 64 * (h % 8), 64), ID, s("GR", b0 + k, b0 + 1024, 16)) for k in range(16)])
+                bg[1] += 1
+
+    def mask_keep():
+        while bg[2] + 4 <= bg[1]:
+            act(w_("MK", 64 * bg[2], 256), w_("P7", 64 * (bg[2] % 8), 256))
+            bg[2] += 4
+
+    act(s("GR", 0, 2048), ind(AW, s("VARS", 0, 128)))
+    for m in range(4):
+        if m:
+            for j in range(4):
+                gat("vs"[j & 1], w_("GR", 1024 * j, 1024), ind(AW, w_("VARS", 64 * j, 64)))
+        else:
+            act(s("GR", 2048, 4096), ind(AW, s("VARS", 128, 256)))
+        if m == 0:
+            dma("y", s("A", 0, V, p=row(2)), s("DEW", 0, V, p=row(4)))
+            dma("s", s("A", 0, V, p=row(3)), s("DEW", 0, V, p=row(5)), True)
+            act(s("SR"), ind(s("CW"), s("LN", 0, 16)))
+        else:
+            mask_fold(1)
+        for h in range(2):
+            for k in range(16):
+                mm(s("P0", 16 * h + k, 256, 32), s("GR", 2048 * h + k, 2048 * h + 2048, 16), s("MAT", mats["SELK"] * 128 + k, mats["SELK"] * 128 + 128, 16))
+        if m == 0:
+            steal_consts()
+            for h in range(2):
+                mm(s("P1", h, 48, 2), w_("SR", 128 * h, 128), SELC)
+            act(s("SCT"), s("P1", 0, 48))
+            for u in range(16):
+                act(w_("CODE", H + 12 * u, 12), s("U12", 0, 12), scale=ic(u))
+        else:
+            mask_keep()
+            mask_fold(1)
+            new_outputs(m - 1)
+            act(w_("SQ", 192 * (m - 1), 192), w_("TT", 192 * (m - 1), 192), AF.Abs)
+            mask_gather(1)
+        scan(s("M1"), s("RSB"), s("P0", 0, 256), 0.0, AL.add, AL.min)
+        cp(s("TI", 0, 16), s("M1", 15, 256, 16))
+        ts(s("OI"), s("TI", 0, 16), 4095, AL.bitwise_and)
+        tt(s("EXP", 0, 256), ind(s("OI"), s("ELX", 0, 16)), s("MASKR", 0, 256), AL.mult)
+        for h in range(2):
+            mm(w_("P1", 64 + 8 * h, 8), w_("EXP", 128 * h, 128), G8)
+        tt(s("YY", 1, 256), s("M1", 0, 255), s("P0", 1, 256), AL.max)
+        LIVE = s("TF", 16, 32)
+        tt(LIVE, s("M1", 15, 256, 16), s("SCT", 0, 16), AL.is_lt)
+        cp(s("L1"), s("P1", 64, 80))
+        ts(s("BE"), ind(s("BITS"), s("L1")), col("ev"), AL.mult)
+        act(s("BO"), ind(s("BITS"), s("L1")), scale=col("od"))
+        act(s("GO"), ind(AW, s("L1")))
+        def gram(gg, bank, c0, lo):
+            B, pp = ("BE", "BO")[gg & 1], slice(32 * (gg // 2), 32 * (gg // 2) + 32)
+            mm(w_(bank, c0, 256 - lo), s(B, lo, lo + 128, p=pp), s(B, lo, 256, p=pp), tile=gg // 2)
+        for gg in (0, 1, 2, 3):
+            gram(gg, "P%d" % (2 + gg // 2), 256 * (gg & 1), 0)
+        for gg in (0, 1, 4, 5):
+            gram(gg, "P0" if gg >= 4 else "P6", 128 * (gg % 4), 128)
+        for gg in (4, 5, 6, 7):
+            gram(gg, "P%d" % (2 + gg // 2), 256 * (gg & 1), 0)
+        for gg in (2, 3, 6, 7):
+            gram(gg, "P0" if gg >= 4 else "P6", 128 * (gg % 4), 128)
+        scan(s("M2"), s("YY"), s("RSB"), 0.0, AL.min, AL.max)
+        ts(s("WL", 0, 16), LIVE, col("pow"), AL.mult)
+        ts(s("WL", 16, 32), LIVE, 2.0 ** 62, AL.mult)
+        tt(s("TI", 16, 32), s("M2", 15, 256, 16), s("SCT", 0, 16), AL.min)
+        tt(s("DO"), s("OI"), s("JT", 16, 32), AL.subtract)
+        ts(s("TI", 32, 48), s("TI", 16, 32), 16, AL.arith_shift_right)
+        ts(s("TF", 32, 48), LIVE, col("thr"), AL.mult)
+        act(s("TH", 0, 512), s("P2"), AF.Relu, bias=-11.0)
+        ts(s("TH", 512, 1024), s("P3"), 11.0, AL.is_gt)
+        act(s("TH", 1024, 1536), s("P4"), AF.Relu, bias=-11.0)
+        for h in range(2):
+            ts(s("VT", 128 * h, 128 * h + 128, 16), s("TI", 32 + h, 48, 2), 0.0, AL.add)
+            ts(s("VT", 128 * h + 1, 128 * h + 128, 16), s("TI", 32 + h, 48, 2), 1.0, AL.add)
+        act(s("TH", 1536, 2048), s("P5"), AF.Relu, bias=-11.0)
+        ts(s("TH", 2048, 2560), s("P6"), 11.0, AL.is_gt)
+        act(s("TH", 2560, 3072), s("P0"), AF.Relu, bias=-11.0)
+        tt(s("DOX"), ind(s("DO"), s("ELX", 0, 16)), s("MASKR", 0, 256), AL.mult)
+        if m == 0:
+            permute(range(0, 2))
+            mask_gather(1)
+            first_replicas()
+        else:
+            permute(range(4 * m, 2 + 4 * m))
+            mask_gather(1)
+        th = lambda gg: 256 * gg
+        for gg in range(8):
+            mm(w_("P1", 96 + 2 * gg, 1), w_("TH", th(gg), 128), w_("WL", 2 * gg, 1))
+        for gg in range(8):
+            o1 = w_("P1", 97 + 2 * gg, 1)
+            mms([(o1, w_("TH", th(gg) + 128, 128), w_("WL", 16 + 2 * gg, 1)), (o1, w_("TH", 2048 + 128 * gg, 128), w_("WL", 2 * gg + 1, 1))])
+        PV = s("P2", 256, 512)
+        mms([(PV, M("SV1"), s("GO")), (PV, M("SV2"), s("SR"))] + [(w_("P2", 256 + 128 * h, 128), w_("VT", 128 * h, 128), ID) for h in range(2)])
+        mm(s("P3", 0, 16), s("IDF"), s("BASEW", 0, 16), True, False)
+        tt(s("ACT"), s("P1", 96, 112), s("TF", 32, 48), AL.is_lt)
+        VAL = w_("VAL", 256 * m, 256)
+        act(VAL, PV)
+        tt(s("EXP", 0, 256), ind(s("ACT"), s("ELX", 0, 16)), s("DOX"), AL.mult)
+        mms([(w_("P3", 8 * h, 8), w_("EXP", 128 * h, 128), G8) for h in range(2)], False)
+        for h in range(2):
+            mm(s("P2", h, 16, 2), w_("GO", 128 * h, 128), sm("SELE"))
+        if m:
+            stale_marks(m - 1)
+            mask_fold(1)
+        L2 = w_("L2", 16 * m, 16)
+        cp(L2, s("P3", 0, 16))
+        cp(ind(AW, L2), VAL)
+        send(1 + m, [w_("A", H + S * d, S) for d in range(3)], "LA", 192 * (m + 1), S)
+        plan_consts(m)
+        if m == 0:
+            meet_consts()
+        else:
+            mask_keep()
+            mask_fold(3)
+            mask_gather(3 if m < 3 else 4)
+        tt(s("TF", 80, 96), s("SCT", 32, 48), LIVE, AL.mult)
+        tt(s("TF", 112, 128), s("SCT", 32, 48), s("JT", 0, 16), AL.subtract)
+        tt(s("TF", 96, 112), s("P2", 0, 16), s("TF", 80, 96), AL.subtract)
+        tt(s("NM", 16, 32), s("TF", 112, 128), s("ACT"), AL.mult)
+        tt(s("TF", 96, 112), s("TF", 96, 112), s("ACT"), AL.mult)
+        tt(s("NM", 0, 16), s("TF", 96, 112), s("TF", 80, 96), AL.add)
+        tt(s("EXP"), ind(s("NM"), s("ELX", 0, 32)), s("MASKR"), AL.mult)
+        mm(s("P4", 0, 192), M("SK"), AREP, True, False)
+        mm(s("P5", 0, 192), M("SD"), AREP, True, False)
+        mms([(s("P1", 160, 192), s("IDF"), s("BASEW", 16, 48))] + [(w_("P1", 160 + 8 * h, 8), w_("EXP", 128 * h, 128), G8) for h in range(4)])
+        if m == 0:
+            mask_gather(3)
+            out_rows()
+        permute(range(2 + 4 * m, 4 + 4 * m))
+        cp(w_("LN", 32 * (m + 1), 32), s("P1", 160, 192))
+        if m < 3:
+            cp(s("VARS"), ind(s("VA"), w_("LN", 32 * (m + 1), 16)))
+            cp(s("SR"), ind(s("CW"), w_("LN", 32 * (m + 1), 16)))
+        else:
+            new_outputs(3)
+        LA = lambda d: w_("LA", 192 * (m + 1) + S * d, S)
+        mms([(w_("P4", S * d, S), M("PK%d" % d), LA(d)) for d in range(3)], False)
+        mms([(w_("P5", S * d, S), M("PD%d" % d), LA(d)) for d in range(3)], False)
+        if m < 3:
+            for h in range(2):
+                mm(s("P1", h, 48, 2), w_("SR", 128 * h, 128), SELC)
+        TTm = w_("TT", 192 * m, 192)
+        ts(s("LS"), s("P4", 0, 192), 0.0, AL.is_gt)
+        tt(TTm, s("P5", 0, 192), s("LS"), AL.mult)
+        tt(AREP, AREP, TTm, AL.add)
+        if m < 3:
+            mask_fold(2)
+            act(s("SCT"), s("P1", 0, 48))
+        else:
+            tt(w_("SQ", 192 * m, 192), TTm, TTm, AL.mult)
+
+    def changed_digits(lst, n):
+        mms(lst)
+        tt(s("T192", 0, 192), lst[0][0], s("CODE", H, V), AL.min)
+        red(col(n), s("T192", 0, 192))
+
+    def mask_test(c0, n, wc):
+        ts(s("MT", 0, n), w_("MK", c0, n), col(wc), AL.add)
+        ts(w_("MT", 512, n), s("MT", 0, n), 0xAAAAAA, AL.bitwise_and)
+        ts(w_("MB", c0, n), w_("MT", 512, n), 0.0, AL.is_gt)
+
+    def outputs_checked(j, part):
+        cw, ow, ab = w_("CW", 512 * j, 512), w_("OW", 512 * j, 512), w_("AB", 512 * j, 512)
+        if part == 0:
+            b = s("P4" if j & 1 else "P5")
+            mms([(b, M("BDE"), w_("GV", 512 * j, 512)), (b, M("NBO"), cw)])
+            act(ab, b, AF.Abs)
+        else:
+            b = s("P7" if j & 1 else "P6")
+            mms([(b, M("MO"), ow), (b, M("MAB"), ab)])
+            act(w_("CW2", 512 * j, 512), b, AF.Relu)
+
+    def replica_x():
+        for d in range(3):
+            ts(w_("T192", S * d, S), w_("P1", 256 + S * d, S), 1.0 if high[d] else 2.0, AL.is_equal)
+        ts(s("T192", 192, 384), s("P1", 256, 448), 0.0, AL.is_equal, STALE, AL.mult)
+        tt(s("T192", 0, 192), s("T192", 0, 192), s("DX"), AL.mult)
+        tt(s("T192", 0, 192), s("T192", 0, 192), s("XR0"), AL.add)
+        tt(XREP, s("T192", 0, 192), s("T192", 192, 384), AL.max)
+
+    mms([(s("P3", 256, 448), M("SU"), w_("SQ", 192 * m, 192)) for m in range(4)])
+    tt(AREP, s("P3", 256, 448), AREP, AL.add)
+    changed_digits([(s("P6", 0, 192), M("BU22"), w_("SQ", 192 * m, 192)) for m in range(4)], "wd")
+
+    def piece(e, lo, hi):
+        gat(e, s("GR", 1024 * lo, 1024 * hi), ind(AW, s("VAP", 64 * lo, 64 * hi)))
+
+    def first_flags(q):
+        o = s("P0", q, 128, 16)
+        mms([(o, s("OW", q, C, 16), sm("SF"))] + ([(o, w_("MB", 128 * q, 128), sm("G8B"))] if q < 10 else
+                                                   [(o, s("GR", 2048 * q + k, 2048 * q + 2048, 16), sm("S8")) for k in range(16)]))
+    mask_keep()
+    mask_fold(8)
+    mms([(s("P3", 0, 128), slide(1, r), s("OW", r, C, 16)) for r in range(16)])
+    piece("s", 30, 32)
+    mask_keep()
+    assert bg == [20, 20, 20]
+    piece("v", 20, 22)
+    ts(s("LO128"), s("P3", 0, 128), float(C), AL.add)
+    piece("s", 28, 30)
+    mask_test(0, 512, "wd")
+    first_flags(15)
+    first_flags(10)
+    piece("v", 22, 24)
+    piece("s", 26, 28)
+    mask_test(512, 512, "wd")
+    first_flags(14)
+    first_flags(11)
+    mask_test(1024, 256, "wd")
+    piece("s", 25, 26)
+    piece("v", 24, 25)
+    act(s("GV", 0, 1024), ind(AW, s("LO128", 0, 64)))
+    for q in list(range(10)) + [13, 12]:
+        first_flags(q)
+    mm(s("P1", 256, 448), M("BU"), AREP)
+    stale_marks(3)
+
+    def fold(t, q, early):
+        o = s("P0", q, 128, 16)
+        mms([(o, ID, s("F", q, 128, 16)), (o, s("OW", q, C, 16), sm("SN%d" % t))] + ([(o, w_("MB", 128 * q, 128), sm("G8B"))] if early else [])
+            + [(o, s("GR", 2048 * q + k, 2048 * q + 2048, 16), sm("SR%d" % t)) for k in range(16)])
+
+    SBX, SBA = (T.SB[:, :, 0:S], [("SB", 0, 3)], []), (T.SB[:, :, S:2 * S], [("SB", 0, 3)], [])
+    for t in range(4):
+        ts(s("F"), s("P0", 0, 128), 0.0, AL.is_gt)
+        scan(s("IP"), s("RS1"), s("F"), 0.0, AL.mult, AL.add)
+        mm(s("P1", 0, 8), M("TRI%d" % t), s("IP", 15, 128, 16))
+        act(s("CR"), ind(s("IP"), s("ELX", 32, 40)))
+        mms([(s("P2", 0, 128), s("F"), M("PM4%d" % t)), (s("P2", 0, 128), s("IP"), M("PM%d" % t)), (s("P2", 0, 128), s("CR"), M("TRS%d" % t))])
+        for gg in range(8):
+            ts(w_("CMP", 256 * gg, 256), s("JI"), w_("P1", gg, 1), AL.is_ge)
+        act(s("POS", 0, 128), s("P2", 0, 128), AF.Identity, bias=-4096.0)
+        if t == 0:
+            outputs_checked(0, 0)
+            outputs_checked(1, 0)
+            act(s("GV", 1024, 2048), ind(AW, s("LO128", 64, 128)))
+        for j in range(16):
+            mm(s("P3", j, 32, 16), s("CMP", j, 2048, 16), s("RH", 32 * t + j, 32 * t + 32, 16))
+        if t == 0:
+            replica_x()
+            outputs_checked(2, 0)
+            outputs_checked(0, 1)
+        cp(s("LB"), s("P3", 0, 16))
+        act(s("BC"), s("P3", 16, 32), AF.Identity, bias=float(40 * t))
+        tt(s("OH"), ind(s("POS"), s("LB")), s("J1"), AL.is_equal)
+        mms([(s("P1", 16, 32), slide(2, r), s("OH", r, 256, 16)) for r in range(16)] + [(s("P1", 16, 32), M("ID16"), s("BC"))])
+        if t == 0:
+            for j, part in ((3, 0), (1, 1), (2, 1), (3, 1)):
+                outputs_checked(j, part)
+            ts(s("GM"), s("LS"), -1.0, AL.mult, 1.0, AL.add)
+        CL, LO, PS = s("CL"), s("LO"), s("P4", 0, 256)
+        cp(CL, s("P1", 16, 32))
+        cp(s("VARS"), ind(s("VA"), CL))
+        act(s("CG"), ind(s("CW2"), CL))
+        mms([(s("P3", 32, 48), slide(3, r), s("CG", r, 256, 16)) for r in range(16)])
+        mm(s("P6", 0, 256), M("BO"), s("CG"))
+        mm(PS, M("BNH"), s("CG"), True, False)
+        for h in range(2):
+            mm(w_("P7", 8 * h, 8), w_("CG", 128 * h, 128), SELW)
+
+        def xg(e, j):
+            gat(e, w_("GR", 1024 * j, 1024), ind(XW_, w_("VARS", 64 * j, 64)))
+
+        def xs(j):
+            mms([(w_("P4", 64 * j, 64), M("NID"), s("GR", 1024 * j + k, 1024 * j + 1024, 16)) for k in range(16)], False, False)
+
+        def wg(e, j):
+            gat(e, w_("GR", 4096 + 1024 * j, 1024), ind(AW, w_("VARS", 64 * j, 64)))
+
+        def ws(h):
+            b0 = 4096 + 2048 * h
+            mms([(w_("P5", 128 * h, 128), w_("EQ", 128 * h, 128), M("ID256"))] + [(s("P5", 128 * h + k, 128 * h + 128, 16), s("GR", b0 + k, b0 + 2048, 16), SELW) for k in range(16)])
+        xg("v", 0)
+        xg("s", 2)
+        tt(s("TF", 0, 16), s("P3", 32, 48), s("BASEW", 48, 64), AL.min)
+        ts(LO, s("TF", 0, 16), 7168.0, AL.add)
+        act(s("ORG"), s("P6", 0, 256), AF.Identity, bias=float(V))
+        xs(0)
+        xs(2)
+        xg("v", 1)
+        xg("s", 3)
+        act(s("KR"), ind(s("KK"), CL))
+        act(s("XO"), ind(XW_, LO))
+        xs(1)
+        xs(3)
+        mms([(PS, ID, s("KR")), (PS, ID, s("XO"))], False)
+        tt(s("EQ"), ind(s("VA"), CL), s("ORG"), AL.is_equal)
+        wg("v", 0)
+        wg("s", 1)
+        ws(0)
+        wg("s", 2)
+        ts(s("MI", 0, 256), PS, 65536.0, AL.add)
+        ts(s("GG"), PS, -11800.0, AL.is_ge)
+        ts(s("MI", 256, 512), s("MI", 0, 256), 255, AL.bitwise_and)
+        ts(s("WT"), PS, -11800.0, AL.is_lt)
+        wg("s", 3)
+        ws(1)
+        act(s("AO"), ind(AW, LO), scale=ic(0))
+        tt(s("NEQ"), s("MI", 256, 512), s("XO"), AL.not_equal)
+        tt(s("NXG"), s("MI", 256, 512), s("GG"), AL.mult)
+        tt(s("XW"), s("XO"), s("WT"), AL.mult)
+        tt(ind(XW_, LO), s("NXG"), s("XW"), AL.add)
+        PB = s("P2", 0, 256)
+        mms([(PB, M("SCL%d" % t), s("ONES")), (PB, M("SCH%d" % t), s("NEQ")), (PB, M("NID"), s("AO"))], True, False)
+        tt(SBX, XREP, s("GM"), AL.mult)
+        scan(s("M1"), s("RSB"), s("P5", 0, 256), 0.0, AL.add, AL.min)
+        for h in range(2):
+            tt(s("VT", 128 * h, 128 * h + 128, 16), s("M1", 128 * h + 15, 128 * h + 128, 16), w_("P7", 8 * h, 8), AL.min)
+        mms([(w_("P2", 128 * h, 128), w_("VT", 128 * h, 128), ID) for h in range(2)], False)
+        tt(s("T1"), PB, s("GG"), AL.mult)
+        tt(ind(AW, LO), s("T1"), s("AO"), AL.add)
+        tt(SBA, AREP, s("GM"), AL.mult)
+        send(5 + t, [(T.SB[:, d, :], [("SB", 0, 3)], []) for d in range(3)], "LP%d" % t, 0, 128)
+        piece("s", 0, 2)
+        piece("s", 2, 3)
+        cp(ind(s("OW"), CL), s("T1"))
+        piece("v", 3, 5)
+        for d in range(3):
+            mm(w_("P6", S * d, S), M("PI%d" % d), w_("LP%d" % t, 128 * d + S, S))
+        for d in range(3):
+            mm(w_("P5", S * d, S), M("PI%d" % d), w_("LP%d" % t, 128 * d, S))
+        tt(AREP, s("P6", 0, 192), SBA, AL.add)
+        piece("s", 5, 6)
+        changed_digits([(s("P7", 0, 192), M("BCH%d" % t), AREP)], "wd")
+        tt(XREP, s("P5", 0, 192), SBX, AL.add)
+        mask_test(0, 384, "wd")
+        if t == 3:
+            ts(s("YB"), s("X", 0, V), 256.0, AL.min)
+            dma("y", ext(T.y[:]), s("YB"))
+            dma("g", ext(T.yw[:]), s("A", 0, V, p=row(0)))
+        if t == 0:
+            mms([(s("P7", 256, 384), slide(3, r), w_("CW2", 128 * r, 128)) for r in range(16)])
+            ts(s("FF"), s("P7", 256, 384), 7168.0, AL.add, float(V), AL.min)
+            dma("y", ext(T.yo[:]), s("FF"))
+        if t < 2:
+            plan_consts(4 + t)
+        piece("s", 30, 32)
+        for q in range(3):
+            fold(t, q, True)
+        fold(t, 15, False)
+        for j in range(6):
+            piece("v", 6 + 2 * j, 8 + 2 * j)
+            fold(t, 3 + j, False)
+            if j < 5:
+                piece("s", 28 - 2 * j, 30 - 2 * j)
+                fold(t, 14 - j, False)
+        piece("s", 19, 20)
+        piece("s" if t == 3 else "v", 18, 19)
+        fold(t, 9, False)
+    ts(s("FF"), s("P0", 0, 128), 0.0, AL.is_gt)
+    for gg in range(8):
+        dma("ys"[gg & 1], ext(T.yf[gg:gg + 1, :]), w_("FF", 16 * gg, 16))
+    for sem, val in cnt.items():
+        wait("g", sem, val)

@@ -4,34 +4,59 @@ from concourse.mybir import AluOpType as AL, AxisListType as AX, ActivationFunct
 V, C, S, N = 3072, 2048, 64, 4
 H = V - 3 * S
 NV, DV0, VW, CWD = 3072, 3088, 3344, 2304
-STALE = 4096.0
+STALE = 65536.0
 BIG = 3.0e7
+ALL = (1 << 128) - 1
 B16, F32, I32, U16 = "bfloat16", "float32", "int32", "uint16"
+NMK = 24
+MP = 32
+EARLY = 2
 _sb = {
     "VA": (CWD, I32), "VAP": (C, U16), "A": (VW, B16), "X": (VW, B16), "KK": (CWD, B16), "CW": (CWD, B16), "CW2": (CWD, B16), "OW": (CWD, B16),
-    "BITS": (DV0, B16), "GR": (32768, B16), "CODE": (V, B16), "MK": (C, F32), "MB": (C, B16), "MT": (1024, I32), "EQ": (256, B16),
+    "CH0": (VW, B16), "CH1": (VW, B16), "GR": (32768, B16), "GW": (4096, B16), "CODE": (V, B16), "MK": (C, F32), "MB": (C, B16), "MT": (1024, I32), "EQ": (256, B16),
     "IO": (256, F32), "ZERO": (256, B16), "GI": (128, F32), "JI": (256, B16), "J1": (256, F32), "II": (128, I32), "CF": (160, F32), "IC": (16, F32),
-    "JW": (128, F32), "TMP": (256, F32), "TMP2": (256, F32), "MAT": (60 * 128, B16), "SM": (256, B16), "ZW": (4 * 160, B16), "IDF": (128, F32), "G8": (8, F32),
-    "MASKR": (512, F32), "RSB": (256, F32), "RS1": (128, B16), "ELX": (48, U16), "BASEW": (64, F32), "JT": (32, F32),
+    "JW": (128, F32), "TMP": (256, F32), "TMP2": (256, F32), "MAT": (48 * 128, B16), "PIT": (160, B16), "SM": (256, B16), "ZW": (6 * 160, B16), "IDF": (128, F32), "G8": (8, F32),
+    "MASKR": (512, F32), "RSB": (256, F32), "RS1": (128, B16), "ELX": (48, U16), "BASEW": (80, F32), "JT": (32, F32),
     "OVI": (128, I32), "OV2": (384, I32), "OVL": (128, U16), "OVB": (256, B16), "WI": (192, I32), "WB": (192, B16), "SI": (128, I32), "SBF": (128, B16), "NLI": (16, I32),
-    "LN": (32 * 5, U16), "VARS": (256, U16), "SR": (256, B16), "M1": (256, F32), "YY": (256, F32), "M2": (256, F32),
-    "TI": (64, I32), "OI": (16, I32), "TF": (256, F32), "SCT": (48, F32), "ACT": (16, F32), "NM": (32, F32), "DO": (16, F32), "EXP": (512, F32), "DOX": (256, F32),
-    "L1": (16, U16), "L2": (64, U16), "BE": (256, B16), "BO": (256, B16), "GO": (256, B16), "WL": (32, B16), "VT": (256, B16), "VAL": (1024, B16), "C4K": (256, B16),
+    "LN": (32 * 5, U16), "VARS": (512, U16), "SR": (256, B16), "M1": (256, F32), "YY": (256, F32), "M2": (256, F32),
+    "TI": (64, I32), "OI": (16, I32), "TF": (256, F32), "SCT": (32, F32), "ACT": (16, F32), "NM": (32, F32), "DO": (16, F32), "EXP": (512, F32), "DOX": (256, F32),
+    "L1": (16, U16), "L2": (64, U16), "BE": (256, B16), "BO": (256, B16), "GO": (256, B16), "WL": (32, B16), "VT": (272, B16), "VAL": (1024, B16), "YW": (192, F32),
     "ONES": (256, B16), "LA": (192 * 5, B16), "LS": (192, B16), "TT": (192 * 4, B16), "SQ": (192 * 4, B16), "XR0": (192, B16), "DX": (192, B16), "NE": (192, B16), "GM": (192, B16),
-    "T192": (384, F32), "U12": (32, F32), "LO128": (128, U16),
-    "F": (128, B16), "FF": (128, F32), "IP": (128, B16), "CR": (128, B16), "CMP": (2048, B16), "POS": (144, F32), "LB": (16, U16), "BC": (16, B16), "OH": (256, B16), "CL": (16, U16),
-    "ORG": (256, F32), "CG": (256, B16), "KR": (256, B16), "XO": (256, B16), "AO": (256, B16), "LO": (16, U16), "MI": (512, I32), "GG": (256, B16), "WT": (256, B16),
-    "NEQ": (256, B16), "T1": (256, B16), "NXG": (256, B16), "XW": (256, B16), "RH": (128, B16),
+    "T192": (384, F32), "LO128": (128, U16), "LC": (192 * 4, B16), "LP": (384 * 5, B16),
+    "F": (128, B16), "FF": (256, F32), "IP": (128, B16), "CR": (128, B16), "CMP": (2048, B16), "POS": (144, F32), "LB": (16, U16), "BC": (16, B16), "OH": (256, B16), "CL": (16, U16),
+    "CG": (512, B16), "KR": (256, B16), "XO": (256, B16), "LO": (48, U16), "FL": (256, I32), "GG": (256, B16), "NX": (256, B16),
+    "NEQ": (256, B16), "T1": (256, B16), "RH": (128, B16), "C256": (256, B16), "GS": (256, B16),
 }
 SCRATCH = {k: ("sbuf", [128, w], d) for k, (w, d) in _sb.items()}
 SCRATCH["SB"] = ("sbuf", [128, 3, 128], B16)
-for _i in range(4):
-    SCRATCH["LP%d" % _i] = ("sbuf", [128, 384], B16)
 for _i in range(8):
     SCRATCH["P%d" % _i] = ("psum", [128, 512], F32)
-SEMAPHORES = ["cv", "cs", "cp", "cg"] + ["d%d" % i for i in range(40)] + ["ar%d" % i for i in range(9)] + ["ls%d" % i for i in range(9)]
-ALIAS = {"TH": ("GR", 4096, 3072), "DEW": ("GR", 8192, DV0 + C), "DVAL": ("GR", 13568, C), "AB": ("GR", 0, C), "GV": ("GR", C, C), "YB": ("BITS", 0, V)}
-SAMEQ = True
+SEMAPHORES = ["cv", "cs", "cp", "cg"] + ["d%d" % i for i in range(56)] + ["ar%d" % i for i in range(14)] + ["ls%d" % i for i in range(14)]
+ALIAS = {"TH": ("GR", 4096, 3072), "DEW": ("GR", 8192, DV0 + C), "DVAL": ("GR", 13568, C), "GV": ("GR", C, C), "YB": ("CH0", 0, V),
+         "BITS": ("CH1", 0, DV0)}
+CY, PECY, GATHER, SCATTER, FIX, WAKE = 0.00088, 0.00044, 1.55, 3.6, 0.05, 0.1
+VPEN = (0.2, 0.3, 0.4, 0.5)
+RATES = ((1.55, 3.6), (1.15, 5.0), (2.0, 2.5), (2.0, 5.5), (1.15, 2.0))
+XW_X = 42.0
+VAP_X = 50.0
+FX = 0.8
+ROUNDS = 6
+WP = 32
+DMA0, DMABW, ROWS = 1.5, 250e3, 0.4
+REMOTE = 3.2
+FIRST = 3.5
+MARGIN = 3.0
+GSLACK = 1.6
+PUSHY = 5.0
+DEAR = 1.5
+W3 = "sv"
+PUSH = 10.0
+PUSHX = 10.0
+CWDMA = 1
+XP = (0, 32, 64, 96, 128, 160, 192, 224, 256)
+SHAKE = 0.0
+PLAN = []
+VAW = 1024
 
 
 def rank_program(g, core, T, topo):
@@ -40,44 +65,36 @@ def rank_program(g, core, T, topo):
         return
     Q = {"v": g.vector, "s": g.scalar, "p": g.tensor, "g": g, "y": g.sync}
     CS = {"v": "cv", "s": "cs", "p": "cp", "g": "cg"}
-    cnt, waited, rec, nd = {}, {}, {}, [0]
+    nodes, rec, banks, nd = [], {}, {}, [0]
 
-    def wait(q, sem, val):
-        if waited.get((q, sem), 0) < val:
-            Q[q].wait_ge(T.sem[sem], val)
-            waited[(q, sem)] = val
-
-    def note(regs, sem, val, wr, beside=None):
-        for (b, lo, hi) in regs:
-            d = rec.setdefault(b, {})
-            if wr and beside is None:
-                for k in [k for k in d if lo <= k[0] and k[1] <= hi]:
-                    del d[k]
-            d[(lo, hi, sem, wr)] = val
-
-    def op(q, fn, outs, ins, sem=None, inc=1, beside=None):
-        own = sem or CS[q]
+    def node(alt, outs, ins, sem=None, inc=1, lat=None, extra=0.0, after=()):
+        me = len(nodes)
         wr = [r for o in outs for r in o[1]]
         rd = [r for o in outs for r in o[2]] + [r for o in ins if isinstance(o, tuple) for r in o[1] + o[2]]
-        need = {}
+        pred = set(after)
+        eng = "".join(alt) if len(alt) == 1 else me
+        for b in {r[0] for r in wr + rd if r[0][0] == "P" and r[0][1:].isdigit()}:
+            st = banks.setdefault(b, [None, [], []])
+            if st[0] != eng:
+                st[0], st[1], st[2] = eng, [], st[1]
+            pred.update(st[2])
+            if eng == "p" and st[1]:
+                pred.add(st[1][-1])
+            st[1].append(me)
         for regs, w in ((wr, True), (rd, False)):
-            for (b, lo, hi) in regs:
-                ps = b[0] == "P" and b[1:].isdigit()
-                for (l2, h2, s2, w2), val in rec.get(b, {}).items():
-                    if s2 == own:
-                        hit = q != "p" and l2 < hi and lo < h2 and ((w2 and not w) or (SAMEQ and (w or w2)))
-                    else:
-                        hit = ps or (l2 < hi and lo < h2 and (w or w2))
-                    if hit and s2 != beside and val > need.get(s2, 0):
-                        need[s2] = val
-        for s2, val in need.items():
-            wait(q, s2, val)
-        cnt[own] = cnt.get(own, 0) + inc
-        ins_ = fn()
-        if ins_ is not None:
-            ins_.then_inc(T.sem[own], inc)
-        note(rd, own, cnt[own], False)
-        note(wr, own, cnt[own], True, beside)
+            for (b, lo, hi, tg) in regs:
+                for (l2, h2, t2, w2, k) in rec.get(b, ()):
+                    if l2 < hi and lo < h2 and (w or w2) and tg & t2:
+                        pred.add(k)
+        for (b, lo, hi, tg) in wr:
+            rec[b] = [e for e in rec.get(b, ()) if not (lo <= e[0] and e[1] <= hi and not e[2] & ~tg)]
+        for regs, w in ((rd, False), (wr, True)):
+            for (b, lo, hi, tg) in regs:
+                rec.setdefault(b, []).append((lo, hi, tg, w, me))
+        pred.discard(me)
+        kind = 2 if any(o[5] == "ind" for o in outs) else 1 if any(isinstance(o, tuple) and o[5] == "ind" for o in ins) else 0
+        nodes.append({"alt": alt, "pred": pred, "sem": sem, "inc": inc, "lat": lat, "extra": extra, "kind": kind})
+        return me
 
     def s(name, lo=0, hi=None, step=1, p=None):
         if name in ALIAS:
@@ -86,88 +103,239 @@ def rank_program(g, core, T, topo):
         t = T[name]
         hi = t.shape[1] if hi is None else hi
         ps = slice(0, 128) if p is None else p
-        return (t[ps, lo:hi:step] if step > 1 else t[ps, lo:hi], [(name, lo, hi)], [])
+        tg = ALL if p is None else sum(1 << x for x in range(128)[p])
+        return (t[ps, lo:hi:step] if step > 1 else t[ps, lo:hi], [(name, lo, hi, tg)], [], len(range(lo, hi, step)), SCRATCH[name][2], SCRATCH[name][0])
 
     def w_(name, lo, n):
         return s(name, lo, lo + n)
 
     def ind(win, off):
-        return (win[0].indirect(off[0]), win[1], off[1])
+        return (win[0].indirect(off[0]), win[1], off[1], 16 * off[3], win[4], "ind")
 
     def a(x):
         return x[0] if isinstance(x, tuple) else x
 
-    def cp(o, i):
-        op("v", lambda: g.vector.tensor_copy(o[0], i[0]), [o], [i])
+    def cost(o, ins, rate=None):
+        full = [o] + [x for x in ins if isinstance(x, tuple)]
+        n = max(x[3] for x in full)
+        if o[5] == "ind":
+            rate = SCATTER
+        elif any(x[5] == "ind" for x in full):
+            rate = GATHER
+        elif rate is None:
+            rate = 0.5 if all(x[4] in (B16, U16) for x in full if x[3] > 1) else 1
+        return FIX + max(64, n * rate) * CY
 
-    def tt(o, x, y, f):
-        op("v", lambda: g.vector.tensor_tensor(o[0], x[0], y[0], f), [o], [x, y])
+    def cp_(o, i):
+        return (cost(o, [i]), lambda: g.vector.tensor_copy(o[0], i[0]))
+
+    def ts_(o, x, s1, f0, s2=None, f1=None):
+        if f1 is None:
+            return (cost(o, [x]), lambda: g.vector.tensor_scalar(o[0], x[0], a(s1), None, f0))
+        return (cost(o, [x]), lambda: g.vector.tensor_scalar(o[0], x[0], a(s1), a(s2), f0, f1))
+
+    def act_(o, i, f=AF.Copy, bias=0.0, scale=1.0):
+        return (cost(o, [i], 1), lambda: g.scalar.activation(o[0], i[0], f, bias=a(bias), scale=a(scale)))
+
+    def cp(o, i, **k):
+        return node({"v": cp_(o, i)}, [o], [i], **k)
+
+    def tt(o, x, y, f, **k):
+        c = cost(o, [x, y], 1 if "psum" in (x[5], y[5]) else 2)
+        return node({"v": (c, lambda: g.vector.tensor_tensor(o[0], x[0], y[0], f))}, [o], [x, y], **k)
 
     def ts(o, x, s1, f0, s2=None, f1=None):
-        if f1 is None:
-            op("v", lambda: g.vector.tensor_scalar(o[0], x[0], a(s1), None, f0), [o], [x, s1])
-        else:
-            op("v", lambda: g.vector.tensor_scalar(o[0], x[0], a(s1), a(s2), f0, f1), [o], [x, s1, s2])
+        return node({"v": ts_(o, x, s1, f0, s2, f1)}, [o], [x, s1, s2])
 
-    def ms(o, c):
-        op("v", lambda: g.vector.memset(o[0], c), [o], [])
+    def ms(o, c, **k):
+        return node({"v": (cost(o, []), lambda: g.vector.memset(o[0], c))}, [o], [], **k)
 
     def scan(o, d0, d1, init, f0, f1):
-        op("v", lambda: g.vector.tensor_tensor_scan(o[0], d0[0], d1[0], a(init), f0, f1), [o], [d0, d1, init])
+        return node({"v": (cost(o, [d0, d1]), lambda: g.vector.tensor_tensor_scan(o[0], d0[0], d1[0], a(init), f0, f1))}, [o], [d0, d1, init])
 
     def red(o, i):
-        op("v", lambda: g.vector.tensor_reduce(o[0], i[0], AX.X, AL.add), [o], [i])
+        return node({"v": (cost(o, [i], 1), lambda: g.vector.tensor_reduce(o[0], i[0], AX.X, AL.add))}, [o], [i])
 
     def act(o, i, f=AF.Copy, bias=0.0, scale=1.0):
-        op("s", lambda: g.scalar.activation(o[0], i[0], f, bias=a(bias), scale=a(scale)), [o], [i, bias, scale])
+        return node({"s": act_(o, i, f, bias, scale)}, [o], [i, bias, scale])
 
-    def gat(e, o, i):
-        cp(o, i) if e == "v" else act(o, i)
+    def lin2(o, i, bias=0.0, scale=1.0, e="sv", **k):
+        plain = not isinstance(bias, tuple) and bias == 0.0
+        one = not isinstance(scale, tuple) and scale == 1.0
+        alt = {"s": act_(o, i, AF.Copy if plain else AF.Identity, bias, scale),
+               "v": cp_(o, i) if plain and one else (ts_(o, i, scale, AL.mult) if plain else ts_(o, i, scale, AL.mult, bias, AL.add))}
+        return node({q: alt[q] for q in e}, [o], [i, bias, scale], **k)
 
-    tiles = {}
+    def over(o, i, thr):
+        return node({"s": act_(o, i, AF.Relu, -0.375 * thr, 0.375), "v": ts_(o, i, thr, AL.is_gt, 0.375, AL.mult)}, [o], [i])
+
+    def mms(lst, st=True, sp=True, tile=None, **k):
+        c = sum(max(min(64, l[3]), r[3]) * (4 if l[4] == F32 else 1) for (o, l, r) in lst) * PECY
+        calls = [(o, l, r, st and n == 0, sp and n == len(lst) - 1, tile) for n, (o, l, r) in enumerate(lst)]
+        return node({"p": (c, calls)}, [x[0] for x in lst], [x[1] for x in lst] + [x[2] for x in lst], inc=len(lst), **k)
 
     def mm(o, l, r, st=True, sp=True, tile=None):
-        bank = o[1][0][0]
-        if bank in tiles and tiles[bank][0] != tile:
-            wait("p", "cp", tiles[bank][1])
-        op("p", lambda: g.tensor.matmul(o[0], l[0], r[0], st, sp), [o], [l, r])
-        tiles[bank] = (tile, cnt["cp"])
+        return mms([(o, l, r)], st, sp, tile)
 
-    def mms(lst, st=True, sp=True):
-        for n, (o, l, r) in enumerate(lst):
-            mm(o, l, r, st and n == 0, sp and n == len(lst) - 1)
+    def mmx(lst):
+        c = sum(max(min(64, l[3]), r[3]) * (4 if l[4] == F32 else 1) for (o, l, r) in lst) * PECY
+        return node({"p": (c, [(o, l, r, True, True, None) for (o, l, r) in lst])}, [x[0] for x in lst], [x[1] for x in lst] + [x[2] for x in lst], inc=len(lst))
 
     def iota(o, pat, base, cm, flt=True):
+        c = GSLACK * (0.13 + 2 * o[3] * CY)
         if flt:
-            op("g", lambda: g.iota(o[0], pat, base, cm, allow_small_or_imprecise_dtypes=True), [o], [])
-        else:
-            op("g", lambda: g.iota(o[0], pat, base, cm), [o], [])
+            return node({"g": (c, lambda: g.iota(o[0], pat, base, cm, allow_small_or_imprecise_dtypes=True))}, [o], [])
+        return node({"g": (c, lambda: g.iota(o[0], pat, base, cm))}, [o], [])
 
-    def dma(q, o, i, beside=False):
+    def fill(name, lo, hi, val=0):
+        for x in range(lo, hi, 512):
+            iota(s(name, x, min(hi, x + 512)), [[0, min(hi, x + 512) - x]], val, 0)
+
+    def sel(o, i, pat, cmp, fil, base, cm=1):
+        return node({"g": (GSLACK * (0.17 + 2 * o[3] * CY), lambda: g.affine_select(o[0], i[0], pat, cmp, fil, base, cm))}, [o], [i])
+
+    def dma(q, o, i, nbytes, **k):
         sem = "d%d" % nd[0]
         nd[0] += 1
-        op(q, lambda: Q[q].dma_start(o[0], i[0]), [o], [i], sem=sem, inc=16, beside="d%d" % (nd[0] - 2) if beside else None)
+        c = ROWS + nbytes / DMABW
+        me = node({"d": (c, lambda: Q[q].dma_start(o[0], i[0]))}, [o], [i], sem=sem, inc=16, lat=DMA0 + c, **k)
+        nodes[me]["by"] = q
+        return me
 
     def ext(ap):
-        return (ap, [], [])
+        return (ap, [], [], 1, None, "hbm")
 
-    def send(m, srcs, land, base, w):
+    sends = []
+    en = [e for e in topo.engines(core, T.cores[rank ^ 1]) if all(e in topo.engines(core, T.cores[rank ^ d]) for d in (2, 3))]
+    pool = {True: en[0::2], False: en[1::2]}
+    lanes = []
+    for d in (1, 2, 3):
+        far_die = topo.die(core) != topo.die(T.cores[rank ^ d])
+        side = far_die if len(pool[far_die]) >= len(en) // 4 else not far_die
+        lanes.append(pool[side][:len(en) // 4])
+        pool[side] = pool[side][len(en) // 4:]
+
+    def send(srcs, land, base, w, extra=0.0):
+        m = len(sends)
         trs, tot = [], 0
         for d in (1, 2, 3):
             dst = T.cores[rank ^ d]
             rid, pid, _ = topo.addr(dst)
-            en = topo.engines(core, dst)
-            k = len(en) // 4
-            mask = sum(1 << e for e in en[k * (d - 1):k * d])
+            k = len(lanes[d - 1])
+            mask = sum(1 << e for e in lanes[d - 1])
             tot += k
             trs.append(RemoteDMATransfer(dst_ids=[DstId(rid=rid, pnc=pid)], dma_engine_mask=mask, remote_sem=T.sem["ar%d" % m],
                                          src=srcs[d - 1][0], dst=T[land][:, base + (d - 1) * w:base + d * w]))
 
         def go():
             g.remote_dma_fused(trs, local_sem=T.sem["ls%d" % m])
-        op("g", go, [], srcs, sem="ls%d" % m, inc=tot)
-        cnt["ar%d" % m] = tot
-        note([(land, base, base + 3 * w)], "ar%d" % m, tot, True)
+        k = node({"g": (0.6 + (0 if m else FIRST), go)}, [], srcs, sem="ls%d" % m, inc=tot, lat=REMOTE + (MARGIN if extra and m < 12 else 0) + (0 if m else FIRST), after=sends[-1:], extra=extra)
+        nodes[k]["order"] = set(sends[-1:])
+        sends.append(k)
+        return node({"-": (0.0, None)}, [s(land, base, base + 3 * w)], [], sem="ar%d" % m, inc=tot, lat=0.01, after=[k])
+
+    def issue():
+        n = len(nodes)
+        succ = [[] for _ in range(n)]
+        for k, x in enumerate(nodes):
+            for j in x["pred"]:
+                succ[j].append(k)
+
+        def delay(j, c, k):
+            x, y = nodes[j], nodes[k]
+            if j in y.get("order", ()):
+                return c
+            return (x["lat"] or c) + (0.0 if "-" in y["alt"] or ("p" in x["alt"] and "p" in y["alt"]) else WAKE)
+
+        def place(key, back, spare):
+            busy, at = {q: [] for q in "vspgd-"}, [None] * n
+            for k in sorted(range(n), key=lambda k: (-key[k], -k if back else k)):
+                x, best = nodes[k], None
+                for q, (c, _) in x["alt"].items():
+                    if back:
+                        t0 = max([at[j][1] + at[j][2] + delay(k, c, j) for j in succ[k]] + [x["lat"] or c]) - c
+                    else:
+                        t0 = max([at[j][1] + delay(j, at[j][2], k) for j in x["pred"]] + [0.0])
+                    lane, i = busy[q], 0
+                    while i < len(lane) and t0 + c > lane[i][0]:
+                        t0 = max(t0, lane[i][1])
+                        i += 1
+                    fin = t0 + DEAR * c + (spare if q == "v" else 0.0)
+                    if best is None or fin < best[0]:
+                        best = (fin, q, t0, c, i)
+                at[k] = best[1:4]
+                if best[1] != "-":
+                    busy[best[1]].insert(best[4], (best[2], best[2] + best[3]))
+            return at
+
+        def length(at, rate):
+            free, t0, c = {}, [0.0] * n, [0.0] * n
+            for k in sorted(range(n), key=lambda k: (at[k][1], k)):
+                q = at[k][0]
+                c[k] = FIX + (at[k][2] - FIX) * rate[nodes[k]["kind"]] if nodes[k]["kind"] else at[k][2]
+                t0[k] = max([t0[j] + delay(j, c[j], k) for j in nodes[k]["pred"]] + [free.get(q, 0.0)])
+                free[q] = t0[k] + c[k]
+            return max(t0[k] + (nodes[k]["lat"] or c[k]) for k in range(n))
+        top = None
+        for spare in VPEN:
+            far = [0.0] * n
+            for k in range(n - 1, -1, -1):
+                x = nodes[k]
+                far[k] += (x["lat"] or min(c for c, _ in x["alt"].values())) + x["extra"]
+                for j in x["pred"]:
+                    far[j] = max(far[j], far[k] + WAKE)
+            for rnd in range(ROUNDS):
+                at = place(far, False, spare)
+                score = sum(length(at, (0, ga / GATHER, sc / SCATTER)) / (1 + ga) for ga, sc in RATES)
+                if top is None or score < top[0]:
+                    top = (score, at)
+                end = [0.0] * n
+                for k, x in enumerate(nodes):
+                    end[k] = max([at[k][1] + (x["lat"] or at[k][2])] + [end[j] + 1e-6 for j in x["pred"]])
+                at = place(end, True, spare)
+                far = [t0 + c + x.get("push", 0.0) for x, (q, t0, c) in zip(nodes, at)]
+                for k in range(n - 1, -1, -1):
+                    for j in nodes[k]["pred"]:
+                        far[j] = max(far[j], far[k] + delay(j, at[j][2], k))
+        PLAN.append(top[0])
+        for x, (q, t0, c) in zip(nodes, top[1]):
+            x["q"], x["t"] = q, t0
+        cnt, waited, tiles = {}, {}, {}
+
+        def wait(q, sem, val):
+            if waited.get((q, sem), 0) < val:
+                Q[q].wait_ge(T.sem[sem], val)
+                waited[(q, sem)] = val
+        for k in sorted(range(n), key=lambda k: (nodes[k]["t"], k)):
+            x = nodes[k]
+            q = x["q"]
+            own = x["sem"] or CS[q]
+            cnt[own] = cnt.get(own, 0) + x["inc"]
+            x["mark"] = (own, cnt[own])
+            if q == "-":
+                continue
+            need = {}
+            for j in x["pred"]:
+                if j in x.get("order", ()) or q == nodes[j]["q"] == "p":
+                    continue
+                sem, val = nodes[j]["mark"]
+                need[sem] = max(need.get(sem, 0), val)
+            for sem, val in need.items():
+                wait(x.get("by", q), sem, val)
+            call = x["alt"][q][1]
+            if q == "p":
+                for i, (o, l, r, st, sp, tile) in enumerate(call):
+                    bank = o[1][0][0]
+                    if bank in tiles and tiles[bank][0] != tile:
+                        wait("p", "cp", tiles[bank][1])
+                    g.tensor.matmul(o[0], l[0], r[0], st, sp).then_inc(T.sem["cp"], 1)
+                    tiles[bank] = (tile, cnt[own] - x["inc"] + i + 1)
+            else:
+                ins_ = call()
+                if ins_ is not None:
+                    ins_.then_inc(T.sem[own], x["inc"])
+        for sem, val in cnt.items():
+            wait("g", sem, val)
 
     high = [rank > (rank ^ d) for d in (1, 2, 3)]
     cols, mats, sms = {}, {}, {}
@@ -181,6 +349,8 @@ def rank_program(g, core, T, topo):
         return w_("IC", i, 1)
 
     def M(n):
+        if n[:2] == "PI":
+            return w_("PIT", 32 - 16 * int(n[2]), 128)
         if n not in mats:
             mats[n] = len(mats)
         return w_("MAT", mats[n] * 128, 128)
@@ -196,19 +366,12 @@ def rank_program(g, core, T, topo):
     def slide(z, r):
         return w_("ZW", 160 * z + 15 - r, 128)
 
-    def lin(n, terms, e="s"):
+    def lin(n, terms):
         for k, (i, w) in enumerate(terms):
-            o = col(n if k == len(terms) - 1 else n + str(k))
-            if e == "s":
-                act(o, ic(i), AF.Identity, bias=col(n + str(k - 1)) if k else 0.0, scale=float(w))
-            else:
-                ts(o, ic(i), float(w), AL.mult, col(n + str(k - 1)) if k else 0.0, AL.add)
-
-    def sel(o, i, pat, cmp, fill, base, cm=1):
-        op("g", lambda: g.affine_select(o[0], i[0], pat, cmp, fill, base, cm), [o], [i])
+            lin2(col(n if k == len(terms) - 1 else n + str(k)), ic(i), col(n + str(k - 1)) if k else 0.0, float(w))
 
     def terms(o, lst, first=True):
-        n = o[1][0][2] - o[1][0][1]
+        n = o[3]
         for (i, j, w) in lst:
             pat = [[-16, 8]] if n == 8 else [[-16, n // 16], [0 if j is None else 256, 16]]
             sel(o, s("ZERO", 0, n) if first else o, pat, AL.not_equal, float(w), -i - 256 * (j or 0))
@@ -217,37 +380,39 @@ def rank_program(g, core, T, topo):
     row = lambda i: slice(i, 128, 16)
     AREP, XREP = s("A", H, V), s("X", H, V)
     AW, XW_ = s("A"), s("X")
-    IO128, ID, G8, BD = s("IO", 0, 128), shift(0), s("G8"), M("BD")
+    ID, G8, BD = shift(0), s("G8"), M("BD")
+    Z128, O128 = s("ZERO", 0, 128), s("ONES", 0, 128)
 
-    dma("y", s("OVI"), ext(T.ov[:]))
-    dma("s", s("VA", 0, C), ext(T.va[:]))
-    dma("y", s("NLI"), ext(T.nl[:]))
-    dma("y", s("WI"), ext(T.wv[:]))
-    dma("y", s("SI"), ext(T.sc[:]))
-    dma("y", XREP, ext(T.xv[:, H:V]))
+    first = [dma("y", s("OVI"), ext(T.ov[:]), 65536), dma("y", s("WI"), ext(T.wv[:]), 98304)]
+    ms(s("ZERO"), 0.0)
+    for i in (4, 5):
+        first.append(dma("y", s("DEW", 0, V, p=row(i)), s("ZERO", 0, 192), 49152))
+    for x in range(0, C, VAW):
+        va_in = dma("y", w_("VA", x, VAW), ext(T.va[:, x:x + VAW]), 512 * VAW, after=first)
+        nodes[va_in]["order"] = set(first)
+    dma("y", s("NLI"), ext(T.nl[:]), 8192)
+    dma("y", s("SI"), ext(T.sc[:]), 65536)
+    dma("y", XREP, ext(T.xv[:, H:V]), 49152)
     iota(s("II", 0, 1), [[0, 1]], 0, 1, False)
     iota(s("IO"), [[1, 256]], 0, 0)
     iota(s("JW"), [[16, 128]], 0, 1)
-    iota(s("II", 16, 48), [[16, 2], [1, 2], [2, 8]], 0, 0, False)
+    iota(s("II", 16, 48), [[1, 32]], 0, 0, False)
     iota(s("II", 48, 56), [[16, 8]], 15, 0, False)
-    iota(s("DEW", V, DV0 + C), [[0, DV0 + C - V]], 0, 0)
-    iota(s("ONES"), [[0, 256]], 1, 0)
-    iota(s("ZERO"), [[0, 256]], 0, 0)
+    ms(s("ONES"), 1.0)
     sel(s("ZW", 0, 160), s("ZERO", 0, 160), [[-1, 160]], AL.not_equal, 1.0, 16)
     iota(M("SELK"), [[0, 8], [4096, 16]], 2048, 0)
     sel(M("SELK"), M("SELK"), [[-16, 8], [0, 16]], AL.is_equal, 0.0, -6)
     terms(M("SELK"), [(0, None, 65536), (4, None, 256), (5, None, 1)], False)
-    sel(s("RSB"), s("ZERO"), [[0, 16], [1, 16]], AL.not_equal, BIG, 0, 0)
+    lin2(s("RSB"), s("ZERO"))
+    lin2(s("RSB", 0, 256, 16), s("ONES", 0, 16), scale=BIG)
     sel(G8, s("ONES", 0, 8), [[-16, 8]], AL.is_ge, 0.0, 0)
     sel(G8, G8, [[16, 8]], AL.is_ge, 0.0, 15, -1)
-    SELC = sm("SELC", 24)
-    SELW = w_("SM", 8, 8)
-    terms(w_("SM", 0, 8), [(0, None, 65536)])
-    terms(SELW, [(0, None, 1)])
-    terms(w_("SM", 16, 8), [(4, None, 256), (5, None, 1)])
-    sel(s("IDF"), s("ZERO", 0, 128), [[-1, 128]], AL.not_equal, 1.0, 0)
-    ms(s("DEW", 0, V), 0.0)
-    act(s("CODE", 0, H), s("DEW", 0, H))
+    terms(sm("SELS"), [(0, None, 65536)])
+    terms(sm("SELC"), [(4, None, 256), (5, None, 1)])
+    lin2(s("IDF"), ID)
+    ms(s("CODE", 0, 960), 0.0)
+    for x in (960, 1920):
+        dma("y", w_("CODE", x, 960), s("CODE", 0, 960), 245760, after=[va_in])
     ms(s("TMP", 0, 8), 2.0)
     ms(s("TMP", 8, 136), 0.0)
     ts(s("II", 1, 2), s("II", 0, 1), 15, AL.bitwise_and)
@@ -263,551 +428,461 @@ def rank_program(g, core, T, topo):
         col("w5_%d" % n)
     for n in range(4):
         col("w4_%d" % n)
-    lin("h5", [(5, 0.5)], "v")
-    lin("h4", [(4, 0.5)], "v")
-    ts(s("TF", 0, 16), s("IC"), -2.0, AL.mult, 1.0, AL.add)
-    lin("ca", [(0, 255), (4, -8), (6, 1), (7, 1)], "v")
+    lin("h5", [(5, 0.5)])
+    lin("h4", [(4, 0.5)])
+    ts(s("TF", 128, 144), s("IC"), -2.0, AL.mult, 1.0, AL.add)
+    lin("cw", [(4, -8), (6, 1), (7, 1)])
+    lin2(col("ca"), ic(0), col("cw"), 255.0)
     scan(w_("CF", cols["w5_0"], 8), s("TMP", 0, 8), s("TMP", 8, 16), col("h5"), AL.mult, AL.add)
     scan(w_("CF", cols["w4_0"], 4), s("TMP", 0, 4), s("TMP", 8, 12), col("h4"), AL.mult, AL.add)
-    ts(s("A", 0, 256), s("IO"), ic(5), AL.mult, col("ca"), AL.add)
-    ts(col("n0"), ic(0), -1.0, AL.mult, 1.0, AL.add)
-
-    def bits(bs):
-        for b in bs:
-            n = 1 << b
-            w = min(n, DV0 - n)
-            act(w_("BITS", n, w), s("BITS", 0, w), scale=w_("TF", b, 1))
-    bits(range(10))
-    for k in range(4):
-        n = 256 << k
-        w = min(n, VW - n)
-        ts(w_("A", n, w), s("A", 0, w), col("w4_%d" % k), AL.add)
-    act(s("CW"), s("A", 0, CWD), scale=col("n0"))
+    for win, c0, wd in (("A", "ca", VW), ("CW", "cw", CWD))[:2 - CWDMA]:
+        lin2(s(win, 0, 256), s("IO"), col(c0), ic(5))
+        for k in range(4):
+            n = 256 << k
+            w = min(n, wd - n)
+            lin2(w_(win, n, w), s(win, 0, w), col("w4_%d" % k))
+    for gg in range(8 * CWDMA):
+        pp = slice(16 * gg + 1, 16 * gg + 16)
+        dma("y", s("CW", p=pp), s("A", 0, CWD, p=pp), 69120)
+    if CWDMA:
+        dma("y", s("CW", C, CWD, p=row(0)), s("ZERO", 0, 16), 4096)
+    for b in range(12):
+        n = 1 << b
+        w = min(n, DV0 - n)
+        lin2(w_("BITS", n, w), s("BITS", 0, w), scale=w_("TF", 128 + b, 1))
     cp(s("WB"), s("WI"))
-    cp(s("DVAL", 0, 16), s("A", 0, C, 128))
+    lin2(s("DVAL", 0, 16), s("IO", 0, 16), col("cw0"), col("h4"))
     ts(s("JW"), s("JW"), col("g16"), AL.subtract)
-    dma("y", s("A", 0, V, p=row(0)), s("WB"))
-    bits(range(10, 12))
-    act(s("MASKR", 0, 16), s("IC"))
+    dma("y", s("A", 0, V, p=row(0)), s("WB"), 49152)
+    lin2(s("MASKR", 0, 16), s("IC"))
     for k in range(5):
-        act(w_("MASKR", 16 << k, 16 << k), s("MASKR", 0, 16 << k))
+        lin2(w_("MASKR", 16 << k, 16 << k), s("MASKR", 0, 16 << k))
     for k in range(7):
-        ts(s("DVAL", 16 << k, 32 << k), s("DVAL", 0, 16 << k), col("w5_%d" % k), AL.add)
+        lin2(s("DVAL", 16 << k, 32 << k), s("DVAL", 0, 16 << k), col("w5_%d" % k))
     ts(s("TMP", 128, 256), s("OVI"), float(V), AL.is_ge)
-    ts(s("TMP2", 128, 256), s("JW"), 16.0, AL.add)
+    lin2(s("TMP2", 128, 256), s("JW"), 16.0)
     cp(s("SBF"), s("SI"))
     tt(s("TMP", 128, 256), s("TMP", 128, 256), s("TMP2", 128, 256), AL.mult)
     cp(s("LN", 0, 16), s("NLI"))
     tt(s("OV2", 0, 128), s("TMP", 128, 256), s("OVI"), AL.add)
-    dma("y", s("CW", 0, C, p=row(0)), s("SBF"))
+    dma("y", s("CW", 0, C, p=row(0)), s("SBF"), 32768)
     cp(s("OVL"), s("OV2", 0, 128))
-    ms(s("U12", 16, 28), 4.0)
-    scan(s("U12", 0, 12), s("U12", 16, 28), s("TMP", 16, 28), 0.25, AL.mult, AL.add)
-    cp(s("VARS"), ind(s("VA"), s("LN", 0, 16)))
-    cp(ind(s("DEW"), s("OVL")), s("DVAL"))
-    dma("y", s("X", 0, H), ext(T.xv[:, 0:H]))
-    dma("y", s("KK", 0, C), ext(T.kc[:]))
-    send(0, [w_("X", H + S * d, S) for d in range(3)], "LA", 0, S)
-    iota(s("JT", 0, 16), [[0, 8], [128, 2]], 0, 1)
-    iota(s("JT", 16, 32), [[0, 8], [128, 2]], DV0, 1)
-    iota(s("VT"), [[0, 256]], 0, 0)
-    sel(BD, s("ONES", 0, 128), [[-16, 8], [0, 16]], AL.is_ge, 0.0, 0)
+    VARS0 = s("VARS", 0, 256)
+    cp(VARS0, ind(s("VA"), s("LN", 0, 16)))
+    for j in range(4):
+        cp(ind(s("DEW"), w_("OVL", 32 * j, 32)), w_("DVAL", 512 * j, 512))
+    send([w_("X", H + S * d, S) for d in range(3)], "LA", 0, S)
+    iota(s("JT", 0, 16), [[128, 2], [0, 8]], 0, 1)
+    iota(s("JT", 16, 32), [[128, 2], [0, 8]], DV0, 1)
+    lin2(s("VT"), s("CODE", 0, 272))
+    sel(BD, O128, [[-16, 8], [0, 16]], AL.is_ge, 0.0, 0)
     sel(BD, BD, [[16, 8], [0, 16]], AL.is_ge, 0.0, 15, -1)
     terms(sm("SELE"), [(2, None, 256), (3, None, 1)])
-    terms(M("SV1"), [(4, 4, 1), (5, 5, 1), (6, 6, 1)])
+    terms(M("SV1"), [(4, 4, 1), (5, 5, 1), (6, 6, 1), (6, 1, 1)])
     terms(M("SV2"), [(4, 2, 1), (5, 3, 1)])
-    for d in range(3):
-        sel(M("PI%d" % d), s("ZERO", 0, 128), [[16, 8], [-1, 16]], AL.not_equal, 1.0, -16 * (d + 1))
-        sel(M("PI%d" % d), M("PI%d" % d), [[16, 8], [-1, 16]], AL.not_equal, 1.0, -16 * (d + 1) - 128)
+    sel(s("PIT"), s("ZERO", 0, 160), [[16, 10], [-1, 16]], AL.not_equal, 1.0, -48)
+    sel(s("PIT"), s("PIT"), [[16, 10], [-1, 16]], AL.not_equal, 1.0, -48 - 128)
     sel(M("B7"), BD, [[0, 8], [1, 16]], AL.is_equal, 0.0, -7, 0)
     terms(M("K1"), [(0, 1, 1), (6, 1, 1), (6, 7, 1)])
     terms(M("K3"), [(2, 1, -1)])
     iota(s("II", 12, 15), [[16, 3]], 143 + 16, -1, False)
     iota(s("GI"), [[16, 8], [0, 16]], 0, 0)
     terms(M("SK"), [(1, None, -1)])
-    terms(M("SD"), [(i, i, -1) for i in (0, 1, 2, 3, 7)])
-
-    def steal_consts():
-        cp(s("ELX", 0, 40), s("II", 16, 56))
-        ts(col("od"), col("odd"), 1.0 / 16, AL.mult)
-        ts(col("ev"), col("odd"), 1.0, AL.is_lt)
-        ms(s("TMP2", 0, 128), 0.5)
-        ms(s("YY", 0, 1), 0.0)
-        scan(s("TMP2", 128, 256), s("TMP2", 0, 128), s("ZERO", 0, 128), 2.0 ** 61, AL.mult, AL.add)
-        ts(s("BASEW", 0, 16), s("JW", 0, 16), float(DV0), AL.add)
-        tt(s("TMP2", 128, 256), s("TMP2", 128, 256), s("IDF"), AL.mult)
-        red(col("pow"), s("TMP2", 128, 256))
-        ts(col("thr"), col("pow"), 2.5, AL.mult)
-
-    def meet_consts():
-        lin("kh", [(1, 1), (6, 0.5)])
-        lin("kl", [(1, 1), (6, -0.5)])
-        lin("r07", [(0, 1), (7, 1)])
-        ts(s("II", 12, 15), s("II", 12, 15), 112, AL.bitwise_and)
-        for n in range(3):
-            col("pg%d" % n)
-        cp(w_("CF", cols["pg0"], 3), s("II", 12, 15))
-        act(s("BASEW", 32, 48), s("JW", 0, 16), AF.Identity, bias=float(C))
-        act(s("BASEW", 16, 32), s("JW", 0, 16), AF.Identity, bias=float(C), scale=0.0)
-        for d in range(3):
-            act(M("PD%d" % d), M("PI%d" % d), scale=col("r07"))
-            ts(M("PK%d" % d), s("GI"), col("pg%d" % d), AL.is_equal, col("kh" if high[d] else "kl"), AL.mult)
-
-    def out_rows():
-        ts(s("OV2", 128, 256), s("OVI"), 8, AL.arith_shift_right)
-        ts(s("OV2", 256, 384), s("OVI"), 255, AL.bitwise_and)
-        ts(s("OVB", 0, 128), s("OV2", 128, 256), -8.0, AL.add)
-        cp(s("OVB", 128, 256), s("OV2", 256, 384))
-        dma("y", s("OW", 0, C, p=row(4)), s("OVB", 0, 128))
-        dma("y", s("OW", 0, C, p=row(5)), s("OVB", 128, 256), True)
+    sel(M("SD"), Z128, [[-1, 128]], AL.not_equal, -1.0, 0)
+    sel(M("SD"), M("SD"), [[0, 8], [-1, 16]], AL.is_ge, 0.0, 3, 0)
+    terms(M("SD"), [(7, 7, -1)], False)
+    cp(s("ELX", 0, 40), s("II", 16, 56))
+    lin2(col("od"), col("odd"), scale=1.0 / 16)
+    ts(col("ev"), col("odd"), 1.0, AL.is_lt)
+    ms(s("TMP2", 0, 128), 0.5)
+    ms(s("YY", 0, 1), 0.0)
+    scan(s("T192", 0, 128), s("TMP2", 0, 128), Z128, 2.0 ** 61, AL.mult, AL.add)
+    lin2(s("BASEW", 0, 16), s("JW", 0, 16), float(DV0))
+    tt(s("T192", 0, 128), s("T192", 0, 128), s("IDF"), AL.mult)
+    red(col("pow"), s("T192", 0, 128))
+    lin2(w_("CODE", H, 16), s("IC"))
+    for n, w in ((16, 16), (32, 32), (64, 64), (128, 64)):
+        lin2(w_("CODE", H + n, w), w_("CODE", H, w), scale=4.0 ** (n // 16), extra=VAP_X)
+    lin("kh", [(1, 1), (6, 0.5)])
+    lin("kl", [(1, 1), (6, -0.5)])
+    lin("r07", [(0, 1), (7, 1)])
+    ts(s("II", 12, 15), s("II", 12, 15), 112, AL.bitwise_and)
+    for n in range(3):
+        col("pg%d" % n)
+    cp(w_("CF", cols["pg0"], 3), s("II", 12, 15))
+    lin2(s("BASEW", 32, 48), s("JW", 0, 16), float(C))
+    ms(s("BASEW", 16, 32), float(C))
+    for d in range(3):
+        lin2(M("PD%d" % d), M("PI%d" % d), scale=col("r07"))
+        ts(M("PK%d" % d), s("GI"), col("pg%d" % d), AL.is_equal, col("kh" if high[d] else "kl"), AL.mult)
+    fill("OW", 0, CWD)
+    ts(s("OV2", 128, 256), s("OVI"), 8, AL.arith_shift_right)
+    ts(s("OV2", 256, 384), s("OVI"), 255, AL.bitwise_and)
+    ts(s("OVB", 0, 128), s("OV2", 128, 256), -8.0, AL.add)
+    cp(s("OVB", 128, 256), s("OV2", 256, 384))
+    dma("y", s("OW", 0, C, p=row(4)), s("OVB", 0, 128), 32768)
+    dma("y", s("OW", 0, C, p=row(5)), s("OVB", 128, 256), 32768)
+    for q in range(16):
+        cp(w_("VAP", 128 * q, 128), s("VA", q, C, 16), extra=VAP_X - 3 * q)
+    fill("X", V, VW)
+    terms(M("STL"), [(6, None, STALE), (7, None, -STALE)])
+    terms(s("ZW", 800, 960), [(0, 15, 1)])
+    fill("C256", 0, 256, 256)
+    fill("KK", C, CWD)
+    lin("t8", [(8, 4096)])
+    lin2(s("CW2", C, CWD), s("ONES"), scale=col("t8"))
+    fill("CH0", 0, VW)
+    terms(s("ZW", 160, 320), [(4, 15, 256), (5, 15, 1)])
+    terms(M("BU22"), [(7, None, -2 ** 22)])
+    terms(M("BU"), [(7, None, 1)])
+    terms(M("BDE"), [(2, 8, 2 ** 20), (3, 8, 4096), (2, 9, -2 ** 20), (3, 9, -4096)])
+    terms(M("NBO"), [(4, 8, -2 ** 20), (5, 8, -4096), (4, 9, 2 ** 20), (5, 9, 4096), (0, 0, 1), (6, 4, 4), (6, 6, 1)])
+    terms(M("BO"), [(4, None, 256), (5, None, -1)])
+    terms(M("MN"), [(4, 4, -1), (6, 4, 4), (5, 5, 1), (6, 6, 1)])
+    terms(sm("SELW"), [(0, None, 1)])
+    terms(sm("SELD"), [(4, None, 256), (5, None, 1), (6, None, -1024)])
+    terms(sm("SN"), [(13, None, -1)])
+    terms(sm("SF"), [(6, None, 1)])
+    if NMK < 32:
+        terms(sm("S8"), [(8, None, 1)])
+        terms(M("SU"), [(7, 8, 1)])
+    terms(M("MO"), [(4, 4, -1), (5, 5, 1)])
+    terms(M("BNH"), [(8, None, 2), (9, None, 2)])
+    terms(s("ZW", 480, 640), [(4, 15, -256), (5, 15, 1), (8, 15, 1), (9, 15, 1)])
+    terms(s("ZW", 640, 800), [(0, 15, -4096)])
+    for n, w in (("NID", -1.0 / 256), ("IDS", 1.0 / 256), ("ID16", 16.0)):
+        sel(M(n), Z128, [[-1, 128]], AL.not_equal, w, 0)
+    sel(M("PERM"), Z128, [[-1, 4], [-4, 32]], AL.not_equal, 1.0, 0)
+    iota(s("II", 64, 72), [[16, 2], [32, 4]], 0, 0, False)
+    ts(s("ELX", 40, 48), s("II", 64, 72), col("i"), AL.add)
+    sel(sm("G8B"), G8, [[0, 8]], AL.is_ge, 0.0, 0)
+    if EARLY:
+        lin2(M("BD22"), BD, scale=-2.0 ** 22)
+    sel(s("RS1"), O128, [[0, 8], [1, 16]], AL.not_equal, 0.0, 0, 0)
+    iota(s("JI"), [[1, 16], [16, 16]], 0, 0)
+    iota(s("J1"), [[1, 256]], 1, 0)
+    lin2(s("POS", 128, 144), s("JW", 0, 16), 1.0)
+    lin2(s("BASEW", 48, 64), s("JW", 0, 16), float(DV0 - V))
+    lin2(s("BASEW", 64, 80), s("JW", 0, 16), float(DV0 - V - 4096))
+    lin2(col("g15"), col("g16"), 15.0)
+    ts(s("ZW", 320, 480), s("IO", 0, 160), col("g15"), AL.is_equal, col("i"), AL.mult)
+    for t in range(4):
+        r = 40 * t
+        for n, cmp in (("TRI", AL.is_ge), ("TRS", AL.is_gt)):
+            o = M("%s%d" % (n, t))
+            sel(o, O128, [[1, 128]], cmp, 0.0, r, -1)
+            if t:
+                c0 = o[1][0][1]
+                sel(s("MAT", c0, c0 + 128, p=slice(0, r)), s("ONES", 0, 128, p=slice(0, r)), [[1, 128]], cmp, 0.0, r - 128, -1)
+        for n, w in (("PM", 1.0), ("PM4", 4096.0)):
+            o = M("%s%d" % (n, t))
+            sel(o, Z128, [[1, 128]], AL.not_equal, w, r, -1)
+            if t:
+                sel(o, o, [[1, 128]], AL.not_equal, w, r - 128, -1)
+        for h, last in ((0, 1), (1, 128 - (127 + r) % 128)):
+            o = w_("RH", 32 * t + 16 * h, 16)
+            iota(o, [[1, 16]], last, 0)
+            sel(o, o, [[0, 16]], AL.is_equal, 1.0, -127)
+            if h and t:
+                sel(o, o, [[0, 16]], AL.not_equal, -127.0, r - 127)
 
     def first_replicas():
-        for d in range(3):
-            mm(w_("P7", S * d, S), M("PI%d" % d), w_("LA", S * d, S))
+        mmx([(w_("P7", S * d, S), M("PI%d" % d), w_("LA", S * d, S)) for d in range(3)])
         tt(s("NE"), s("P7", 0, 192), XREP, AL.not_equal)
         tt(s("DX"), s("P7", 0, 192), XREP, AL.subtract)
-        cp(s("XR0"), XREP)
+        lin2(s("XR0"), XREP)
         mm(s("P7", 0, 192), M("K1"), AREP)
         mms([(s("P7", 256, 448), M("K3"), AREP)] + [(w_("P7", 256 + S * d, S), M("B7"), w_("NE", S * d, S)) for d in range(3) if high[d]])
         ts(s("LS"), s("P7", 256, 448), 0.0, AL.is_gt)
         tt(s("LS"), s("P7", 0, 192), s("LS"), AL.mult)
         tt(AREP, AREP, s("LS"), AL.add)
 
-    CR = [13, 14, 15, 7]
+    def replica_digits():
+        for h in range(NMK):
+            b0 = 16384 + 1024 * (h % 16)
+            for x in range(0, 64, MP):
+                lin2(w_("GR", b0 + 16 * x, 16 * MP), ind(s("CODE"), w_("VAP", 64 * h + x, MP)))
+            mms([(w_("P7", 64 * (h % 8), 64), ID, s("GR", b0 + k, b0 + 1024, 16)) for k in range(16)])
+            if h % 4 == 3 or h == NMK - 1:
+                h0 = h - h % 4
+                lin2(s("MK", 64 * h0, 64 * h + 64), s("P7", 64 * (h0 % 8), 64 * (h % 8) + 64))
 
-    def plan_consts(part):
-        Z128, O128 = s("ZERO", 0, 128), s("ONES", 0, 128)
-        if part == 0:
-            iota(s("OW"), [[0, CWD]], 0, 0)
-            iota(s("X", V, VW), [[0, VW - V]], 0, 0)
-            iota(s("C4K"), [[0, 256]], int(STALE), 0)
-            terms(s("ZW", 160, 320), [(4, 15, 256), (5, 15, 1)])
-            terms(M("BU22"), [(7, None, 2 ** 22)])
-            terms(M("BU"), [(7, None, 1)])
-            terms(M("BDE"), [(2, 1, 256), (3, 1, 1)])
-            terms(M("NBO"), [(4, 1, -256), (5, 1, -1), (0, 0, 1), (6, 6, 1)])
-            terms(M("BO"), [(4, None, -256), (5, None, 1)])
-            terms(sm("SF"), [(6, None, 1)])
-            terms(sm("S8"), [(8, None, 1)])
-            terms(M("SU"), [(7, 8, 1)])
-        if part == 1:
-            terms(M("MO"), [(4, 4, -1), (5, 5, 1)])
-            terms(M("MAB"), [(0, 0, 1), (6, 6, 1), (6, 4, 4), (1, 4, -4096), (1, 5, -4096), (1, 6, -4096), (1, 7, 4096)])
-            terms(M("BNH"), [(7, None, 32)])
-            terms(s("ZW", 480, 640), [(4, 15, -256), (5, 15, 1), (6, 15, -4096)])
-            for n, w in (("NID", -1.0), ("ID16", 16.0), ("ID256", 256.0)):
-                sel(M(n), Z128, [[-1, 128]], AL.not_equal, w, 0)
-            sel(sm("G8B"), G8, [[0, 8]], AL.is_ge, 0.0, 0)
-            sel(s("RS1"), O128, [[0, 8], [1, 16]], AL.not_equal, 0.0, 0, 0)
-            iota(s("JI"), [[1, 16], [16, 16]], 0, 0)
-            iota(s("J1"), [[1, 256]], 1, 0)
-            iota(s("KK", C, CWD), [[0, CWD - C]], 0, 0)
-            iota(s("CW2", C, CWD), [[0, CWD - C]], 0, 0)
-            act(s("POS", 128, 144), s("JW", 0, 16), AF.Identity, bias=1.0)
-            act(s("BASEW", 48, 64), s("JW", 0, 16), AF.Identity, bias=float(DV0 - 7168))
-            ts(col("g15"), col("g16"), 15.0, AL.add)
-            ts(s("ZW", 320, 480), s("IO", 0, 160), col("g15"), AL.is_equal, col("i"), AL.mult)
-        if part >= 2:
-            t = part - 2
-            r = 40 * t
-            for n, cmp in (("TRI", AL.is_ge), ("TRS", AL.is_gt)):
-                o = M("%s%d" % (n, t))
-                sel(o, O128, [[1, 128]], cmp, 0.0, r, -1)
-                if t:
-                    c0 = o[1][0][1]
-                    sel(s("MAT", c0, c0 + 128, p=slice(0, r)), s("ONES", 0, 128, p=slice(0, r)), [[1, 128]], cmp, 0.0, r - 128, -1)
-            for n, w in (("PM", 1.0), ("PM4", 4096.0)):
-                o = M("%s%d" % (n, t))
-                sel(o, Z128, [[1, 128]], AL.not_equal, w, r, -1)
-                if t:
-                    sel(o, o, [[1, 128]], AL.not_equal, w, r - 128, -1)
-            sel(M("SCH%d" % t), BD, [[0, 8], [1, 16]], AL.is_equal, 0.0, -9 - t, 0)
-            terms(M("SCL%d" % t), [(0, CR[t], 1)])
-            terms(M("BCH%d" % t), [(9 + t, None, 2 ** 22)])
-            terms(sm("SN%d" % t), [(CR[t], None, -1)])
-            terms(sm("SR%d" % t), [(9 + t, None, 1)])
-            for h, last in ((0, 1), (1, 128 - (127 + r) % 128)):
-                o = w_("RH", 32 * t + 16 * h, 16)
-                iota(o, [[1, 16]], last, 0)
-                sel(o, o, [[0, 16]], AL.is_equal, 1.0, -127)
-                if h and t:
-                    sel(o, o, [[0, 16]], AL.not_equal, -127.0, r - 127)
+    def lane_numbers():
+        mmx([(w_("P1", 16 * i + 8 * h, 8), w_("SR", 128 * h, 128), sm(n)) for h in range(2) for i, n in enumerate(("SELS", "SELC"))])
+        lin2(s("SCT"), s("P1", 0, 32))
 
-    def permute(qs):
-        for q in qs:
-            cp(w_("VAP", 128 * q, 128), s("VA", q, C, 16))
-
-    def new_outputs(m):
-        cp(ind(s("OW"), w_("LN", 32 * (m + 1) + 16, 16)), w_("VAL", 256 * m, 256))
-
-    def stale_marks(m):
-        cp(ind(XW_, w_("L2", 16 * m, 16)), s("C4K"))
-
-    bg = [0, 0, 0]
-
-    def mask_gather(n, e="s"):
-        for _ in range(n):
-            if bg[0] < 32:
-                h = bg[0]
-                gat(e, w_("GR", 16384 + 1024 * (h % 16), 1024), ind(s("CODE"), w_("VAP", 64 * h, 64)))
-                bg[0] += 1
-
-    def mask_fold(n):
-        for _ in range(n):
-            if bg[1] < min(bg[0], bg[2] + 8):
-                h = bg[1]
-                b0 = 16384 + 1024 * (h % 16)
-                mms([(w_("P7", 64 * (h % 8), 64), ID, s("GR", b0 + k, b0 + 1024, 16)) for k in range(16)])
-                bg[1] += 1
-
-    def mask_keep():
-        while bg[2] + 4 <= bg[1]:
-            act(w_("MK", 64 * bg[2], 256), w_("P7", 64 * (bg[2] % 8), 256))
-            bg[2] += 4
-
-    act(s("GR", 0, 2048), ind(AW, s("VARS", 0, 128)))
     for m in range(4):
-        if m:
-            for j in range(4):
-                gat("vs"[j & 1], w_("GR", 1024 * j, 1024), ind(AW, w_("VARS", 64 * j, 64)))
-        else:
-            act(s("GR", 2048, 4096), ind(AW, s("VARS", 128, 256)))
+        for j in range(4):
+            lin2(w_("GR", 1024 * j, 1024), ind(AW, w_("VARS", 64 * j, 64)))
         if m == 0:
-            dma("y", s("A", 0, V, p=row(2)), s("DEW", 0, V, p=row(4)))
-            dma("s", s("A", 0, V, p=row(3)), s("DEW", 0, V, p=row(5)), True)
-            act(s("SR"), ind(s("CW"), s("LN", 0, 16)))
-        else:
-            mask_fold(1)
+            dma("y", s("A", 0, V, p=row(2)), s("DEW", 0, V, p=row(4)), 49152)
+            dma("y", s("A", 0, V, p=row(3)), s("DEW", 0, V, p=row(5)), 49152)
+            lin2(s("SR"), ind(s("CW"), s("LN", 0, 16)))
         for h in range(2):
-            for k in range(16):
-                mm(s("P0", 16 * h + k, 256, 32), s("GR", 2048 * h + k, 2048 * h + 2048, 16), s("MAT", mats["SELK"] * 128 + k, mats["SELK"] * 128 + 128, 16))
+            mmx([(s("P0", 128 * h + k, 128 * h + 128, 16), s("GR", 2048 * h + k, 2048 * h + 2048, 16), s("MAT", mats["SELK"] * 128 + k, mats["SELK"] * 128 + 128, 16)) for k in range(16)])
         if m == 0:
-            steal_consts()
-            for h in range(2):
-                mm(s("P1", h, 48, 2), w_("SR", 128 * h, 128), SELC)
-            act(s("SCT"), s("P1", 0, 48))
-            for u in range(16):
-                act(w_("CODE", H + 12 * u, 12), s("U12", 0, 12), scale=ic(u))
-        else:
-            mask_keep()
-            mask_fold(1)
-            new_outputs(m - 1)
-            act(w_("SQ", 192 * (m - 1), 192), w_("TT", 192 * (m - 1), 192), AF.Abs)
-            mask_gather(1)
+            lane_numbers()
         scan(s("M1"), s("RSB"), s("P0", 0, 256), 0.0, AL.add, AL.min)
+        tt(s("YY", 1, 256), s("M1", 0, 255), s("P0", 1, 256), AL.max)
         cp(s("TI", 0, 16), s("M1", 15, 256, 16))
         ts(s("OI"), s("TI", 0, 16), 4095, AL.bitwise_and)
         tt(s("EXP", 0, 256), ind(s("OI"), s("ELX", 0, 16)), s("MASKR", 0, 256), AL.mult)
-        for h in range(2):
-            mm(w_("P1", 64 + 8 * h, 8), w_("EXP", 128 * h, 128), G8)
-        tt(s("YY", 1, 256), s("M1", 0, 255), s("P0", 1, 256), AL.max)
+        mmx([(w_("P1", 64 + 8 * h, 8), w_("EXP", 128 * h, 128), G8) for h in range(2)])
         LIVE = s("TF", 16, 32)
         tt(LIVE, s("M1", 15, 256, 16), s("SCT", 0, 16), AL.is_lt)
         cp(s("L1"), s("P1", 64, 80))
-        ts(s("BE"), ind(s("BITS"), s("L1")), col("ev"), AL.mult)
-        act(s("BO"), ind(s("BITS"), s("L1")), scale=col("od"))
-        act(s("GO"), ind(AW, s("L1")))
+        lin2(s("BE"), ind(s("BITS"), s("L1")), scale=col("ev"))
+        lin2(s("BO"), ind(s("BITS"), s("L1")), scale=col("od"))
+        if m == 0:
+            first_replicas()
+        lin2(s("GO"), ind(AW, s("L1")))
+
         def gram(gg, bank, c0, lo):
             B, pp = ("BE", "BO")[gg & 1], slice(32 * (gg // 2), 32 * (gg // 2) + 32)
             mm(w_(bank, c0, 256 - lo), s(B, lo, lo + 128, p=pp), s(B, lo, 256, p=pp), tile=gg // 2)
-        for gg in (0, 1, 2, 3):
+        for gg in range(8):
             gram(gg, "P%d" % (2 + gg // 2), 256 * (gg & 1), 0)
-        for gg in (0, 1, 4, 5):
-            gram(gg, "P0" if gg >= 4 else "P6", 128 * (gg % 4), 128)
-        for gg in (4, 5, 6, 7):
-            gram(gg, "P%d" % (2 + gg // 2), 256 * (gg & 1), 0)
-        for gg in (2, 3, 6, 7):
+        for gg in range(8):
             gram(gg, "P0" if gg >= 4 else "P6", 128 * (gg % 4), 128)
         scan(s("M2"), s("YY"), s("RSB"), 0.0, AL.min, AL.max)
         ts(s("WL", 0, 16), LIVE, col("pow"), AL.mult)
-        ts(s("WL", 16, 32), LIVE, 2.0 ** 62, AL.mult)
+        ts(s("WL", 16, 24), s("TF", 16, 24), 2.0 ** 62, AL.mult)
         tt(s("TI", 16, 32), s("M2", 15, 256, 16), s("SCT", 0, 16), AL.min)
         tt(s("DO"), s("OI"), s("JT", 16, 32), AL.subtract)
         ts(s("TI", 32, 48), s("TI", 16, 32), 16, AL.arith_shift_right)
-        ts(s("TF", 32, 48), LIVE, col("thr"), AL.mult)
-        act(s("TH", 0, 512), s("P2"), AF.Relu, bias=-11.0)
-        ts(s("TH", 512, 1024), s("P3"), 11.0, AL.is_gt)
-        act(s("TH", 1024, 1536), s("P4"), AF.Relu, bias=-11.0)
-        for h in range(2):
-            ts(s("VT", 128 * h, 128 * h + 128, 16), s("TI", 32 + h, 48, 2), 0.0, AL.add)
-            ts(s("VT", 128 * h + 1, 128 * h + 128, 16), s("TI", 32 + h, 48, 2), 1.0, AL.add)
-        act(s("TH", 1536, 2048), s("P5"), AF.Relu, bias=-11.0)
-        ts(s("TH", 2048, 2560), s("P6"), 11.0, AL.is_gt)
-        act(s("TH", 2560, 3072), s("P0"), AF.Relu, bias=-11.0)
-        tt(s("DOX"), ind(s("DO"), s("ELX", 0, 16)), s("MASKR", 0, 256), AL.mult)
-        if m == 0:
-            permute(range(0, 2))
-            mask_gather(1)
-            first_replicas()
-        else:
-            permute(range(4 * m, 2 + 4 * m))
-            mask_gather(1)
+        for j, b in enumerate((2, 3, 4, 5, 6, 0)):
+            over(w_("TH", 512 * j, 512), s("P%d" % b), 11.0)
+        cp(s("VT", 16, 272, 16), s("TI", 32, 48))
         th = lambda gg: 256 * gg
+        for g0 in range(0, 8, 2):
+            mmx([(w_("P1", 96 + gg, 1), w_("TH", th(gg), 128), w_("WL", gg, 1)) for gg in (g0, g0 + 1)])
         for gg in range(8):
-            mm(w_("P1", 96 + 2 * gg, 1), w_("TH", th(gg), 128), w_("WL", 2 * gg, 1))
-        for gg in range(8):
-            o1 = w_("P1", 97 + 2 * gg, 1)
-            mms([(o1, w_("TH", th(gg) + 128, 128), w_("WL", 16 + 2 * gg, 1)), (o1, w_("TH", 2048 + 128 * gg, 128), w_("WL", 2 * gg + 1, 1))])
+            o1 = w_("P1", 104 + gg, 1)
+            mms([(o1, w_("TH", th(gg) + 128, 128), w_("WL", 16 + gg, 1)), (o1, w_("TH", 2048 + 128 * gg, 128), w_("WL", 8 + gg, 1))])
         PV = s("P2", 256, 512)
-        mms([(PV, M("SV1"), s("GO")), (PV, M("SV2"), s("SR"))] + [(w_("P2", 256 + 128 * h, 128), w_("VT", 128 * h, 128), ID) for h in range(2)])
+        mms([(PV, M("SV1"), s("GO")), (PV, M("SV2"), s("SR"))] + [(w_("P2", 256 + 128 * h, 128), w_("VT", 16 - i + 128 * h, 128), ID) for h in range(2) for i in range(2)])
         mm(s("P3", 0, 16), s("IDF"), s("BASEW", 0, 16), True, False)
-        tt(s("ACT"), s("P1", 96, 112), s("TF", 32, 48), AL.is_lt)
+        tt(s("ACT"), s("P1", 96, 112), s("WL", 0, 16), AL.is_lt)
         VAL = w_("VAL", 256 * m, 256)
-        act(VAL, PV)
-        tt(s("EXP", 0, 256), ind(s("ACT"), s("ELX", 0, 16)), s("DOX"), AL.mult)
+        lin2(VAL, PV)
+        tt(s("DO"), s("DO"), s("ACT"), AL.mult)
+        tt(s("EXP", 0, 256), ind(s("DO"), s("ELX", 0, 16)), s("MASKR", 0, 256), AL.mult)
         mms([(w_("P3", 8 * h, 8), w_("EXP", 128 * h, 128), G8) for h in range(2)], False)
-        for h in range(2):
-            mm(s("P2", h, 16, 2), w_("GO", 128 * h, 128), sm("SELE"))
-        if m:
-            stale_marks(m - 1)
-            mask_fold(1)
+        if m < 3:
+            mmx([(w_("P2", 8 * h, 8), w_("GO", 128 * h, 128), sm("SELE")) for h in range(2)])
         L2 = w_("L2", 16 * m, 16)
         cp(L2, s("P3", 0, 16))
         cp(ind(AW, L2), VAL)
-        send(1 + m, [w_("A", H + S * d, S) for d in range(3)], "LA", 192 * (m + 1), S)
-        plan_consts(m)
+        landed = send([w_("A", H + S * d, S) for d in range(3)], "LA", 192 * (m + 1), S)
         if m == 0:
-            meet_consts()
-        else:
-            mask_keep()
-            mask_fold(3)
-            mask_gather(3 if m < 3 else 4)
-        tt(s("TF", 80, 96), s("SCT", 32, 48), LIVE, AL.mult)
-        tt(s("TF", 112, 128), s("SCT", 32, 48), s("JT", 0, 16), AL.subtract)
-        tt(s("TF", 96, 112), s("P2", 0, 16), s("TF", 80, 96), AL.subtract)
+            dma("y", s("X", 0, H), ext(T.xv[:, 0:H]), 737280, after=[landed])
+        if m == 1:
+            dma("y", s("KK", 0, C), ext(T.kc[:]), 524288, after=[landed])
+        tt(s("TF", 112, 128), s("SCT", 16, 32), s("JT", 0, 16), AL.subtract)
         tt(s("NM", 16, 32), s("TF", 112, 128), s("ACT"), AL.mult)
-        tt(s("TF", 96, 112), s("TF", 96, 112), s("ACT"), AL.mult)
-        tt(s("NM", 0, 16), s("TF", 96, 112), s("TF", 80, 96), AL.add)
-        tt(s("EXP"), ind(s("NM"), s("ELX", 0, 32)), s("MASKR"), AL.mult)
-        mm(s("P4", 0, 192), M("SK"), AREP, True, False)
-        mm(s("P5", 0, 192), M("SD"), AREP, True, False)
-        mms([(s("P1", 160, 192), s("IDF"), s("BASEW", 16, 48))] + [(w_("P1", 160 + 8 * h, 8), w_("EXP", 128 * h, 128), G8) for h in range(4)])
-        if m == 0:
-            mask_gather(3)
-            out_rows()
-        permute(range(2 + 4 * m, 4 + 4 * m))
-        cp(w_("LN", 32 * (m + 1), 32), s("P1", 160, 192))
+        lo = 0 if m < 3 else 16
         if m < 3:
-            cp(s("VARS"), ind(s("VA"), w_("LN", 32 * (m + 1), 16)))
-            cp(s("SR"), ind(s("CW"), w_("LN", 32 * (m + 1), 16)))
-        else:
-            new_outputs(3)
+            tt(s("TF", 80, 96), s("SCT", 16, 32), LIVE, AL.mult)
+            tt(s("TF", 96, 112), s("P2", 0, 16), s("TF", 80, 96), AL.subtract)
+            tt(s("TF", 96, 112), s("TF", 96, 112), s("ACT"), AL.mult)
+            tt(s("NM", 0, 16), s("TF", 96, 112), s("TF", 80, 96), AL.add)
+        tt(s("EXP", 16 * lo, 512), ind(s("NM"), s("ELX", lo, 32)), s("MASKR", 16 * lo, 512), AL.mult)
+        mm(s("P4", 0, 192), M("SK"), AREP, True, False)
+        mms([(s("P5", 0, 192), M("SD"), AREP), (s("P5", 256, 448), ID, AREP)], True, False)
+        mms([(s("P1", 160 + lo, 192), s("IDF"), s("BASEW", 16 + lo, 48))] + [(w_("P1", 160 + 8 * h, 8), w_("EXP", 128 * h, 128), G8) for h in range(lo // 8, 4)])
+        cp(s("LN", 32 * (m + 1) + lo, 32 * (m + 2)), s("P1", 160 + lo, 192))
+        if m < 3:
+            cp(VARS0, ind(s("VA"), w_("LN", 32 * (m + 1), 16)))
+            lin2(s("SR"), ind(s("CW"), w_("LN", 32 * (m + 1), 16)))
+            lane_numbers()
+        cp(ind(s("OW"), w_("LN", 32 * (m + 1) + 16, 16)), VAL)
         LA = lambda d: w_("LA", 192 * (m + 1) + S * d, S)
         mms([(w_("P4", S * d, S), M("PK%d" % d), LA(d)) for d in range(3)], False)
         mms([(w_("P5", S * d, S), M("PD%d" % d), LA(d)) for d in range(3)], False)
-        if m < 3:
-            for h in range(2):
-                mm(s("P1", h, 48, 2), w_("SR", 128 * h, 128), SELC)
         TTm = w_("TT", 192 * m, 192)
         ts(s("LS"), s("P4", 0, 192), 0.0, AL.is_gt)
         tt(TTm, s("P5", 0, 192), s("LS"), AL.mult)
-        tt(AREP, AREP, TTm, AL.add)
-        if m < 3:
-            mask_fold(2)
-            act(s("SCT"), s("P1", 0, 48))
-        else:
-            tt(w_("SQ", 192 * m, 192), TTm, TTm, AL.mult)
+        tt(AREP, s("P5", 256, 448), TTm, AL.add)
+        act(w_("SQ", 192 * m, 192), TTm, AF.Abs)
+    replica_digits()
+    fill("CH1", 0, VW)
 
     def changed_digits(lst, n):
-        mms(lst)
-        tt(s("T192", 0, 192), lst[0][0], s("CODE", H, V), AL.min)
-        red(col(n), s("T192", 0, 192))
+        b, o = lst[0][0], s("T192", 0, 192)
+        mms([(b, ID, s("CODE", H, V))] + lst)
+        node({"s": (cost(o, [b], 1) + 0.02, lambda: g.scalar.activation(o[0], b[0], AF.Relu, accum_out=col(n)[0]))}, [o, col(n)], [b])
 
-    def mask_test(c0, n, wc):
-        ts(s("MT", 0, n), w_("MK", c0, n), col(wc), AL.add)
+    def mask_test(c0, n, wc, src=None):
+        ts(s("MT", 0, n), src or w_("MK", c0, n), col(wc), AL.subtract, float(0x555555), AL.add)
         ts(w_("MT", 512, n), s("MT", 0, n), 0xAAAAAA, AL.bitwise_and)
         ts(w_("MB", c0, n), w_("MT", 512, n), 0.0, AL.is_gt)
 
-    def outputs_checked(j, part):
-        cw, ow, ab = w_("CW", 512 * j, 512), w_("OW", 512 * j, 512), w_("AB", 512 * j, 512)
-        if part == 0:
-            b = s("P4" if j & 1 else "P5")
-            mms([(b, M("BDE"), w_("GV", 512 * j, 512)), (b, M("NBO"), cw)])
-            act(ab, b, AF.Abs)
-        else:
-            b = s("P7" if j & 1 else "P6")
-            mms([(b, M("MO"), ow), (b, M("MAB"), ab)])
-            act(w_("CW2", 512 * j, 512), b, AF.Relu)
+    def piece(win, lo, hi, **k):
+        lin2(s("GR", 1024 * lo, 1024 * hi), ind(win, s("VAP", 64 * lo, 64 * hi)), **k)
 
-    def replica_x():
-        for d in range(3):
-            ts(w_("T192", S * d, S), w_("P1", 256 + S * d, S), 1.0 if high[d] else 2.0, AL.is_equal)
-        ts(s("T192", 192, 384), s("P1", 256, 448), 0.0, AL.is_equal, STALE, AL.mult)
-        tt(s("T192", 0, 192), s("T192", 0, 192), s("DX"), AL.mult)
-        tt(s("T192", 0, 192), s("T192", 0, 192), s("XR0"), AL.add)
-        tt(XREP, s("T192", 0, 192), s("T192", 192, 384), AL.max)
-
-    mms([(s("P3", 256, 448), M("SU"), w_("SQ", 192 * m, 192)) for m in range(4)])
-    tt(AREP, s("P3", 256, 448), AREP, AL.add)
     changed_digits([(s("P6", 0, 192), M("BU22"), w_("SQ", 192 * m, 192)) for m in range(4)], "wd")
-
-    def piece(e, lo, hi):
-        gat(e, s("GR", 1024 * lo, 1024 * hi), ind(AW, s("VAP", 64 * lo, 64 * hi)))
-
-    def first_flags(q):
+    if NMK < 32:
+        mms([(s("P3", 256, 448), M("SU"), w_("SQ", 192 * m, 192)) for m in range(4)])
+        tt(AREP, s("P3", 256, 448), AREP, AL.add)
+    for c0 in range(0, 64 * NMK, 512):
+        mask_test(c0, min(512, 64 * NMK - c0), "wd")
+    for j in range(NMK, 32):
+        piece(AW, j, j + 1)
+    for q in range(16):
         o = s("P0", q, 128, 16)
-        mms([(o, s("OW", q, C, 16), sm("SF"))] + ([(o, w_("MB", 128 * q, 128), sm("G8B"))] if q < 10 else
+        mms([(o, s("OW", q, C, 16), sm("SF"))] + ([(o, w_("MB", 128 * q, 128), sm("G8B"))] if 2 * q < NMK else
                                                    [(o, s("GR", 2048 * q + k, 2048 * q + 2048, 16), sm("S8")) for k in range(16)]))
-    mask_keep()
-    mask_fold(8)
     mms([(s("P3", 0, 128), slide(1, r), s("OW", r, C, 16)) for r in range(16)])
-    piece("s", 30, 32)
-    mask_keep()
-    assert bg == [20, 20, 20]
-    piece("v", 20, 22)
     ts(s("LO128"), s("P3", 0, 128), float(C), AL.add)
-    piece("s", 28, 30)
-    mask_test(0, 512, "wd")
-    first_flags(15)
-    first_flags(10)
-    piece("v", 22, 24)
-    piece("s", 26, 28)
-    mask_test(512, 512, "wd")
-    first_flags(14)
-    first_flags(11)
-    mask_test(1024, 256, "wd")
-    piece("s", 25, 26)
-    piece("v", 24, 25)
-    act(s("GV", 0, 1024), ind(AW, s("LO128", 0, 64)))
-    for q in list(range(10)) + [13, 12]:
-        first_flags(q)
-    mm(s("P1", 256, 448), M("BU"), AREP)
-    stale_marks(3)
+    for j in range(4):
+        lin2(w_("GV", 512 * j, 512), ind(AW, w_("LO128", 32 * j, 32)))
+        b, o = s("P4" if j & 1 else "P5"), w_("CW2", 512 * j, 512)
+        mms([(b, M("NBO"), w_("CW", 512 * j, 512)), (b, M("MO"), w_("OW", 512 * j, 512)), (b, M("BDE"), w_("GV", 512 * j, 512))])
+        node({"s": act_(o, b, AF.Relu), "v": ts_(o, b, 0.0, AL.max)}, [o], [b])
+    mms([(s("P7", 256, 384), slide(3, r), w_("CW2", 128 * r, 128)) for r in range(16)])
+    ts(s("FF", 128, 256), s("P7", 256, 384), float(V), AL.add, float(V), AL.min)
+    dma("y", ext(T.yo[:]), s("FF", 128, 256), 65536)
+    for j in range(6):
+        b, o = s("P6" if j & 1 else "P7", 0, 480), w_("X", 480 * j, 480)
+        mms([(b, ID, o), (b, M("STL"), w_("A", 480 * j, 480))])
+        lin2(o, b)
+    mm(s("P3", 256, 448), M("BU"), AREP)
+    for d in range(3):
+        ts(w_("T192", S * d, S), w_("P3", 256 + S * d, S), 1.0 if high[d] else 2.0, AL.is_equal)
+    ts(s("T192", 192, 384), s("P3", 256, 448), 0.0, AL.is_equal, STALE, AL.mult)
+    tt(s("T192", 0, 192), s("T192", 0, 192), s("DX"), AL.mult)
+    tt(s("T192", 0, 192), s("T192", 0, 192), s("XR0"), AL.add)
+    tt(XREP, s("T192", 0, 192), s("T192", 192, 384), AL.max)
+    lin2(s("GM"), s("LS"), 1.0, -1.0)
+    GM = s("P2", 256, 448)
+    mm(GM, ID, s("GM"))
 
-    def fold(t, q, early):
-        o = s("P0", q, 128, 16)
-        mms([(o, ID, s("F", q, 128, 16)), (o, s("OW", q, C, 16), sm("SN%d" % t))] + ([(o, w_("MB", 128 * q, 128), sm("G8B"))] if early else [])
-            + [(o, s("GR", 2048 * q + k, 2048 * q + 2048, 16), sm("SR%d" % t)) for k in range(16)])
+    SBX = (T.SB[:, :, 0:S], [("SB", 0, 1, ALL)], [], 192, B16, "sbuf")
+    SBA = (T.SB[:, :, S:2 * S], [("SB", 1, 2, ALL)], [], 192, B16, "sbuf")
 
-    SBX, SBA = (T.SB[:, :, 0:S], [("SB", 0, 3)], []), (T.SB[:, :, S:2 * S], [("SB", 0, 3)], [])
+    def part(d, lo, hi):
+        return (T.SB[:, d, S * lo:S * hi], [("SB", lo, hi, ALL)], [], S * (hi - lo), B16, "sbuf")
+
+    def strengths(t):
+        u = t & 1
+        CG, LOD = w_("CG", 256 * u, 256), w_("LO", 16 + 16 * u, 16)
+        mmx([(w_("P7", 8 * h, 8), w_("CG", 256 * u + 128 * h, 128), sm("SELW")) for h in range(2)])
+        for j in range(0, 256, WP):
+            lin2(w_("GW", 16 * j, 16 * WP), ind(AW, w_("VARS", 256 * u + j, WP)), e=W3 if t == 3 else "sv")
+
+        def turn(c0, h, n):
+            return [(s("P5", c0 + 128 * h + k, c0 + 128 * h + 128, 16), s("GW", 2048 * h + k, 2048 * h + 2048, 16), sm(n)) for k in range(16)]
+        for h in range(2):
+            mms([(w_("P5", 256 + 128 * h, 128), w_("CG", 256 * u + 128 * h, 128), M("BO"))] + turn(256, h, "SELD"))
+        ts(s("EQ"), s("P5", 256, 512), 0.0, AL.is_equal, 256.0, AL.mult)
+        mms([(s("P5", 0, 256), ID, s("EQ"))] + turn(0, 0, "SELW") + turn(0, 1, "SELW"))
+        scan(s("M1"), s("RSB"), s("P5", 0, 256), 0.0, AL.add, AL.min)
+        tt(s("VT", 16, 272, 16), s("M1", 15, 256, 16), s("P7", 0, 16), AL.min)
+        mms([(s("P7", 256, 512), M("MN"), CG)] + [(w_("P7", 256 + 128 * h, 128), w_("VT", 16 + 128 * h, 128), ID) for h in range(2)])
+        lin2(s("T1"), s("P7", 256, 512))
+        cp(ind(AW, LOD), s("T1"))
+        tt(SBA, AREP, GM, AL.mult)
+
+    def take_w(base, w):
+        mmx([(w_("P7", 16 + S * d, S), M("PI%d" % d), w_("LP", base + w * d, S)) for d in range(3)])
+        tt(AREP, s("P7", 16, 208), SBA, AL.add)
+
     for t in range(4):
+        u = t & 1
+        CH, CHREP = s("CH%d" % u), s("CH%d" % u, H, V)
         ts(s("F"), s("P0", 0, 128), 0.0, AL.is_gt)
         scan(s("IP"), s("RS1"), s("F"), 0.0, AL.mult, AL.add)
         mm(s("P1", 0, 8), M("TRI%d" % t), s("IP", 15, 128, 16))
-        act(s("CR"), ind(s("IP"), s("ELX", 32, 40)))
+        lin2(s("CR"), ind(s("IP"), s("ELX", 32, 40)))
         mms([(s("P2", 0, 128), s("F"), M("PM4%d" % t)), (s("P2", 0, 128), s("IP"), M("PM%d" % t)), (s("P2", 0, 128), s("CR"), M("TRS%d" % t))])
         for gg in range(8):
             ts(w_("CMP", 256 * gg, 256), s("JI"), w_("P1", gg, 1), AL.is_ge)
-        act(s("POS", 0, 128), s("P2", 0, 128), AF.Identity, bias=-4096.0)
-        if t == 0:
-            outputs_checked(0, 0)
-            outputs_checked(1, 0)
-            act(s("GV", 1024, 2048), ind(AW, s("LO128", 64, 128)))
-        for j in range(16):
-            mm(s("P3", j, 32, 16), s("CMP", j, 2048, 16), s("RH", 32 * t + j, 32 * t + 32, 16))
-        if t == 0:
-            replica_x()
-            outputs_checked(2, 0)
-            outputs_checked(0, 1)
+        lin2(s("POS", 0, 128), s("P2", 0, 128), -4096.0)
+        mmx([(s("P3", j, 32, 16), s("CMP", j, 2048, 16), s("RH", 32 * t + j, 32 * t + 32, 16)) for j in range(16)])
         cp(s("LB"), s("P3", 0, 16))
-        act(s("BC"), s("P3", 16, 32), AF.Identity, bias=float(40 * t))
+        lin2(s("BC"), s("P3", 16, 32), float(40 * t))
         tt(s("OH"), ind(s("POS"), s("LB")), s("J1"), AL.is_equal)
         mms([(s("P1", 16, 32), slide(2, r), s("OH", r, 256, 16)) for r in range(16)] + [(s("P1", 16, 32), M("ID16"), s("BC"))])
-        if t == 0:
-            for j, part in ((3, 0), (1, 1), (2, 1), (3, 1)):
-                outputs_checked(j, part)
-            ts(s("GM"), s("LS"), -1.0, AL.mult, 1.0, AL.add)
-        CL, LO, PS = s("CL"), s("LO"), s("P4", 0, 256)
+        CL, LO, LOD, PS = s("CL"), s("LO", 0, 16), w_("LO", 16 + 16 * u, 16), s("P4", 0, 256)
+        CG, c0 = w_("CG", 256 * u, 256), 256 * u
         cp(CL, s("P1", 16, 32))
-        cp(s("VARS"), ind(s("VA"), CL))
-        act(s("CG"), ind(s("CW2"), CL))
-        mms([(s("P3", 32, 48), slide(3, r), s("CG", r, 256, 16)) for r in range(16)])
-        mm(s("P6", 0, 256), M("BO"), s("CG"))
-        mm(PS, M("BNH"), s("CG"), True, False)
-        for h in range(2):
-            mm(w_("P7", 8 * h, 8), w_("CG", 128 * h, 128), SELW)
-
-        def xg(e, j):
-            gat(e, w_("GR", 1024 * j, 1024), ind(XW_, w_("VARS", 64 * j, 64)))
-
-        def xs(j):
-            mms([(w_("P4", 64 * j, 64), M("NID"), s("GR", 1024 * j + k, 1024 * j + 1024, 16)) for k in range(16)], False, False)
-
-        def wg(e, j):
-            gat(e, w_("GR", 4096 + 1024 * j, 1024), ind(AW, w_("VARS", 64 * j, 64)))
-
-        def ws(h):
-            b0 = 4096 + 2048 * h
-            mms([(w_("P5", 128 * h, 128), w_("EQ", 128 * h, 128), M("ID256"))] + [(s("P5", 128 * h + k, 128 * h + 128, 16), s("GR", b0 + k, b0 + 2048, 16), SELW) for k in range(16)])
-        xg("v", 0)
-        xg("s", 2)
+        cp(w_("VARS", c0, 256), ind(s("VA"), CL))
+        lin2(CG, ind(s("CW2"), CL))
+        lin2(s("KR"), ind(s("KK"), CL))
+        mms([(s("P3", 32, 48), slide(3, r), s("CG", c0 + r, c0 + 256, 16)) for r in range(16)])
         tt(s("TF", 0, 16), s("P3", 32, 48), s("BASEW", 48, 64), AL.min)
-        ts(LO, s("TF", 0, 16), 7168.0, AL.add)
-        act(s("ORG"), s("P6", 0, 256), AF.Identity, bias=float(V))
-        xs(0)
-        xs(2)
-        xg("v", 1)
-        xg("s", 3)
-        act(s("KR"), ind(s("KK"), CL))
-        act(s("XO"), ind(XW_, LO))
-        xs(1)
-        xs(3)
-        mms([(PS, ID, s("KR")), (PS, ID, s("XO"))], False)
-        tt(s("EQ"), ind(s("VA"), CL), s("ORG"), AL.is_equal)
-        wg("v", 0)
-        wg("s", 1)
-        ws(0)
-        wg("s", 2)
-        ts(s("MI", 0, 256), PS, 65536.0, AL.add)
-        ts(s("GG"), PS, -11800.0, AL.is_ge)
-        ts(s("MI", 256, 512), s("MI", 0, 256), 255, AL.bitwise_and)
-        ts(s("WT"), PS, -11800.0, AL.is_lt)
-        wg("s", 3)
-        ws(1)
-        act(s("AO"), ind(AW, LO), scale=ic(0))
-        tt(s("NEQ"), s("MI", 256, 512), s("XO"), AL.not_equal)
-        tt(s("NXG"), s("MI", 256, 512), s("GG"), AL.mult)
-        tt(s("XW"), s("XO"), s("WT"), AL.mult)
-        tt(ind(XW_, LO), s("NXG"), s("XW"), AL.add)
-        PB = s("P2", 0, 256)
-        mms([(PB, M("SCL%d" % t), s("ONES")), (PB, M("SCH%d" % t), s("NEQ")), (PB, M("NID"), s("AO"))], True, False)
-        tt(SBX, XREP, s("GM"), AL.mult)
-        scan(s("M1"), s("RSB"), s("P5", 0, 256), 0.0, AL.add, AL.min)
-        for h in range(2):
-            tt(s("VT", 128 * h, 128 * h + 128, 16), s("M1", 128 * h + 15, 128 * h + 128, 16), w_("P7", 8 * h, 8), AL.min)
-        mms([(w_("P2", 128 * h, 128), w_("VT", 128 * h, 128), ID) for h in range(2)], False)
-        tt(s("T1"), PB, s("GG"), AL.mult)
-        tt(ind(AW, LO), s("T1"), s("AO"), AL.add)
-        tt(SBA, AREP, s("GM"), AL.mult)
-        send(5 + t, [(T.SB[:, d, :], [("SB", 0, 3)], []) for d in range(3)], "LP%d" % t, 0, 128)
-        piece("s", 0, 2)
-        piece("s", 2, 3)
-        cp(ind(s("OW"), CL), s("T1"))
-        piece("v", 3, 5)
-        for d in range(3):
-            mm(w_("P6", S * d, S), M("PI%d" % d), w_("LP%d" % t, 128 * d + S, S))
-        for d in range(3):
-            mm(w_("P5", S * d, S), M("PI%d" % d), w_("LP%d" % t, 128 * d, S))
-        tt(AREP, s("P6", 0, 192), SBA, AL.add)
-        piece("s", 5, 6)
-        changed_digits([(s("P7", 0, 192), M("BCH%d" % t), AREP)], "wd")
-        tt(XREP, s("P5", 0, 192), SBX, AL.add)
-        mask_test(0, 384, "wd")
-        if t == 3:
-            ts(s("YB"), s("X", 0, V), 256.0, AL.min)
-            dma("y", ext(T.y[:]), s("YB"))
-            dma("g", ext(T.yw[:]), s("A", 0, V, p=row(0)))
-        if t == 0:
-            mms([(s("P7", 256, 384), slide(3, r), w_("CW2", 128 * r, 128)) for r in range(16)])
-            ts(s("FF"), s("P7", 256, 384), 7168.0, AL.add, float(V), AL.min)
-            dma("y", ext(T.yo[:]), s("FF"))
+        ts(LO, s("TF", 0, 16), float(V), AL.add)
+        lin2(s("XO"), ind(XW_, LO), scale=1.0 / 256)
+        for j, n in zip(XP[:-1], XP[1:]):
+            lin2(s("GR", 16 * j, 16 * n), ind(XW_, s("VARS", c0 + j, c0 + n)))
+        for j in range(4):
+            mms([(w_("P4", 64 * j, 64), M("NID"), s("GR", 1024 * j + k, 1024 * j + 1024, 16)) for k in range(16)], j == 0, j == 3)
+            if j == 2:
+                mms([(s("P4", lo, hi), l, s(b, o + lo, o + hi)) for lo, hi in ((0, 192), (192, 256))
+                     for l, b, o in ((M("BNH"), "CG", c0), (M("IDS"), "KR", 0), (ID, "XO", 0))], False, False)
+        ts(s("FL"), PS, -0.498, AL.add)
+        tt(s("NX"), PS, s("FL"), AL.subtract)
+        GG, GS = s("GG"), s("GS")
+        node({"s": act_(GG, PS, AF.Relu, 640.0), "v": ts_(GG, PS, -640.0, AL.is_ge)}, [GG], [PS])
+        act(GS, PS, AF.Sign, 640.0)
+        mm(s("P2", 0, 256), ID, s("XO"))
+        tt(s("NEQ"), s("P2", 0, 256), s("NX"), AL.not_equal)
+        tt(ind(CH, LO), s("NEQ"), GG, AL.mult)
+        send([w_("CH%d" % u, H + S * d, S) for d in range(3)], "LC", 192 * t, S)
+        DOWN = ("OW", "CW")[u]
+        cp(ind(s(DOWN), CL), GS)
+        mms([(s("P3", 48, 64), slide(3, r), s("CG", c0 + r, c0 + 256, 16)) for r in range(16)] + [(s("P3", 48, 64), slide(4, r), s("GS", r, 256, 16)) for r in range(16)])
+        tt(s("TF", 48, 64), s("P3", 48, 64), s("BASEW", 64, 80), AL.min)
+        if t:
+            strengths(t - 1)
+        ts(LOD, s("TF", 48, 64), float(V + 4096), AL.add)
+        tt(ind(XW_, LOD), s("NX"), s("C256"), AL.mult)
+        tt(SBX, XREP, GM, AL.mult)
+        if t:
+            send([part(d, 0, 2) for d in range(3)], "LP", 384 * t, 128, XW_X)
+        else:
+            send([part(d, 0, 1) for d in range(3)], "LP", 0, S, XW_X)
+        nodes[sends[-1]]["push"] = PUSHX
+        left = lambda j: (32 - j) * 0.5 * 1024 * GATHER * CY
+        for j in range(2 * EARLY):
+            piece(CH, j, j + 1)
+        mmx([(w_("P6", S * d, S), M("PI%d" % d), w_("LC", 192 * t + S * d, S)) for d in range(3)])
+        tt(CHREP, s("P6", 0, 192), CHREP, AL.add)
+        if EARLY:
+            changed_digits([(s("P6", 0, 192), M("BD22"), CHREP)], "wd")
+            mask_test(0, 128 * EARLY, "wd")
+        for j in range(2 * EARLY, 28, 2):
+            piece(CH, j, j + 2)
+        for j in range(28, 32):
+            piece(CH, j, j + 1)
+        for n, q in enumerate(list(range(EARLY, 8)) + list(range(EARLY)) + list(range(8, 16))):
+            o = s("P0", q, 128, 16)
+            mms([(o, ID, s("F", q, 128, 16)), (o, s(DOWN, q, C, 16), sm("SN"))] + ([(o, w_("MB", 128 * q, 128), sm("G8B"))] if q < EARLY else [])
+                + [(o, s("GR", 2048 * q + k, 2048 * q + 2048, 16), sm("G8B")) for k in range(16)], extra=FX * left(2 * n + 2))
+        wx = 128 if t else S
+        mmx([(w_("P6", S * d, S), M("PI%d" % d), w_("LP", 384 * t + wx * d, S)) for d in range(3)])
+        tt(XREP, s("P6", 0, 192), SBX, AL.add)
+        if t:
+            take_w(384 * t + S, 128)
         if t < 2:
-            plan_consts(4 + t)
-        piece("s", 30, 32)
-        for q in range(3):
-            fold(t, q, True)
-        fold(t, 15, False)
-        for j in range(6):
-            piece("v", 6 + 2 * j, 8 + 2 * j)
-            fold(t, 3 + j, False)
-            if j < 5:
-                piece("s", 28 - 2 * j, 30 - 2 * j)
-                fold(t, 14 - j, False)
-        piece("s", 19, 20)
-        piece("s" if t == 3 else "v", 18, 19)
-        fold(t, 9, False)
-    ts(s("FF"), s("P0", 0, 128), 0.0, AL.is_gt)
-    for gg in range(8):
-        dma("ys"[gg & 1], ext(T.yf[gg:gg + 1, :]), w_("FF", 16 * gg, 16))
-    for sem, val in cnt.items():
-        wait("g", sem, val)
+            fill("CH%d" % u, 0, VW)
+            fill(DOWN, 0, C)
+    strengths(3)
+    send([part(d, 1, 2) for d in range(3)], "LP", 384 * 4, S)
+    nodes[sends[-1]]["push"] = PUSH
+    take_w(384 * 4, S)
+    for r0 in range(0, 15, 5):
+        mms([(s("P5", 0, 192), slide(5, r), w_("A", 192 * r, 192)) for r in range(r0, r0 + 5)], r0 == 0, False)
+    mm(s("P5", 0, 192), slide(5, 15), AREP, False, True)
+    lin2(s("YW"), s("P5", 0, 192))
+    nodes[dma("y", ext(T.yw[:]), s("YW"), 98304)]["push"] = PUSHY
+    ts(s("YB"), s("X", 0, V), 256.0, AL.min)
+    nodes[dma("y", ext(T.y[:]), s("YB"), 786432)]["push"] = PUSHY
+    ts(s("F"), s("P0", 0, 128), 0.0, AL.is_gt)
+    mm(s("P1", 0, 128), s("F"), M("PERM"))
+    o, i = s("POS", 0, 128), s("P1", 0, 128)
+    node({"v": (cost(o, [i]), lambda: g.vector.transpose(o[0], i[0]))}, [o], [i])
+    lin2(s("FF", 0, 128), ind(s("POS", 0, 128), s("ELX", 40, 48)))
+    for h in range(2):
+        dma("ys"[h], ext(T.yf[h:8:2, :]), w_("FF", 64 * h, 64), 32768)
+    issue()

@@ -8,24 +8,31 @@ STALE = 65536.0
 BIG = 3.0e7
 ALL = (1 << 128) - 1
 B16, F32, I32, U16 = "bfloat16", "float32", "int32", "uint16"
-NMK = 24
+NP = 4
+NP0 = 3
+PN, EW = 128 * NP, 48 * 48
+SINGLE = [q for q in range(16) if q % 8 >= NP]
+NS = len(SINGLE)
+LN2 = 0.6931471805599453
+EPS = 2.0 ** -10
 MP = 32
 EARLY = 2
 _sb = {
     "VA": (CWD, I32), "VAP": (C, U16), "A": (VW, B16), "X": (VW, B16), "KK": (CWD, B16), "CW": (CWD, B16), "CW2": (CWD, B16), "OW": (CWD, B16),
-    "CH0": (VW, B16), "CH1": (VW, B16), "GR": (32768, B16), "GW": (4096, B16), "CODE": (V, B16), "MK": (C, F32), "MB": (C, B16), "MT": (1024, I32), "EQ": (256, B16),
+    "CH0": (VW, B16), "CH1": (VW, B16), "GR": (32768, B16), "GW": (4096, B16), "CODE": (V, B16), "MK": (C, F32), "MB": (128 * NS, B16), "MT": (1024, I32), "EQ": (256, B16),
     "IO": (256, F32), "ZERO": (256, B16), "GI": (128, F32), "JI": (256, B16), "J1": (256, F32), "II": (128, I32), "CF": (160, F32), "IC": (16, F32),
-    "JW": (128, F32), "TMP": (256, F32), "TMP2": (256, F32), "MAT": (48 * 128, B16), "PIT": (160, B16), "SM": (256, B16), "ZW": (6 * 160, B16), "IDF": (128, F32), "G8": (8, F32),
+    "JW": (128, F32), "TMP": (256, F32), "TMP2": (256, F32), "MAT": (50 * 128, B16), "PIT": (160, B16), "SM": (128, B16), "ZW": (6 * 160, B16), "IDF": (128, F32), "G8": (8, F32),
     "MASKR": (512, F32), "RSB": (256, F32), "RS1": (128, B16), "ELX": (48, U16), "BASEW": (80, F32), "JT": (32, F32),
     "OVI": (128, I32), "OV2": (384, I32), "OVL": (128, U16), "OVB": (256, B16), "WI": (192, I32), "WB": (192, B16), "SI": (128, I32), "SBF": (128, B16), "NLI": (16, I32),
     "LN": (32 * 5, U16), "VARS": (512, U16), "SR": (256, B16), "M1": (256, F32), "YY": (256, F32), "M2": (256, F32),
-    "TI": (64, I32), "OI": (16, I32), "TF": (256, F32), "SCT": (32, F32), "ACT": (16, F32), "NM": (32, F32), "DO": (16, F32), "EXP": (512, F32), "DOX": (256, F32),
+    "TI": (64, I32), "OI": (16, I32), "TF": (256, F32), "SCT": (32, F32), "ACT": (16, F32), "NM": (32, F32), "DO": (16, F32), "EXP": (512, F32),
     "L1": (16, U16), "L2": (64, U16), "BE": (256, B16), "BO": (256, B16), "GO": (256, B16), "WL": (32, B16), "VT": (272, B16), "VAL": (1024, B16), "YW": (192, F32),
     "ONES": (256, B16), "LA": (192 * 5, B16), "LS": (192, B16), "TT": (192 * 4, B16), "SQ": (192 * 4, B16), "XR0": (192, B16), "DX": (192, B16), "NE": (192, B16), "GM": (192, B16),
-    "T192": (384, F32), "LO128": (128, U16), "LC": (192 * 4, B16), "LP": (384 * 5, B16),
+    "T192": (384, F32), "LO128": (128, U16), "LC": (320 * 4, B16), "LP": (384 * 5, B16),
     "F": (128, B16), "FF": (256, F32), "IP": (128, B16), "CR": (128, B16), "CMP": (2048, B16), "POS": (144, F32), "LB": (16, U16), "BC": (16, B16), "OH": (256, B16), "CL": (16, U16),
     "CG": (512, B16), "KR": (256, B16), "XO": (256, B16), "LO": (48, U16), "FL": (256, I32), "GG": (256, B16), "NX": (256, B16),
     "NEQ": (256, B16), "T1": (256, B16), "RH": (128, B16), "C256": (256, B16), "GS": (256, B16),
+    "OHT": (EW, B16), "PIX": (PN, U16), "BIN": (256, B16), "FT": (4 * 112, B16), "WT": (128, B16), "RR": (1024, B16), "CUM": (544, B16), "MIX": (PN, U16),
 }
 SCRATCH = {k: ("sbuf", [128, w], d) for k, (w, d) in _sb.items()}
 SCRATCH["SB"] = ("sbuf", [128, 3, 128], B16)
@@ -33,8 +40,9 @@ for _i in range(8):
     SCRATCH["P%d" % _i] = ("psum", [128, 512], F32)
 SEMAPHORES = ["cv", "cs", "cp", "cg"] + ["d%d" % i for i in range(56)] + ["ar%d" % i for i in range(14)] + ["ls%d" % i for i in range(14)]
 ALIAS = {"TH": ("GR", 4096, 3072), "DEW": ("GR", 8192, DV0 + C), "DVAL": ("GR", 13568, C), "GV": ("GR", C, C), "YB": ("CH0", 0, V),
-         "BITS": ("CH1", 0, DV0)}
-CY, PECY, GATHER, SCATTER, FIX, WAKE = 0.00088, 0.00044, 1.55, 3.6, 0.05, 0.1
+         "BITS": ("CH1", 0, DV0), "MASK": ("GR", 32768 - 16 * PN, 16 * PN), "TBM": ("GR", 8192, 4096), "E": ("CODE", 0, EW),
+         "PR": ("GW", 0, 2 * PN), "VAF": ("MK", 128 * NS, 2 * PN)}
+CY, PECY, GATHER, SCATTER, FIX, WAKE = 0.00088, 0.00044, 1.2, 3.0, 0.05, 0.1
 VPEN = (0.2, 0.3, 0.4, 0.5)
 RATES = ((1.55, 3.6), (1.15, 5.0), (2.0, 2.5), (2.0, 5.5), (1.15, 2.0))
 XW_X = 42.0
@@ -46,17 +54,30 @@ DMA0, DMABW, ROWS = 1.5, 250e3, 0.4
 REMOTE = 3.2
 FIRST = 3.5
 MARGIN = 3.0
-GSLACK = 1.6
+GSLACK = 1.3
 PUSHY = 5.0
 DEAR = 1.5
 W3 = "sv"
-PUSH = 10.0
+PUSH = 3.0
 PUSHX = 10.0
 CWDMA = 1
 XP = (0, 32, 64, 96, 128, 160, 192, 224, 256)
 SHAKE = 0.0
 PLAN = []
+POLISH = ((1.55, 3.6, 1.0, 1.0), (1.1, 2.5, 1.4, 1.5), (1.15, 5.0, 1.3, 0.8), (1.25, 3.0, 0.9, 1.8))
+START = 0
+TRIES, HEAT = 24000, 0.001
 VAW = 1024
+EB = ("P3", "P4", "P1", "P3", "P4")
+EQ = ("sv",) * 5
+ZB = ("P1", "P3", "P4")
+GAPS = ("dmdd", "xddd", "dxdm", "")
+SCANS = 1
+PUSHE = 0.0
+PUSHT, PUSHM, PUSHP = 10.0, 0.0, 0.0
+SCALLS = ("bb", "bb", "b", "b", "b", "b", "bb", "bb")
+PCALLS = ((1, 1, 1, 2), (1, 2, 2, 2))
+SUMS = "s2s0s1s3p0s4p1s5p2s6p3s7"
 
 
 def rank_program(g, core, T, topo):
@@ -95,6 +116,9 @@ def rank_program(g, core, T, topo):
         kind = 2 if any(o[5] == "ind" for o in outs) else 1 if any(isinstance(o, tuple) and o[5] == "ind" for o in ins) else 0
         nodes.append({"alt": alt, "pred": pred, "sem": sem, "inc": inc, "lat": lat, "extra": extra, "kind": kind})
         return me
+
+    def writers(*xs):
+        return [k for x in xs for (b, lo, hi, tg) in x[1] for (l2, h2, t2, w2, k) in rec.get(b, ()) if w2 and l2 < hi and lo < h2]
 
     def s(name, lo=0, hi=None, step=1, p=None):
         if name in ALIAS:
@@ -205,7 +229,7 @@ def rank_program(g, core, T, topo):
     def ext(ap):
         return (ap, [], [], 1, None, "hbm")
 
-    sends = []
+    sends, lands = [], []
     en = [e for e in topo.engines(core, T.cores[rank ^ 1]) if all(e in topo.engines(core, T.cores[rank ^ d]) for d in (2, 3))]
     pool = {True: en[0::2], False: en[1::2]}
     lanes = []
@@ -215,7 +239,7 @@ def rank_program(g, core, T, topo):
         lanes.append(pool[side][:len(en) // 4])
         pool[side] = pool[side][len(en) // 4:]
 
-    def send(srcs, land, base, w, extra=0.0):
+    def send(srcs, land, base, w, extra=0.0, gap=0):
         m = len(sends)
         trs, tot = [], 0
         for d in (1, 2, 3):
@@ -225,14 +249,14 @@ def rank_program(g, core, T, topo):
             mask = sum(1 << e for e in lanes[d - 1])
             tot += k
             trs.append(RemoteDMATransfer(dst_ids=[DstId(rid=rid, pnc=pid)], dma_engine_mask=mask, remote_sem=T.sem["ar%d" % m],
-                                         src=srcs[d - 1][0], dst=T[land][:, base + (d - 1) * w:base + d * w]))
+                                         src=srcs[d - 1][0], dst=w_(land, base + (d - 1) * (w + gap), w)[0]))
 
         def go():
             g.remote_dma_fused(trs, local_sem=T.sem["ls%d" % m])
         k = node({"g": (0.6 + (0 if m else FIRST), go)}, [], srcs, sem="ls%d" % m, inc=tot, lat=REMOTE + (MARGIN if extra and m < 12 else 0) + (0 if m else FIRST), after=sends[-1:], extra=extra)
         nodes[k]["order"] = set(sends[-1:])
         sends.append(k)
-        return node({"-": (0.0, None)}, [s(land, base, base + 3 * w)], [], sem="ar%d" % m, inc=tot, lat=0.01, after=[k])
+        return node({"-": (0.0, None)}, [w_(land, base + d * (w + gap), w) for d in range(3)], [], sem="ar%d" % m, inc=tot, lat=0.01, after=[k])
 
     def issue():
         n = len(nodes)
@@ -276,8 +300,162 @@ def rank_program(g, core, T, topo):
                 t0[k] = max([t0[j] + delay(j, c[j], k) for j in nodes[k]["pred"]] + [free.get(q, 0.0)])
                 free[q] = t0[k] + c[k]
             return max(t0[k] + (nodes[k]["lat"] or c[k]) for k in range(n))
-        top = None
-        for spare in VPEN:
+
+        def polish(at):
+            edge = [[(j, None if j in y.get("order", ()) or not nodes[j]["lat"] else nodes[j]["lat"],
+                      delay(j, 0.0, k) - (0.0 if j in y.get("order", ()) else nodes[j]["lat"] or 0.0)) for j in y["pred"]] for k, y in enumerate(nodes)]
+            order = sorted(range(n), key=lambda k: (at[k][1], k))
+            que = [x[0] for x in at]
+            rates = [(0, ga / GATHER, sc / SCATTER) for ga, sc, slow, wake in POLISH]
+            tail = [k for k in range(n) if not succ[k]]
+
+            def times(k):
+                c = nodes[k]["alt"][que[k]][0]
+                return [FIX + (c - FIX) * r[nodes[k]["kind"]] if nodes[k]["kind"] else c for r in rates]
+            cs = [list(z) for z in zip(*[times(k) for k in range(n)])]
+
+            def run(c, old, p0):
+                t0, free = old[:], {}
+                for p in range(p0 - 1, -1, -1):
+                    k = order[p]
+                    if que[k] not in free:
+                        free[que[k]] = t0[k] + c[k]
+                        if len(free) == 6:
+                            break
+                for k in order[p0:]:
+                    q = que[k]
+                    t = free.get(q, 0.0) if q != "-" else 0.0
+                    for j, lat, w in c[n][k]:
+                        e = t0[j] + (lat or c[j]) + w
+                        if e > t:
+                            t = e
+                    t0[k] = t
+                    free[q] = t + c[k]
+                return t0, max(t0[k] + (nodes[k]["lat"] or c[k]) for k in tail)
+
+            for c, (ga, sc, slow, wake) in zip(cs, POLISH):
+                c.append([[(j, lat and lat * slow, w * wake) for j, lat, w in e] for e in edge])
+                c.append([[] for _ in range(n)])
+                for k in range(n):
+                    for j, lat, w in c[n][k]:
+                        c[n + 1][j].append((k, lat, w))
+
+            def tails(c):
+                y, nxt = [0.0] * n, {}
+                for k in reversed(order):
+                    q = que[k]
+                    t = c[k] + nxt.get(q, 0.0) if q != "-" else 0.0
+                    for j, lat, w in c[n + 1][k]:
+                        e = (lat or c[k]) + w + y[j]
+                        if e > t:
+                            t = e
+                    y[k] = nxt[q] = max(t, nodes[k]["lat"] or c[k])
+                return y
+
+            def least(c, old, y, p0, p1):
+                t0, free, top_ = {}, {}, 0.0
+                part = order[p0:p1 + 1]
+                need = {que[k] for k in part}
+                for p in range(p0 - 1, -1, -1):
+                    k = order[p]
+                    if que[k] in need and que[k] not in free:
+                        free[que[k]] = old[k] + c[k]
+                        if len(free) == len(need):
+                            break
+                for k in part:
+                    q = que[k]
+                    t = free.get(q, 0.0) if q != "-" else 0.0
+                    for j, lat, w in c[n][k]:
+                        e = t0.get(j, old[j]) + (lat or c[j]) + w
+                        if e > t:
+                            t = e
+                    t0[k] = t
+                    free[q] = t + c[k]
+                for k in part:
+                    for j, lat, w in c[n + 1][k]:
+                        if j not in t0:
+                            e = t0[k] + (lat or c[k]) + w + y[j]
+                            if e > top_:
+                                top_ = e
+                need.discard("-")
+                for p in range(p1 + 1, n):
+                    if not need:
+                        break
+                    k = order[p]
+                    if que[k] in need:
+                        need.discard(que[k])
+                        top_ = max(top_, free[que[k]] + y[k])
+                return top_
+
+            def waits(c, t0):
+                before, last, out = [None] * n, {}, []
+                for k in order:
+                    before[k], last[que[k]] = last.get(que[k]), k
+                k = max(tail, key=lambda k: t0[k] + (nodes[k]["lat"] or c[k]))
+                while t0[k] > 0.0:
+                    on = [j for j, lat, w in c[n][k] if t0[j] + (lat or c[j]) + w >= t0[k] - 1e-9]
+                    if not on:
+                        out.append((before[k], k))
+                    k = on[0] if on else before[k]
+                return out
+            now = [run(c, [0.0] * n, 0) for c in cs]
+            norm = [1.0 / x[1] for x in now]
+            score, seed, cand = float(len(rates)), 1, None
+            best = (score, order[:], que[:], now[0][0])
+            for it in range(TRIES):
+                if cand is None:
+                    cand = [e for c, x in zip(cs, now) for e in waits(c, x[0])]
+                    rest = [tails(c) for c in cs]
+                seed = (seed * 1103515245 + 12345) % 2147483648
+                j, k = cand[(seed >> 8) % len(cand)]
+                move, pj, pk = (seed >> 4) % 4, order.index(j), order.index(k)
+                for hop in range((seed >> 20) % 4 if move < 2 else 0):
+                    step = 1 if move else -1
+                    p = (pk if move else pj) + step
+                    while 0 <= p < n and que[order[p]] != que[k]:
+                        p += step
+                    if 0 <= p < n:
+                        pj, pk = (pj, p) if move else (p, pk)
+                        j, k = order[pj], order[pk]
+                keep, moved = order[pj:pk + 1], None
+                if move < 2:
+                    grp = {k if move == 0 else j}
+                    for z in (reversed(keep) if move == 0 else keep):
+                        if z in grp:
+                            grp.update(nodes[z]["pred"] if move == 0 else succ[z])
+                    if (j if move == 0 else k) in grp:
+                        continue
+                    a0, a1 = [z for z in keep if z in grp], [z for z in keep if z not in grp]
+                    order[pj:pk + 1] = a0 + a1 if move == 0 else a1 + a0
+                else:
+                    moved = (j, k)[move - 2]
+                    other = [q for q in nodes[moved]["alt"] if q != que[moved]]
+                    if not other:
+                        continue
+                    was, que[moved] = que[moved], other[0]
+                    for c, x in zip(cs, times(moved)):
+                        c[moved] = x
+                bar = score + HEAT * (1.0 - it / TRIES) * ((seed >> 12) % 16) / 16
+                got = sum(least(c, x[0], y, pj, pk) * w for c, x, y, w in zip(cs, now, rest, norm))
+                if got <= bar:
+                    new = [run(c, x[0], pj) for c, x in zip(cs, now)]
+                    got = sum(x[1] * w for x, w in zip(new, norm))
+                if got <= bar:
+                    score, now, cand = got, new, None
+                    if got < best[0]:
+                        best = (got, order[:], que[:], now[0][0])
+                else:
+                    order[pj:pk + 1] = keep
+                    if moved is not None:
+                        que[moved] = was
+                        for c, x in zip(cs, times(moved)):
+                            c[moved] = x
+            out = [None] * n
+            for p, k in enumerate(best[1]):
+                out[k] = (best[2][k], best[3][k], nodes[k]["alt"][best[2][k]][0], p)
+            return out
+        top = []
+        for spare in (() if PLAN else VPEN):
             far = [0.0] * n
             for k in range(n - 1, -1, -1):
                 x = nodes[k]
@@ -287,8 +465,7 @@ def rank_program(g, core, T, topo):
             for rnd in range(ROUNDS):
                 at = place(far, False, spare)
                 score = sum(length(at, (0, ga / GATHER, sc / SCATTER)) / (1 + ga) for ga, sc in RATES)
-                if top is None or score < top[0]:
-                    top = (score, at)
+                top.append((score, len(top), at))
                 end = [0.0] * n
                 for k, x in enumerate(nodes):
                     end[k] = max([at[k][1] + (x["lat"] or at[k][2])] + [end[j] + 1e-6 for j in x["pred"]])
@@ -297,9 +474,10 @@ def rank_program(g, core, T, topo):
                 for k in range(n - 1, -1, -1):
                     for j in nodes[k]["pred"]:
                         far[j] = max(far[j], far[k] + delay(j, at[j][2], k))
-        PLAN.append(top[0])
-        for x, (q, t0, c) in zip(nodes, top[1]):
-            x["q"], x["t"] = q, t0
+        if not PLAN:
+            PLAN.append(polish(sorted(top)[START][2]))
+        for x, at in zip(nodes, PLAN[0]):
+            x["q"], x["t"] = at[0], max([at[3]] + [nodes[j]["t"] for j in x["pred"]])
         cnt, waited, tiles = {}, {}, {}
 
         def wait(q, sem, val):
@@ -418,9 +596,12 @@ def rank_program(g, core, T, topo):
     ts(s("II", 1, 2), s("II", 0, 1), 15, AL.bitwise_and)
     ts(s("II", 2, 3), s("II", 0, 1), 112, AL.bitwise_and)
     ts(s("II", 3, 4), s("II", 0, 1), 16, AL.bitwise_and)
-    for n in ("p", "i", "g16", "odd"):
+    ts(s("II", 4, 5), s("II", 0, 1), 1, AL.bitwise_and)
+    ts(s("II", 5, 6), s("II", 0, 1), 14, AL.bitwise_and)
+    for n in ("p", "i", "g16", "odd", "par", "r2"):
         col(n)
     cp(s("CF", 0, 4), s("II", 0, 4))
+    cp(s("CF", 4, 6), s("II", 4, 6))
     ms(s("VA", C, CWD), NV)
     ts(s("IC"), s("IO", 0, 16), col("i"), AL.is_equal)
     ts(s("BITS", 0, 1), col("i"), 12.0, AL.is_lt)
@@ -469,8 +650,8 @@ def rank_program(g, core, T, topo):
     cp(s("OVL"), s("OV2", 0, 128))
     VARS0 = s("VARS", 0, 256)
     cp(VARS0, ind(s("VA"), s("LN", 0, 16)))
-    for j in range(4):
-        cp(ind(s("DEW"), w_("OVL", 32 * j, 32)), w_("DVAL", 512 * j, 512))
+    for j in range(8):
+        cp(ind(s("DEW"), w_("OVL", 16 * j, 16)), w_("DVAL", 256 * j, 256))
     send([w_("X", H + S * d, S) for d in range(3)], "LA", 0, S)
     iota(s("JT", 0, 16), [[128, 2], [0, 8]], 0, 1)
     iota(s("JT", 16, 32), [[128, 2], [0, 8]], DV0, 1)
@@ -514,8 +695,9 @@ def rank_program(g, core, T, topo):
     ms(s("BASEW", 16, 32), float(C))
     for d in range(3):
         lin2(M("PD%d" % d), M("PI%d" % d), scale=col("r07"))
-        ts(M("PK%d" % d), s("GI"), col("pg%d" % d), AL.is_equal, col("kh" if high[d] else "kl"), AL.mult)
-    fill("OW", 0, CWD)
+        k = ts(M("PK%d" % d), s("GI"), col("pg%d" % d), AL.is_equal, col("kh" if high[d] else "kl"), AL.mult)
+        nodes[k]["pred"].update(writers(col("kh"), col("kl")))
+    dma("y", s("OW"), s("CODE", 0, CWD), 256 * CWD)
     ts(s("OV2", 128, 256), s("OVI"), 8, AL.arith_shift_right)
     ts(s("OV2", 256, 384), s("OVI"), 255, AL.bitwise_and)
     ts(s("OVB", 0, 128), s("OV2", 128, 256), -8.0, AL.add)
@@ -531,7 +713,6 @@ def rank_program(g, core, T, topo):
     fill("KK", C, CWD)
     lin("t8", [(8, 4096)])
     lin2(s("CW2", C, CWD), s("ONES"), scale=col("t8"))
-    fill("CH0", 0, VW)
     terms(s("ZW", 160, 320), [(4, 15, 256), (5, 15, 1)])
     terms(M("BU22"), [(7, None, -2 ** 22)])
     terms(M("BU"), [(7, None, 1)])
@@ -543,7 +724,7 @@ def rank_program(g, core, T, topo):
     terms(sm("SELD"), [(4, None, 256), (5, None, 1), (6, None, -1024)])
     terms(sm("SN"), [(13, None, -1)])
     terms(sm("SF"), [(6, None, 1)])
-    if NMK < 32:
+    if NP0 < NP:
         terms(sm("S8"), [(8, None, 1)])
         terms(M("SU"), [(7, 8, 1)])
     terms(M("MO"), [(4, 4, -1), (5, 5, 1)])
@@ -592,20 +773,87 @@ def rank_program(g, core, T, topo):
         tt(s("DX"), s("P7", 0, 192), XREP, AL.subtract)
         lin2(s("XR0"), XREP)
         mm(s("P7", 0, 192), M("K1"), AREP)
-        mms([(s("P7", 256, 448), M("K3"), AREP)] + [(w_("P7", 256 + S * d, S), M("B7"), w_("NE", S * d, S)) for d in range(3) if high[d]])
+        mms([(s("P7", 256, 448), M("K3"), AREP)] + [(w_("P7", 256 + S * d, S), M("B7"), w_("NE", S * d, S)) for d in range(3) if high[d]],
+            after=writers(M("B7"), s("NE")))
         ts(s("LS"), s("P7", 256, 448), 0.0, AL.is_gt)
         tt(s("LS"), s("P7", 0, 192), s("LS"), AL.mult)
         tt(AREP, AREP, s("LS"), AL.add)
 
     def replica_digits():
-        for h in range(NMK):
-            b0 = 16384 + 1024 * (h % 16)
+        i = len(done["d"])
+        q = SINGLE[i]
+        for h in (2 * i, 2 * i + 1):
+            b0 = 16384 + 1024 * (h % NS)
             for x in range(0, 64, MP):
-                lin2(w_("GR", b0 + 16 * x, 16 * MP), ind(s("CODE"), w_("VAP", 64 * h + x, MP)))
-            mms([(w_("P7", 64 * (h % 8), 64), ID, s("GR", b0 + k, b0 + 1024, 16)) for k in range(16)])
-            if h % 4 == 3 or h == NMK - 1:
-                h0 = h - h % 4
-                lin2(s("MK", 64 * h0, 64 * h + 64), s("P7", 64 * (h0 % 8), 64 * (h % 8) + 64))
+                lin2(w_("GR", b0 + 16 * x, 16 * MP), ind(s("CODE"), w_("VAP", 128 * q + 64 * (h & 1) + x, MP)))
+            mms([(w_("P7", 384 + 64 * (h & 1), 64), ID, s("GR", b0 + k, b0 + 1024, 16)) for k in range(16)])
+        lin2(w_("MK", 128 * i, 128), s("P7", 384, 512))
+
+    def pair_list():
+        nh = PN // 2
+        o, c0 = s("P7", 0, nh), nh * len(done["x"])
+        mms([(o, s("IDF"), w_("VAF", c0, nh))], True, False)
+        mms([(o, s("IDF"), w_("VAF", PN + c0, nh))], False, False)
+        mms([(o, M("N2304"), w_("PR", c0, nh)), (o, M("N48"), w_("PR", PN + c0, nh))], False)
+        ts(w_("PIX", c0, nh), o, 129.0 * 2352, AL.add)
+
+    def pair_mask():
+        nh = PN // 2
+        o, c0 = s("P7", 0, nh), nh * len(done["m"])
+        mms([(o, M("I64"), w_("PR", c0, nh)), (o, ID, w_("PR", PN + c0, nh))])
+        ts(w_("MIX", c0, nh), o, -129.0 * 65, AL.add)
+        for x in range(c0, c0 + nh, MP):
+            nodes[lin2(w_("MASK", 16 * x, 16 * MP), ind(s("TBM"), w_("MIX", x, MP)))]["push"] = PUSHM
+
+    done = {"d": [], "x": [], "m": []}
+
+    def gap_work(plan):
+        for c in plan:
+            {"d": replica_digits, "x": pair_list, "m": pair_mask}[c]()
+            done[c].append(c)
+
+    def pair_tables():
+        for j in range(2):
+            vp = w_("VAP", 1024 * j, PN)
+            ts(w_("PR", PN * j, PN), vp, 1.0 / 48, AL.mult, 128.5 + 1.0 / 96, AL.add)
+            ts(w_("VAF", PN * j, PN), vp, 1.0 if j else 48.0, AL.mult)
+        lin2(M("I64"), ID, scale=64.0)
+        lin2(col("npar"), col("par"), 1.0, -1.0)
+        lin2(col("c2"), col("par"), 1.0)
+        B = lambda j: w_("BIN", 64 * j, 64)
+        iota(B(0), [[0, 8], [1, 8]], 0, 0)
+        iota(B(1), [[2, 8], [0, 8]], 0, 0)
+        ts(B(2), B(0), 0.0, AL.is_equal, 2.0 ** -8, AL.mult)
+        ts(B(3), B(0), 0.0, AL.is_gt, col("c2"), AL.mult)
+        scan(B(0), B(3), B(2), 0.0, AL.mult, AL.add)
+        ts(B(1), B(1), col("r2"), AL.is_equal, col("npar"), AL.max)
+        tt(s("TBM", 0, 64), B(0), B(1), AL.mult)
+        for j, w in enumerate((1.0, 3.0, 15.0)):
+            lin2(col("e%d" % j), col("npar"), 1.0, w)
+            lin2(s("TBM", 64 << j, 128 << j), s("TBM", 0, 64 << j), scale=col("e%d" % j))
+        ts(s("TF", 144, 152), s("IO", 0, 16, 2), col("r2"), AL.is_equal, col("par"), AL.max)
+        for j in range(7, -1, -1):
+            lin2(w_("TBM", 512 * j, 512), s("TBM", 0, 512), scale=w_("TF", 144 + j, 1))
+
+    def window_tables():
+        lin2(M("N2304"), ID, scale=-2304.0)
+        lin2(M("N48"), ID, scale=-48.0)
+        lin2(M("NI"), ID, scale=-1.0)
+        ms(s("CUM", 0, 273, 272), 0.0)
+        c0 = sm("SELP", 16)[1][0][1]
+        lin2(s("SM", c0, c0 + 16, 2), G8, scale=col("npar"))
+        lin2(s("SM", c0 + 1, c0 + 16, 2), G8, scale=col("par"))
+        for x in range(0, EW, 480):
+            n = min(480, EW - x)
+            sel(w_("OHT", x, n), s("CODE", 0, n), [[2, n // 48], [0, 48]], AL.not_equal, 1.0, x // 24, -1)
+            sel(w_("OHT", x, n), w_("OHT", x, n), [[0, n // 48], [2, 48]], AL.not_equal, 1.0, 1, -1)
+        sel(s("FT", 0, 112), s("ZERO", 0, 112), [[-1, 112]], AL.not_equal, 128.0, 1, 2)
+        sel(s("FT", 0, 112), s("FT", 0, 112), [[-1, 112]], AL.not_equal, 64.0, -95, 2)
+        for j in range(1, 4):
+            lin2(w_("FT", 112 * j, 112), s("FT", 0, 112), scale=0.25 ** j)
+        terms(sm("S7"), [(7, None, 1)])
+        for t in range(8):
+            fill("LC", 320 * (t // 2) + 64 + 128 * (t & 1), 320 * (t // 2) + 128 + 128 * (t & 1))
 
     def lane_numbers():
         mmx([(w_("P1", 16 * i + 8 * h, 8), w_("SR", 128 * h, 128), sm(n)) for h in range(2) for i, n in enumerate(("SELS", "SELC"))])
@@ -649,6 +897,7 @@ def rank_program(g, core, T, topo):
         ts(s("WL", 16, 24), s("TF", 16, 24), 2.0 ** 62, AL.mult)
         tt(s("TI", 16, 32), s("M2", 15, 256, 16), s("SCT", 0, 16), AL.min)
         tt(s("DO"), s("OI"), s("JT", 16, 32), AL.subtract)
+        tt(s("TMP"), ind(s("DO"), s("ELX", 0, 16)), s("MASKR", 0, 256), AL.mult)
         ts(s("TI", 32, 48), s("TI", 16, 32), 16, AL.arith_shift_right)
         for j, b in enumerate((2, 3, 4, 5, 6, 0)):
             over(w_("TH", 512 * j, 512), s("P%d" % b), 11.0)
@@ -665,8 +914,7 @@ def rank_program(g, core, T, topo):
         tt(s("ACT"), s("P1", 96, 112), s("WL", 0, 16), AL.is_lt)
         VAL = w_("VAL", 256 * m, 256)
         lin2(VAL, PV)
-        tt(s("DO"), s("DO"), s("ACT"), AL.mult)
-        tt(s("EXP", 0, 256), ind(s("DO"), s("ELX", 0, 16)), s("MASKR", 0, 256), AL.mult)
+        tt(s("EXP", 0, 256), ind(s("ACT"), s("ELX", 0, 16)), s("TMP"), AL.mult)
         mms([(w_("P3", 8 * h, 8), w_("EXP", 128 * h, 128), G8) for h in range(2)], False)
         if m < 3:
             mmx([(w_("P2", 8 * h, 8), w_("GO", 128 * h, 128), sm("SELE")) for h in range(2)])
@@ -674,10 +922,13 @@ def rank_program(g, core, T, topo):
         cp(L2, s("P3", 0, 16))
         cp(ind(AW, L2), VAL)
         landed = send([w_("A", H + S * d, S) for d in range(3)], "LA", 192 * (m + 1), S)
-        if m == 0:
-            dma("y", s("X", 0, H), ext(T.xv[:, 0:H]), 737280, after=[landed])
+        lands.append(landed)
         if m == 1:
+            dma("y", s("X", 0, H), ext(T.xv[:, 0:H]), 737280, after=[landed])
+        if m == 2:
             dma("y", s("KK", 0, C), ext(T.kc[:]), 524288, after=[landed])
+            dma("y", s("CH0", 0, H), s("CODE", 0, H), 256 * H, after=[landed])
+            fill("CH0", H, VW)
         tt(s("TF", 112, 128), s("SCT", 16, 32), s("JT", 0, 16), AL.subtract)
         tt(s("NM", 16, 32), s("TF", 112, 128), s("ACT"), AL.mult)
         lo = 0 if m < 3 else 16
@@ -704,8 +955,21 @@ def rank_program(g, core, T, topo):
         tt(TTm, s("P5", 0, 192), s("LS"), AL.mult)
         tt(AREP, s("P5", 256, 448), TTm, AL.add)
         act(w_("SQ", 192 * m, 192), TTm, AF.Abs)
-    replica_digits()
-    fill("CH1", 0, VW)
+        if m == 0:
+            k0 = len(nodes)
+            pair_tables()
+            for x in nodes[k0:]:
+                x["push"] = PUSHT
+            window_tables()
+        gap_work(GAPS[m])
+    mmx([(w_("P7", 8 * d, 8), M("PI%d" % d), sm("G8B")) for d in range(3)])
+    lin2(sm("G8P", 24), s("P7", 0, 24))
+    dma("y", s("CH1", 0, H), s("CH0", 0, H), 256 * H, after=[lands[3]])
+    fill("CH1", H, VW)
+    for j in range(6):
+        b, o = s("P6" if j & 1 else "P7", 0, 480), w_("X", 480 * j, 480)
+        mms([(b, ID, o), (b, M("STL"), w_("A", 480 * j, 480))])
+        lin2(o, b)
 
     def changed_digits(lst, n):
         b, o = lst[0][0], s("T192", 0, 192)
@@ -717,23 +981,74 @@ def rank_program(g, core, T, topo):
         ts(w_("MT", 512, n), s("MT", 0, n), 0xAAAAAA, AL.bitwise_and)
         ts(w_("MB", c0, n), w_("MT", 512, n), 0.0, AL.is_gt)
 
-    def piece(win, lo, hi, **k):
-        lin2(s("GR", 1024 * lo, 1024 * hi), ind(win, s("VAP", 64 * lo, 64 * hi)), **k)
+    def piece(win, q, slot, e):
+        n = 128 // len(e)
+        for x, eng in zip(range(0, 128, n), e):
+            lin2(w_("GR", 2048 * slot + 16 * x, 16 * n), ind(win, w_("VAP", 128 * q + x, n)), e={"b": "sv"}.get(eng, eng))
+
+    P96 = slice(0, 96)
+    marks = lambda b: s("P1", 64 * (b % 4) + b // 4, 64 * (b % 4) + 64, 8, p=P96)
+
+    def signs(lo, hi, step=1):
+        o, i = s("BIN", lo, hi, step, p=P96), s("P1", lo, hi, step, p=P96)
+        node({"s": act_(o, i, AF.Sign), "v": ts_(o, i, 0.0, AL.is_gt)}, [o], [i])
+
+    def pair_window(EB=EB):
+        for h in range(2):
+            mms([(s("P1", 256 + h, 384, 2, p=P96), s("FT", 112 * j + 1 - h, 112 * j + 97 - h, p=P96), s("BIN", 64 * j, 64 * j + 64, p=P96)) for j in range(4)])
+        lin2(s("WT", p=P96), s("P1", 256, 384, p=P96))
+        for x in range(0, EW, 480):
+            n, b = min(480, EW - x), EB[x // 480]
+            mm(s(b, 0, n), s("WT", p=P96), s("OHT", x, x + n, p=P96))
+            nodes[lin2(w_("E", x, n), s(b, 0, n), e=EQ[x // 480])]["push"] = PUSHE
+
+    def pair_gather(b, calls):
+        n = 128 // calls
+        for x in range(0, 128, n):
+            k = tt(w_("GR", 2048 * (NS + b) + 16 * x, 16 * n), ind(s("E"), w_("PIX", 128 * b + x, n)), w_("MASK", 2048 * b + 16 * x, 16 * n), AL.mult)
+            nodes[k]["push"] = PUSHP
+
+    def pair_flags(b, lst, last, ZB=ZB, **kw):
+        z, g0, r0 = s(ZB[b % len(ZB)], 0, 256), 2048 * (NS + b), 512 * (b & 1)
+        mmx([(s(z[1][0][0], k, 256, 16), s("GR", g0 + k, g0 + 2048, 16), sm("SELP", 16)) for k in range(16)])
+        lin2(w_("RR", r0, 256), z, 128.0 + EPS)
+        lin2(w_("RR", r0 + 256, 256), z, -128.5 - EPS, -1.0)
+        o = s("P0", b, 128, 8)
+        if last:
+            c0 = 272 * (b & 1)
+            scan(w_("CUM", c0 + 1, 256), w_("RR", r0, 256), w_("RR", r0 + 256, 256), 0.0, AL.add, AL.add)
+            lst = lst + [(o, ID, s("CUM", c0 + 16, c0 + 257, 16)), (o, M("NI"), s("CUM", c0, c0 + 256, 16))]
+        else:
+            lst = lst + [(o, ID, s("RR", r0 + 256 * h + k, r0 + 256 * h + 256, 16)) for h in range(2) for k in range(16)]
+        mms([(o, M("ID16"), s("ONES", 0, 16))] + lst, **kw)
 
     changed_digits([(s("P6", 0, 192), M("BU22"), w_("SQ", 192 * m, 192)) for m in range(4)], "wd")
-    if NMK < 32:
+    mms([(s("P1", 0, 256, p=P96), s("ZERO", 0, 96), s("ZERO"))] + [(marks(30 + j), w_("SQ", 192 * m + 96 * j, 96), sm("S7")) for m in range(4) for j in range(2)])
+    signs(0, 256)
+    if NP0 < NP:
         mms([(s("P3", 256, 448), M("SU"), w_("SQ", 192 * m, 192)) for m in range(4)])
-        tt(AREP, s("P3", 256, 448), AREP, AL.add)
-    for c0 in range(0, 64 * NMK, 512):
-        mask_test(c0, min(512, 64 * NMK - c0), "wd")
-    for j in range(NMK, 32):
-        piece(AW, j, j + 1)
-    for q in range(16):
-        o = s("P0", q, 128, 16)
-        mms([(o, s("OW", q, C, 16), sm("SF"))] + ([(o, w_("MB", 128 * q, 128), sm("G8B"))] if 2 * q < NMK else
-                                                   [(o, s("GR", 2048 * q + k, 2048 * q + 2048, 16), sm("S8")) for k in range(16)]))
-    mms([(s("P3", 0, 128), slide(1, r), s("OW", r, C, 16)) for r in range(16)])
-    ts(s("LO128"), s("P3", 0, 128), float(C), AL.add)
+        lin2(s("CH0", H, V), s("P3", 256, 448))
+    pair_window(("P2", "P3", "P1", "P2", "P3"))
+    for c0 in range(0, 128 * NS, 384):
+        mask_test(c0, min(384, 128 * NS - c0), "wd")
+    rest = [(b + 8 * h, (NS + b, NS - 1 - b + NP0)[h]) for b in range(NP0, NP) for h in range(2)]
+    for q, slot in rest:
+        piece(s("CH0"), q, slot, "bb")
+    if rest:
+        lin2(s("CH0", H, V), s("ZERO", 0, 192))
+    for b in range(NP0):
+        pair_gather(b, 2)
+    first_term = lambda q: (s("P0", q, 128, 16), s("OW", q, C, 16), sm("SF"))
+    for i, q in enumerate(SINGLE):
+        mms([first_term(q), (s("P0", q, 128, 16), w_("MB", 128 * i, 128), sm("G8B"))])
+    for n in range(max(NP0, len(rest))):
+        if n < len(rest):
+            q, slot = rest[n]
+            mms([first_term(q)] + [(s("P0", q, 128, 16), s("GR", 2048 * slot + k, 2048 * slot + 2048, 16), sm("S8")) for k in range(16)])
+        if n < NP0:
+            pair_flags(n, [first_term(n), first_term(n + 8)], n == NP0 - 1, ("P1", "P2"))
+    mms([(s("P4", 0, 128), slide(1, r), s("OW", r, C, 16)) for r in range(16)])
+    ts(s("LO128"), s("P4", 0, 128), float(C), AL.add)
     for j in range(4):
         lin2(w_("GV", 512 * j, 512), ind(AW, w_("LO128", 32 * j, 32)))
         b, o = s("P4" if j & 1 else "P5"), w_("CW2", 512 * j, 512)
@@ -742,14 +1057,10 @@ def rank_program(g, core, T, topo):
     mms([(s("P7", 256, 384), slide(3, r), w_("CW2", 128 * r, 128)) for r in range(16)])
     ts(s("FF", 128, 256), s("P7", 256, 384), float(V), AL.add, float(V), AL.min)
     dma("y", ext(T.yo[:]), s("FF", 128, 256), 65536)
-    for j in range(6):
-        b, o = s("P6" if j & 1 else "P7", 0, 480), w_("X", 480 * j, 480)
-        mms([(b, ID, o), (b, M("STL"), w_("A", 480 * j, 480))])
-        lin2(o, b)
-    mm(s("P3", 256, 448), M("BU"), AREP)
+    mm(s("P6", 256, 448), M("BU"), AREP)
     for d in range(3):
-        ts(w_("T192", S * d, S), w_("P3", 256 + S * d, S), 1.0 if high[d] else 2.0, AL.is_equal)
-    ts(s("T192", 192, 384), s("P3", 256, 448), 0.0, AL.is_equal, STALE, AL.mult)
+        ts(w_("T192", S * d, S), w_("P6", 256 + S * d, S), 1.0 if high[d] else 2.0, AL.is_equal)
+    ts(s("T192", 192, 384), s("P6", 256, 448), 0.0, AL.is_equal, STALE, AL.mult)
     tt(s("T192", 0, 192), s("T192", 0, 192), s("DX"), AL.mult)
     tt(s("T192", 0, 192), s("T192", 0, 192), s("XR0"), AL.add)
     tt(XREP, s("T192", 0, 192), s("T192", 192, 384), AL.max)
@@ -828,7 +1139,7 @@ def rank_program(g, core, T, topo):
         mm(s("P2", 0, 256), ID, s("XO"))
         tt(s("NEQ"), s("P2", 0, 256), s("NX"), AL.not_equal)
         tt(ind(CH, LO), s("NEQ"), GG, AL.mult)
-        send([w_("CH%d" % u, H + S * d, S) for d in range(3)], "LC", 192 * t, S)
+        send([w_("CH%d" % u, H + S * d, S) for d in range(3)], "LC", 320 * t, S, gap=S)
         DOWN = ("OW", "CW")[u]
         cp(ind(s(DOWN), CL), GS)
         mms([(s("P3", 48, 64), slide(3, r), s("CG", c0 + r, c0 + 256, 16)) for r in range(16)] + [(s("P3", 48, 64), slide(4, r), s("GS", r, 256, 16)) for r in range(16)])
@@ -844,21 +1155,34 @@ def rank_program(g, core, T, topo):
             send([part(d, 0, 1) for d in range(3)], "LP", 0, S, XW_X)
         nodes[sends[-1]]["push"] = PUSHX
         left = lambda j: (32 - j) * 0.5 * 1024 * GATHER * CY
-        for j in range(2 * EARLY):
-            piece(CH, j, j + 1)
-        mmx([(w_("P6", S * d, S), M("PI%d" % d), w_("LC", 192 * t + S * d, S)) for d in range(3)])
+        for i in range(EARLY):
+            piece(CH, SINGLE[i], i, SCALLS[i])
+        mmx([(marks(b), w_("CH%d" % u, 96 * b, 96), sm("G8B")) for b in range(30)])
+        signs(0, 256)
+        far = lambda d, c0: (w_("LC", 320 * t + c0, 96), w_("SM", sm("G8P", 24)[1][0][1] + 8 * d, 8))
+        mms([(marks(30), w_("CH%d" % u, H, 96), sm("G8B")), (marks(30), *far(0, 0)), (marks(30), *far(1, 64))])
+        mms([(marks(31), w_("CH%d" % u, H + 96, 96), sm("G8B")), (marks(31), *far(1, 160)), (marks(31), *far(2, 224))])
+        signs(135, 256, 8)
+        mmx([(w_("P6", S * d, S), M("PI%d" % d), w_("LC", 320 * t + 2 * S * d, S)) for d in range(3)])
         tt(CHREP, s("P6", 0, 192), CHREP, AL.add)
+        pair_window()
         if EARLY:
             changed_digits([(s("P6", 0, 192), M("BD22"), CHREP)], "wd")
             mask_test(0, 128 * EARLY, "wd")
-        for j in range(2 * EARLY, 28, 2):
-            piece(CH, j, j + 2)
-        for j in range(28, 32):
-            piece(CH, j, j + 1)
-        for n, q in enumerate(list(range(EARLY, 8)) + list(range(EARLY)) + list(range(8, 16))):
-            o = s("P0", q, 128, 16)
-            mms([(o, ID, s("F", q, 128, 16)), (o, s(DOWN, q, C, 16), sm("SN"))] + ([(o, w_("MB", 128 * q, 128), sm("G8B"))] if q < EARLY else [])
-                + [(o, s("GR", 2048 * q + k, 2048 * q + 2048, 16), sm("G8B")) for k in range(16)], extra=FX * left(2 * n + 2))
+        for i in range(EARLY, NS):
+            piece(CH, SINGLE[i], i, SCALLS[i])
+        for b in range(NP):
+            pair_gather(b, PCALLS[t == 3][b])
+        down = lambda q: (s("P0", q, 128, 16), s(DOWN, q, C, 16), sm("SN"))
+        for n, (kind, i) in enumerate(zip(SUMS[::2], map(int, SUMS[1::2]))):
+            extra = FX * left(32 * (n + 1) // (NS + NP))
+            if kind == "p":
+                pair_flags(i, [(s("P0", i, 128, 8), ID, s("F", i, 128, 8)), down(i), down(i + 8)], i >= NP - SCANS, extra=extra)
+            else:
+                q = SINGLE[i]
+                o = s("P0", q, 128, 16)
+                mms([(o, ID, s("F", q, 128, 16)), down(q)] + ([(o, w_("MB", 128 * i, 128), sm("G8B"))] if i < EARLY else [])
+                    + [(o, s("GR", 2048 * i + k, 2048 * i + 2048, 16), sm("G8B")) for k in range(16)], extra=extra)
         wx = 128 if t else S
         mmx([(w_("P6", S * d, S), M("PI%d" % d), w_("LP", 384 * t + wx * d, S)) for d in range(3)])
         tt(XREP, s("P6", 0, 192), SBX, AL.add)
@@ -876,7 +1200,8 @@ def rank_program(g, core, T, topo):
     mm(s("P5", 0, 192), slide(5, 15), AREP, False, True)
     lin2(s("YW"), s("P5", 0, 192))
     nodes[dma("y", ext(T.yw[:]), s("YW"), 98304)]["push"] = PUSHY
-    ts(s("YB"), s("X", 0, V), 256.0, AL.min)
+    for lo, hi in ((0, 960), (960, 1920), (1920, H), (H, V)):
+        ts(s("YB", lo, hi), s("X", lo, hi), 256.0, AL.min)
     nodes[dma("y", ext(T.y[:]), s("YB"), 786432)]["push"] = PUSHY
     ts(s("F"), s("P0", 0, 128), 0.0, AL.is_gt)
     mm(s("P1", 0, 128), s("F"), M("PERM"))

@@ -8,27 +8,31 @@ STALE = 65536.0
 BIG = 3.0e7
 ALL = (1 << 128) - 1
 B16, F32, I32, U16 = "bfloat16", "float32", "int32", "uint16"
-NP = 4
+NP = 5
 NP0 = 3
 PN, EW = 128 * NP, 48 * 48
 SINGLE = [q for q in range(16) if q % 8 >= NP]
 NS = len(SINGLE)
+NP1 = 4
+DIG = [q for q in range(16) if NP1 <= q % 8 < NP] + SINGLE
+PE0 = 0
+ND = len(DIG)
 LN2 = 0.6931471805599453
 EPS = 2.0 ** -10
 MP = 32
-EARLY = 2
+EARLY = 1
 _sb = {
     "VA": (CWD, I32), "VAP": (C, U16), "A": (VW, B16), "X": (VW, B16), "KK": (CWD, B16), "CW": (CWD, B16), "CW2": (CWD, B16), "OW": (CWD, B16),
-    "CH0": (VW, B16), "CH1": (VW, B16), "GR": (32768, B16), "GW": (4096, B16), "CODE": (V, B16), "MK": (C, F32), "MB": (128 * NS, B16), "MT": (1024, I32), "EQ": (256, B16),
+    "CH0": (VW, B16), "CH1": (VW, B16), "GR": (32768, B16), "GW": (4096, B16), "CODE": (V, B16), "MK": (128 * ND + 2 * PN, F32), "MB": (128 * ND, B16), "MT": (768, I32), "EQ": (256, B16),
     "IO": (256, F32), "ZERO": (256, B16), "GI": (128, F32), "JI": (256, B16), "J1": (256, F32), "II": (128, I32), "CF": (160, F32), "IC": (16, F32),
-    "JW": (128, F32), "TMP": (256, F32), "TMP2": (256, F32), "MAT": (50 * 128, B16), "PIT": (160, B16), "SM": (128, B16), "ZW": (6 * 160, B16), "IDF": (128, F32), "G8": (8, F32),
+    "JW": (128, F32), "TMP": (256, F32), "TMP2": (256, F32), "MAT": (58 * 128, B16), "PIT": (160, B16), "SM": (128, B16), "ZW": (6 * 160, B16), "IDF": (128, F32), "G8": (8, F32),
     "MASKR": (512, F32), "RSB": (256, F32), "RS1": (128, B16), "ELX": (48, U16), "BASEW": (80, F32), "JT": (32, F32),
     "OVI": (128, I32), "OV2": (384, I32), "OVL": (128, U16), "OVB": (256, B16), "WI": (192, I32), "WB": (192, B16), "SI": (128, I32), "SBF": (128, B16), "NLI": (16, I32),
     "LN": (32 * 5, U16), "VARS": (512, U16), "SR": (256, B16), "M1": (256, F32), "YY": (256, F32), "M2": (256, F32),
     "TI": (64, I32), "OI": (16, I32), "TF": (256, F32), "SCT": (32, F32), "ACT": (16, F32), "NM": (32, F32), "DO": (16, F32), "EXP": (512, F32),
     "L1": (16, U16), "L2": (64, U16), "BE": (256, B16), "BO": (256, B16), "GO": (256, B16), "WL": (32, B16), "VT": (272, B16), "VAL": (1024, B16), "YW": (192, F32),
     "ONES": (256, B16), "LA": (192 * 5, B16), "LS": (192, B16), "TT": (192 * 4, B16), "SQ": (192 * 4, B16), "XR0": (192, B16), "DX": (192, B16), "NE": (192, B16), "GM": (192, B16),
-    "T192": (384, F32), "LO128": (128, U16), "LC": (320 * 4, B16), "LP": (384 * 5, B16),
+    "T192": (384, F32), "LO128": (128, U16), "LC": (192 * 4, B16), "RW": (384, B16), "BX": (384, B16), "WR": (128, B16), "ZC": (224, B16), "LP": (384 * 5, B16),
     "F": (128, B16), "FF": (256, F32), "IP": (128, B16), "CR": (128, B16), "CMP": (2048, B16), "POS": (144, F32), "LB": (16, U16), "BC": (16, B16), "OH": (256, B16), "CL": (16, U16),
     "CG": (512, B16), "KR": (256, B16), "XO": (256, B16), "LO": (48, U16), "FL": (256, I32), "GG": (256, B16), "NX": (256, B16),
     "NEQ": (256, B16), "T1": (256, B16), "RH": (128, B16), "C256": (256, B16), "GS": (256, B16),
@@ -41,43 +45,62 @@ for _i in range(8):
 SEMAPHORES = ["cv", "cs", "cp", "cg"] + ["d%d" % i for i in range(56)] + ["ar%d" % i for i in range(14)] + ["ls%d" % i for i in range(14)]
 ALIAS = {"TH": ("GR", 4096, 3072), "DEW": ("GR", 8192, DV0 + C), "DVAL": ("GR", 13568, C), "GV": ("GR", C, C), "YB": ("CH0", 0, V),
          "BITS": ("CH1", 0, DV0), "MASK": ("GR", 32768 - 16 * PN, 16 * PN), "TBM": ("GR", 8192, 4096), "E": ("CODE", 0, EW),
-         "PR": ("GW", 0, 2 * PN), "VAF": ("MK", 128 * NS, 2 * PN)}
+         "PR": ("GW", 0, 2 * PN), "VAF": ("MK", 128 * ND, 2 * PN)}
 CY, PECY, GATHER, SCATTER, FIX, WAKE = 0.00088, 0.00044, 1.2, 3.0, 0.05, 0.1
-VPEN = (0.2, 0.3, 0.4, 0.5)
+VPEN = (0.3, 0.5)
 RATES = ((1.55, 3.6), (1.15, 5.0), (2.0, 2.5), (2.0, 5.5), (1.15, 2.0))
 XW_X = 42.0
 VAP_X = 50.0
 FX = 0.8
-ROUNDS = 6
+ROUNDS = 3
 WP = 32
 DMA0, DMABW, ROWS = 1.5, 250e3, 0.4
 REMOTE = 3.2
 FIRST = 3.5
 MARGIN = 3.0
-GSLACK = 1.3
+GSLACK = 1.15
 PUSHY = 5.0
 DEAR = 1.5
 W3 = "sv"
-PUSH = 3.0
-PUSHX = 10.0
+PUSH = 8.0
+PUSHX = 14.0
 CWDMA = 1
 XP = (0, 32, 64, 96, 128, 160, 192, 224, 256)
 SHAKE = 0.0
 PLAN = []
-POLISH = ((1.55, 3.6, 1.0, 1.0), (1.1, 2.5, 1.4, 1.5), (1.15, 5.0, 1.3, 0.8), (1.25, 3.0, 0.9, 1.8))
+SFIX = 0.015
+POLISH = ((1.5, 3.6, 1.0, 1.6, 1.0, 0.62), (1.1, 2.5, 1.4, 2.2, 1.0, 0.62), (1.15, 4.5, 1.1, 1.4, 1.1, 0.62), (1.35, 3.0, 1.2, 2.6, 1.0, 0.62))
 START = 0
-TRIES, HEAT = 24000, 0.001
+TRIES, HEAT = 24000, 0.005
+SWEEPS = ((60, 600), (60, 600), (100, 800), (160, 1000, 450), (100, 800)) * 2 + ((140, 600), (140, 600), (80, 500), (80, 500), (120, 600), (120, 600), (80, 400))
+NEAR = 0.5
+COOL = 7
+LOG = []
+DEBUG = []
+MOVES = 12
+OWN_X, PUSHO = 12.0, 6.0
 VAW = 1024
 EB = ("P3", "P4", "P1", "P3", "P4")
 EQ = ("sv",) * 5
+EP = ("sv",) * 5
 ZB = ("P1", "P3", "P4")
 GAPS = ("dmdd", "xddd", "dxdm", "")
-SCANS = 1
-PUSHE = 0.0
+SCAN0 = 1
+TWO = (0, 1, 2, 3, 4, 5, 7, 9, 11)
+BOG = 1
+QUICK = (1, 2)
+HALVES = 1
+LANES = 0
+AD, TBE = 0, "sv"
+SG = 2
+HOLD = (9, 1)
+RRC, RRE = 1, ("sv", "sv")
+SCANS = 2
+PUSHE = 3.0
 PUSHT, PUSHM, PUSHP = 10.0, 0.0, 0.0
-SCALLS = ("bb", "bb", "b", "b", "b", "b", "bb", "bb")
-PCALLS = ((1, 1, 1, 2), (1, 2, 2, 2))
-SUMS = "s2s0s1s3p0s4p1s5p2s6p3s7"
+SCALLS = ("ssss", "s", "s", "s", "ss", "bbbb")
+PCALLS = ((1, 1, 1, 1, 2), (1, 1, 2, 2, 2))
+SUMS = "s0s1s2p0s3p1p2s4p3p4s5"
 
 
 def rank_program(g, core, T, topo):
@@ -88,19 +111,21 @@ def rank_program(g, core, T, topo):
     CS = {"v": "cv", "s": "cs", "p": "cp", "g": "cg"}
     nodes, rec, banks, nd = [], {}, {}, [0]
 
-    def node(alt, outs, ins, sem=None, inc=1, lat=None, extra=0.0, after=()):
+    def node(alt, outs, ins, sem=None, inc=1, lat=None, extra=0.0, after=(), whole=True):
         me = len(nodes)
         wr = [r for o in outs for r in o[1]]
         rd = [r for o in outs for r in o[2]] + [r for o in ins if isinstance(o, tuple) for r in o[1] + o[2]]
         pred = set(after)
         eng = "".join(alt) if len(alt) == 1 else me
         for b in {r[0] for r in wr + rd if r[0][0] == "P" and r[0][1:].isdigit()}:
-            st = banks.setdefault(b, [None, [], []])
+            st = banks.setdefault(b, [None, [], [], []])
             if st[0] != eng:
                 st[0], st[1], st[2] = eng, [], st[1]
             pred.update(st[2])
-            if eng == "p" and st[1]:
-                pred.add(st[1][-1])
+            if eng == "p":
+                pred.update(st[3] if whole else st[1] + st[3])
+                if not whole:
+                    st[3] = [me]
             st[1].append(me)
         for regs, w in ((wr, True), (rd, False)):
             for (b, lo, hi, tg) in regs:
@@ -114,7 +139,7 @@ def rank_program(g, core, T, topo):
                 rec.setdefault(b, []).append((lo, hi, tg, w, me))
         pred.discard(me)
         kind = 2 if any(o[5] == "ind" for o in outs) else 1 if any(isinstance(o, tuple) and o[5] == "ind" for o in ins) else 0
-        nodes.append({"alt": alt, "pred": pred, "sem": sem, "inc": inc, "lat": lat, "extra": extra, "kind": kind})
+        nodes.append({"alt": alt, "pred": pred, "sem": sem, "inc": inc, "lat": lat, "extra": extra, "kind": kind, "name": (wr + rd + [("", 0)])[0][:2]})
         return me
 
     def writers(*xs):
@@ -196,7 +221,7 @@ def rank_program(g, core, T, topo):
     def mms(lst, st=True, sp=True, tile=None, **k):
         c = sum(max(min(64, l[3]), r[3]) * (4 if l[4] == F32 else 1) for (o, l, r) in lst) * PECY
         calls = [(o, l, r, st and n == 0, sp and n == len(lst) - 1, tile) for n, (o, l, r) in enumerate(lst)]
-        return node({"p": (c, calls)}, [x[0] for x in lst], [x[1] for x in lst] + [x[2] for x in lst], inc=len(lst), **k)
+        return node({"p": (c, calls)}, [x[0] for x in lst], [x[1] for x in lst] + [x[2] for x in lst], inc=len(lst), whole=st and sp, **k)
 
     def mm(o, l, r, st=True, sp=True, tile=None):
         return mms([(o, l, r)], st, sp, tile)
@@ -218,10 +243,10 @@ def rank_program(g, core, T, topo):
     def sel(o, i, pat, cmp, fil, base, cm=1):
         return node({"g": (GSLACK * (0.17 + 2 * o[3] * CY), lambda: g.affine_select(o[0], i[0], pat, cmp, fil, base, cm))}, [o], [i])
 
-    def dma(q, o, i, nbytes, **k):
+    def dma(q, o, i, nbytes, rows=128, **k):
         sem = "d%d" % nd[0]
         nd[0] += 1
-        c = ROWS + nbytes / DMABW
+        c = ROWS * rows / 128 + nbytes / DMABW
         me = node({"d": (c, lambda: Q[q].dma_start(o[0], i[0]))}, [o], [i], sem=sem, inc=16, lat=DMA0 + c, **k)
         nodes[me]["by"] = q
         return me
@@ -238,10 +263,15 @@ def rank_program(g, core, T, topo):
         side = far_die if len(pool[far_die]) >= len(en) // 4 else not far_die
         lanes.append(pool[side][:len(en) // 4])
         pool[side] = pool[side][len(en) // 4:]
+    near = sorted(range(3), key=lambda d: topo.die(core) != topo.die(T.cores[rank ^ (d + 1)]))
+    wide = [None] * 3
+    wide[near[0]], wide[near[1]], wide[near[2]] = en[0::2], en[1::2], en
+    ways = (([[0, 1, 2]], lanes), ([near[:2], near[2:]], wide))
 
     def send(srcs, land, base, w, extra=0.0, gap=0):
         m = len(sends)
         trs, tot = [], 0
+        calls, lanes = ways[m in TWO]
         for d in (1, 2, 3):
             dst = T.cores[rank ^ d]
             rid, pid, _ = topo.addr(dst)
@@ -252,8 +282,9 @@ def rank_program(g, core, T, topo):
                                          src=srcs[d - 1][0], dst=w_(land, base + (d - 1) * (w + gap), w)[0]))
 
         def go():
-            g.remote_dma_fused(trs, local_sem=T.sem["ls%d" % m])
-        k = node({"g": (0.6 + (0 if m else FIRST), go)}, [], srcs, sem="ls%d" % m, inc=tot, lat=REMOTE + (MARGIN if extra and m < 12 else 0) + (0 if m else FIRST), after=sends[-1:], extra=extra)
+            for c in calls:
+                g.remote_dma_fused([trs[d] for d in c], local_sem=T.sem["ls%d" % m])
+        k = node({"g": (0.6 * len(calls) + (0 if m else FIRST), go)}, [], srcs, sem="ls%d" % m, inc=tot, lat=REMOTE - 0.2 * (m in TWO) + (MARGIN if extra and m < 12 else 0) + (0 if m else FIRST), after=sends[-1:], extra=extra)
         nodes[k]["order"] = set(sends[-1:])
         sends.append(k)
         return node({"-": (0.0, None)}, [w_(land, base + d * (w + gap), w) for d in range(3)], [], sem="ar%d" % m, inc=tot, lat=0.01, after=[k])
@@ -454,6 +485,272 @@ def rank_program(g, core, T, topo):
             for p, k in enumerate(best[1]):
                 out[k] = (best[2][k], best[3][k], nodes[k]["alt"][best[2][k]][0], p)
             return out
+        def improve(at):
+            order = sorted(range(n), key=lambda k: (at[k][1], k))
+            que = [x[0] for x in at]
+            ns = len(POLISH)
+
+            def times(k):
+                c, kind = nodes[k]["alt"][que[k]][0], nodes[k]["kind"]
+                if que[k] == "p":
+                    return [c * x[4] for x in POLISH]
+                if que[k] in "vs" and not kind:
+                    return [c * x[5] if c < FIX + 65 * CY else c for x in POLISH]
+                more = SFIX if que[k] == "s" else 0.0
+                return [FIX + more + (c - FIX) * (0, x[0] / GATHER, x[1] / SCATTER)[kind] if kind else c for x in POLISH]
+            cs = [list(z) for z in zip(*[times(k) for k in range(n)])]
+            ins, outs, last = [], [], []
+            for ga, sc, slow, wake, pe, fix in POLISH:
+                e = [[(j, None if j in y.get("order", ()) or not nodes[j]["lat"] else nodes[j]["lat"] * slow,
+                       (delay(j, 0.0, k) - (0.0 if j in y.get("order", ()) else nodes[j]["lat"] or 0.0)) * wake) for j in y["pred"]] for k, y in enumerate(nodes)]
+                o = [[] for _ in range(n)]
+                for k in range(n):
+                    for j, lat, w in e[k]:
+                        o[j].append((k, lat, w))
+                ins.append(e)
+                outs.append(o)
+            own = [x["lat"] or 0.0 for x in nodes]
+
+            def heads(c, e, t0, part, rel, free):
+                for k in part:
+                    q = que[k]
+                    t = rel[k]
+                    if q != "-" and free[q] > t:
+                        t = free[q]
+                    for j, lat, w in e[k]:
+                        x = t0[j] + (lat or c[j]) + w
+                        if x > t:
+                            t = x
+                    t0[k] = t
+                    free[q] = t + c[k]
+                return t0
+
+            def tails(c, o, y, part, oc, ol, nxt):
+                for k in reversed(part):
+                    q, ck = que[k], c[k]
+                    t = ck + oc[k]
+                    if q != "-" and ck + nxt[q] > t:
+                        t = ck + nxt[q]
+                    if ol[k] > t:
+                        t = ol[k]
+                    for j, lat, w in o[k]:
+                        x = (lat or ck) + w + y[j]
+                        if x > t:
+                            t = x
+                    y[k] = nxt[q] = t
+                return y
+            zero, seed = [0.0] * n, 1
+            blank = lambda: dict.fromkeys("vspgd-", 0.0)
+            for sweep, (width, tries, *upto) in enumerate(SWEEPS):
+                ys = [tails(cs[r], outs[r], [0.0] * n, order, zero, own, blank()) for r in range(ns)]
+                ts0 = [heads(cs[r], ins[r], [0.0] * n, order, zero, blank()) for r in range(ns)]
+                norm = [1.0 / max(y) for y in ys]
+                LOG.append([round(max(y), 1) for y in ys])
+                for p0 in range(-(width // 4) * (sweep & 1), (upto + [n])[0], width // 2):
+                    p0, p1 = max(p0, 0), min(n, p0 + width)
+                    part = order[p0:p1]
+                    m, inside = len(part), set(part)
+                    sub = []
+                    for r in range(ns):
+                        c, t0, y, rel, oc, ol, qf, qt = cs[r], ts0[r], ys[r], {}, {}, {}, blank(), blank()
+                        e, o = {}, {}
+                        for k in part:
+                            e[k] = [z for z in ins[r][k] if z[0] in inside]
+                            o[k] = [z for z in outs[r][k] if z[0] in inside]
+                            rel[k] = max([t0[j] + (lat or c[j]) + w for j, lat, w in ins[r][k] if j not in inside] + [0.0])
+                            oc[k] = max([w + y[j] for j, lat, w in outs[r][k] if j not in inside and not lat] + [0.0])
+                            ol[k] = max([lat + w + y[j] for j, lat, w in outs[r][k] if j not in inside and lat] + [own[k]])
+                        for k in order[:p0]:
+                            qf[que[k]] = t0[k] + c[k]
+                        for k in reversed(order[p1:]):
+                            qt[que[k]] = y[k]
+                        sub.append((c, e, o, rel, oc, ol, qf, qt))
+
+                    def full(pj, pk, now):
+                        out, cand, total = [], [], 0.0
+                        before, seen, nxt = {}, {}, {}
+                        for k in part[:pj]:
+                            before[k], seen[que[k]] = seen.get(que[k]), k
+                        prev = dict(seen)
+                        for k in part[pj:]:
+                            before[k], seen[que[k]] = seen.get(que[k]), k
+                        for k in part[:pk:-1]:
+                            nxt[que[k]] = k
+                        late, early = part[pj:], part[:pk + 1]
+                        for (c, e, o, rel, oc, ol, qf, qt), (t0, y), w0 in zip(sub, now, norm):
+                            t0 = heads(c, e, dict(t0), late, rel, {q: t0[prev[q]] + c[prev[q]] if q in prev else qf[q] for q in qf})
+                            y = tails(c, o, dict(y), early, oc, ol, {q: y[nxt[q]] if q in nxt else qt[q] for q in qt})
+                            thru = [t0[k] + y[k] for k in part]
+                            top_ = max(thru)
+                            total += top_ * w0
+                            bar_ = top_ - NEAR
+                            for k, x in zip(part, thru):
+                                if x >= bar_:
+                                    j = before[k]
+                                    if j is not None and t0[j] + c[j] >= t0[k] - 1e-9 and que[k] != "-":
+                                        cand.append((j, k))
+                            out.append((t0, y))
+                        return total, out, cand
+
+                    def least(pj, pk):
+                        seg, total = part[pj:pk + 1], 0.0
+                        need = {que[k] for k in seg}
+                        need.discard("-")
+                        prev, nxt = {}, {}
+                        for p in range(pj - 1, -1, -1):
+                            q = que[part[p]]
+                            if q in need and q not in prev:
+                                prev[q] = part[p]
+                                if len(prev) == len(need):
+                                    break
+                        for p in range(pk + 1, m):
+                            q = que[part[p]]
+                            if q in need and q not in nxt:
+                                nxt[q] = part[p]
+                                if len(nxt) == len(need):
+                                    break
+                        for (c, e, o, rel, oc, ol, qf, qt), (old, y), w0 in zip(sub, now, norm):
+                            free = {q: old[prev[q]] + c[prev[q]] if q in prev else qf[q] for q in need}
+                            free["-"] = 0.0
+                            t0, top_ = {}, 0.0
+                            for k in seg:
+                                q = que[k]
+                                t = rel[k]
+                                if q != "-" and free[q] > t:
+                                    t = free[q]
+                                for j, lat, w in e[k]:
+                                    x = (t0[j] if j in t0 else old[j]) + (lat or c[j]) + w
+                                    if x > t:
+                                        t = x
+                                t0[k] = t
+                                free[q] = t + c[k]
+                            for k in seg:
+                                ck = c[k]
+                                x = max(ck + oc[k], ol[k])
+                                for j, lat, w in o[k]:
+                                    if j not in t0:
+                                        z = (lat or ck) + w + y[j]
+                                        if z > x:
+                                            x = z
+                                if t0[k] + x > top_:
+                                    top_ = t0[k] + x
+                            for q in need:
+                                x = free[q] + (y[nxt[q]] if q in nxt else qt[q])
+                                if x > top_:
+                                    top_ = x
+                            total += top_ * w0
+                        return total
+                    score, now, cand = full(0, m - 1, [({}, {})] * ns)
+                    best = (score, part[:], [que[k] for k in part])
+                    for it in range(tries if cand else 0):
+                        seed = (seed * 1103515245 + 12345) % 2147483648
+                        j, k = cand[(seed >> 8) % len(cand)]
+                        move, pj, pk = (seed >> 4) % MOVES, part.index(j), part.index(k)
+                        if move >= 4:
+                            v = (j, k)[move & 1]
+                            pv = part.index(v)
+                            lo, hi = pv - 1, pv + 1
+                            while lo >= 0 and part[lo] not in nodes[v]["pred"]:
+                                lo -= 1
+                            while hi < m and v not in nodes[part[hi]]["pred"]:
+                                hi += 1
+                            was, pick, ends = que[v], None, []
+                            for (c, e, o, rel, oc, ol, qf, qt), (t0, y) in zip(sub, now):
+                                ends.append((max([t0[z] + (lat or c[z]) + w for z, lat, w in e[v]] + [rel[v]]),
+                                             max([w + y[z] for z, lat, w in o[v] if not lat] + [oc[v]]),
+                                             max([lat + w + y[z] for z, lat, w in o[v] if lat] + [ol[v]])))
+                            for q in nodes[v]["alt"]:
+                                que[v] = q
+                                cv = times(v)
+                                p = lo
+                                while p >= 0 and (que[part[p]] != q or p == pv):
+                                    p -= 1
+                                u = part[p] if p >= 0 else None
+                                for p in range(lo + 1, m + 1):
+                                    x = part[p] if p < m else None
+                                    if p == pv or (x is not None and que[x] != q):
+                                        continue
+                                    if not (q == was and (u is None or part.index(u) < pv) and p > pv):
+                                        est = 0.0
+                                        for sb, (t0, y), en_, cc, w0 in zip(sub, now, ends, cv, norm):
+                                            a_ = sb[6][q] if u is None else t0[u] + sb[0][u]
+                                            b_ = sb[7][q] if x is None else y[x]
+                                            est += w0 * (max(a_, en_[0]) + max(cc + max(b_, en_[1]), en_[2]))
+                                        seed = (seed * 1103515245 + 12345) % 2147483648
+                                        est += HEAT * ((seed >> 10) % 32) / 32
+                                        if pick is None or est < pick[0]:
+                                            pick = (est, q, min(p, hi))
+                                    if p >= hi:
+                                        break
+                                    u = x
+                            que[v] = was
+                            if pick is None:
+                                continue
+                            p = pick[2]
+                            pj, pk = min(p, pv), max(p - 1, pv)
+                            keep, moved = part[pj:pk + 1], v
+                            rest_ = [z for z in keep if z != v]
+                            part[pj:pk + 1] = [v] + rest_ if p <= pv else rest_ + [v]
+                            que[v] = pick[1]
+                            for c, x in zip(cs, times(v)):
+                                c[v] = x
+                        for hop in range((seed >> 20) % 4 if move < 2 else 0):
+                            step = 1 if move else -1
+                            p = (pk if move else pj) + step
+                            while 0 <= p < m and que[part[p]] != que[k]:
+                                p += step
+                            if 0 <= p < m:
+                                pj, pk = (pj, p) if move else (p, pk)
+                                j, k = part[pj], part[pk]
+                        if move < 4:
+                            keep, moved = part[pj:pk + 1], None
+                        if move < 2:
+                            grp = {k if move == 0 else j}
+                            for z in (reversed(keep) if move == 0 else keep):
+                                if z in grp:
+                                    grp.update(nodes[z]["pred"] if move == 0 else succ[z])
+                            if (j if move == 0 else k) in grp:
+                                continue
+                            a0, a1 = [z for z in keep if z in grp], [z for z in keep if z not in grp]
+                            part[pj:pk + 1] = a0 + a1 if move == 0 else a1 + a0
+                        elif move < 4:
+                            moved = (j, k)[move - 2]
+                            other = [q for q in nodes[moved]["alt"] if q != que[moved]]
+                            if not other:
+                                continue
+                            was, que[moved] = que[moved], other[0]
+                            for c, x in zip(cs, times(moved)):
+                                c[moved] = x
+                        bar = score + HEAT * (1.0 if sweep < len(SWEEPS) - COOL else 0.3) * (1.0 - it / tries) * ((seed >> 12) % 16) / 16
+                        new = full(pj, pk, now) if least(pj, pk) <= bar else None
+                        if new and new[0] <= bar and new[2]:
+                            score, now, cand = new
+                            part.sort(key=now[0][0].get)
+                            if score < best[0]:
+                                best = (score, part[:], [que[k] for k in part])
+                        else:
+                            part[pj:pk + 1] = keep
+                            if moved is not None:
+                                que[moved] = was
+                                for c, x in zip(cs, times(moved)):
+                                    c[moved] = x
+                    part = order[p0:p1] = best[1]
+                    for k, q in zip(part, best[2]):
+                        if que[k] != q:
+                            que[k] = q
+                            for c, x in zip(cs, times(k)):
+                                c[k] = x
+                    for r, (c, e, o, rel, oc, ol, qf, qt) in enumerate(sub):
+                        heads(c, e, ts0[r], part, rel, dict(qf))
+            if DEBUG:
+                for r in range(ns):
+                    y = tails(cs[r], outs[r], [0.0] * n, order, zero, own, blank())
+                    t0 = heads(cs[r], ins[r], [0.0] * n, order, zero, blank())
+                    DEBUG.append([(round(t0[k], 2), que[k], round(cs[r][k], 2), nodes[k]["name"], round(max(y) - t0[k] - y[k], 2)) for k in order])
+            out = [None] * n
+            for p, k in enumerate(order):
+                out[k] = (que[k], 0.0, nodes[k]["alt"][que[k]][0], p)
+            return out
         top = []
         for spare in (() if PLAN else VPEN):
             far = [0.0] * n
@@ -475,7 +772,7 @@ def rank_program(g, core, T, topo):
                     for j in nodes[k]["pred"]:
                         far[j] = max(far[j], far[k] + delay(j, at[j][2], k))
         if not PLAN:
-            PLAN.append(polish(sorted(top)[START][2]))
+            PLAN.append(improve(sorted(top)[START][2]))
         for x, at in zip(nodes, PLAN[0]):
             x["q"], x["t"] = at[0], max([at[3]] + [nodes[j]["t"] for j in x["pred"]])
         cnt, waited, tiles = {}, {}, {}
@@ -561,22 +858,24 @@ def rank_program(g, core, T, topo):
     ID, G8, BD = shift(0), s("G8"), M("BD")
     Z128, O128 = s("ZERO", 0, 128), s("ONES", 0, 128)
 
-    first = [dma("y", s("OVI"), ext(T.ov[:]), 65536), dma("y", s("WI"), ext(T.wv[:]), 98304)]
+    first = [dma("y", s("WI"), ext(T.wv[:]), 98304), dma("y", s("OVI"), ext(T.ov[:]), 65536), dma("y", s("NLI"), ext(T.nl[:]), 8192)]
     ms(s("ZERO"), 0.0)
+    ms(s("CODE", 0, 960), 0.0)
     for i in (4, 5):
-        first.append(dma("y", s("DEW", 0, V, p=row(i)), s("ZERO", 0, 192), 49152))
+        first.append(dma("y", s("DEW", 0, V, p=row(i)), s("CODE", 0, 768, p=slice(0, 32)), 49152, rows=32))
+    first.append(dma("y", s("SI"), ext(T.sc[:]), 65536))
+    dma("y", XREP, ext(T.xv[:, H:V]), 49152)
     for x in range(0, C, VAW):
         va_in = dma("y", w_("VA", x, VAW), ext(T.va[:, x:x + VAW]), 512 * VAW, after=first)
         nodes[va_in]["order"] = set(first)
-    dma("y", s("NLI"), ext(T.nl[:]), 8192)
-    dma("y", s("SI"), ext(T.sc[:]), 65536)
-    dma("y", XREP, ext(T.xv[:, H:V]), 49152)
+        first = [va_in]
     iota(s("II", 0, 1), [[0, 1]], 0, 1, False)
     iota(s("IO"), [[1, 256]], 0, 0)
     iota(s("JW"), [[16, 128]], 0, 1)
     iota(s("II", 16, 48), [[1, 32]], 0, 0, False)
     iota(s("II", 48, 56), [[16, 8]], 15, 0, False)
-    ms(s("ONES"), 1.0)
+    const = lambda o, c: lin2(o, s("ZERO", 0, o[3]), c)
+    const(s("ONES"), 1.0)
     sel(s("ZW", 0, 160), s("ZERO", 0, 160), [[-1, 160]], AL.not_equal, 1.0, 16)
     iota(M("SELK"), [[0, 8], [4096, 16]], 2048, 0)
     sel(M("SELK"), M("SELK"), [[-16, 8], [0, 16]], AL.is_equal, 0.0, -6)
@@ -585,24 +884,24 @@ def rank_program(g, core, T, topo):
     lin2(s("RSB", 0, 256, 16), s("ONES", 0, 16), scale=BIG)
     sel(G8, s("ONES", 0, 8), [[-16, 8]], AL.is_ge, 0.0, 0)
     sel(G8, G8, [[16, 8]], AL.is_ge, 0.0, 15, -1)
-    terms(sm("SELS"), [(0, None, 65536)])
+    terms(sm("SELS"), [(8, None, 65536)])
     terms(sm("SELC"), [(4, None, 256), (5, None, 1)])
     lin2(s("IDF"), ID)
-    ms(s("CODE", 0, 960), 0.0)
     for x in (960, 1920):
         dma("y", w_("CODE", x, 960), s("CODE", 0, 960), 245760, after=[va_in])
-    ms(s("TMP", 0, 8), 2.0)
-    ms(s("TMP", 8, 136), 0.0)
+    const(s("TMP", 0, 8), 2.0)
     ts(s("II", 1, 2), s("II", 0, 1), 15, AL.bitwise_and)
     ts(s("II", 2, 3), s("II", 0, 1), 112, AL.bitwise_and)
     ts(s("II", 3, 4), s("II", 0, 1), 16, AL.bitwise_and)
     ts(s("II", 4, 5), s("II", 0, 1), 1, AL.bitwise_and)
     ts(s("II", 5, 6), s("II", 0, 1), 14, AL.bitwise_and)
-    for n in ("p", "i", "g16", "odd", "par", "r2"):
+    ts(s("II", 6, 7), s("II", 0, 1), 7, AL.bitwise_and)
+    for n in ("p", "i", "g16", "odd", "par", "r2", "r8"):
         col(n)
     cp(s("CF", 0, 4), s("II", 0, 4))
-    cp(s("CF", 4, 6), s("II", 4, 6))
-    ms(s("VA", C, CWD), NV)
+    cp(s("CF", 4, 7), s("II", 4, 7))
+    ms(s("VA", C, C + 16), NV)
+    iota(s("VA", C + 16, CWD), [[0, CWD - C - 16]], NV, 0, False)
     ts(s("IC"), s("IO", 0, 16), col("i"), AL.is_equal)
     ts(s("BITS", 0, 1), col("i"), 12.0, AL.is_lt)
     for n in range(8):
@@ -614,19 +913,13 @@ def rank_program(g, core, T, topo):
     ts(s("TF", 128, 144), s("IC"), -2.0, AL.mult, 1.0, AL.add)
     lin("cw", [(4, -8), (6, 1), (7, 1)])
     lin2(col("ca"), ic(0), col("cw"), 255.0)
-    scan(w_("CF", cols["w5_0"], 8), s("TMP", 0, 8), s("TMP", 8, 16), col("h5"), AL.mult, AL.add)
-    scan(w_("CF", cols["w4_0"], 4), s("TMP", 0, 4), s("TMP", 8, 12), col("h4"), AL.mult, AL.add)
-    for win, c0, wd in (("A", "ca", VW), ("CW", "cw", CWD))[:2 - CWDMA]:
-        lin2(s(win, 0, 256), s("IO"), col(c0), ic(5))
-        for k in range(4):
-            n = 256 << k
-            w = min(n, wd - n)
-            lin2(w_(win, n, w), s(win, 0, w), col("w4_%d" % k))
-    for gg in range(8 * CWDMA):
-        pp = slice(16 * gg + 1, 16 * gg + 16)
-        dma("y", s("CW", p=pp), s("A", 0, CWD, p=pp), 69120)
-    if CWDMA:
-        dma("y", s("CW", C, CWD, p=row(0)), s("ZERO", 0, 16), 4096)
+    scan(w_("CF", cols["w5_0"], 8), s("TMP", 0, 8), s("ZERO", 0, 8), col("h5"), AL.mult, AL.add)
+    scan(w_("CF", cols["w4_0"], 4), s("TMP", 0, 4), s("ZERO", 0, 4), col("h4"), AL.mult, AL.add)
+    lin2(s("A", 0, 256), s("IO"), col("ca"), ic(5))
+    for k in range(4):
+        n = 256 << k
+        w = min(n, VW - n)
+        lin2(w_("A", n, w), s("A", 0, w), col("w4_%d" % k))
     for b in range(12):
         n = 1 << b
         w = min(n, DV0 - n)
@@ -646,12 +939,12 @@ def rank_program(g, core, T, topo):
     tt(s("TMP", 128, 256), s("TMP", 128, 256), s("TMP2", 128, 256), AL.mult)
     cp(s("LN", 0, 16), s("NLI"))
     tt(s("OV2", 0, 128), s("TMP", 128, 256), s("OVI"), AL.add)
-    dma("y", s("CW", 0, C, p=row(0)), s("SBF"), 32768)
+    dma("y", s("A", 0, C, p=row(8)), s("SBF"), 32768)
     cp(s("OVL"), s("OV2", 0, 128))
     VARS0 = s("VARS", 0, 256)
-    cp(VARS0, ind(s("VA"), s("LN", 0, 16)))
+    cp(VARS0, ind(s("VA", 0, C + 16), s("LN", 0, 16)))
     for j in range(8):
-        cp(ind(s("DEW"), w_("OVL", 16 * j, 16)), w_("DVAL", 256 * j, 256))
+        nodes[cp(ind(s("DEW"), w_("OVL", 16 * j, 16)), w_("DVAL", 256 * j, 256), extra=OWN_X - j)]["push"] = PUSHO
     send([w_("X", H + S * d, S) for d in range(3)], "LA", 0, S)
     iota(s("JT", 0, 16), [[128, 2], [0, 8]], 0, 1)
     iota(s("JT", 16, 32), [[128, 2], [0, 8]], DV0, 1)
@@ -659,7 +952,7 @@ def rank_program(g, core, T, topo):
     sel(BD, O128, [[-16, 8], [0, 16]], AL.is_ge, 0.0, 0)
     sel(BD, BD, [[16, 8], [0, 16]], AL.is_ge, 0.0, 15, -1)
     terms(sm("SELE"), [(2, None, 256), (3, None, 1)])
-    terms(M("SV1"), [(4, 4, 1), (5, 5, 1), (6, 6, 1), (6, 1, 1)])
+    terms(M("SV1"), [(4, 4, 1), (5, 5, 1), (6, 6, 1), (6, 1, 1), (8, 8, 1)])
     terms(M("SV2"), [(4, 2, 1), (5, 3, 1)])
     sel(s("PIT"), s("ZERO", 0, 160), [[16, 10], [-1, 16]], AL.not_equal, 1.0, -48)
     sel(s("PIT"), s("PIT"), [[16, 10], [-1, 16]], AL.not_equal, 1.0, -48 - 128)
@@ -675,8 +968,8 @@ def rank_program(g, core, T, topo):
     cp(s("ELX", 0, 40), s("II", 16, 56))
     lin2(col("od"), col("odd"), scale=1.0 / 16)
     ts(col("ev"), col("odd"), 1.0, AL.is_lt)
-    ms(s("TMP2", 0, 128), 0.5)
-    ms(s("YY", 0, 1), 0.0)
+    const(s("TMP2", 0, 128), 0.5)
+    lin2(s("YY", 0, 256, 128), s("ZERO", 0, 2))
     scan(s("T192", 0, 128), s("TMP2", 0, 128), Z128, 2.0 ** 61, AL.mult, AL.add)
     lin2(s("BASEW", 0, 16), s("JW", 0, 16), float(DV0))
     tt(s("T192", 0, 128), s("T192", 0, 128), s("IDF"), AL.mult)
@@ -692,7 +985,7 @@ def rank_program(g, core, T, topo):
         col("pg%d" % n)
     cp(w_("CF", cols["pg0"], 3), s("II", 12, 15))
     lin2(s("BASEW", 32, 48), s("JW", 0, 16), float(C))
-    ms(s("BASEW", 16, 32), float(C))
+    const(s("BASEW", 16, 32), float(C))
     for d in range(3):
         lin2(M("PD%d" % d), M("PI%d" % d), scale=col("r07"))
         k = ts(M("PK%d" % d), s("GI"), col("pg%d" % d), AL.is_equal, col("kh" if high[d] else "kl"), AL.mult)
@@ -715,9 +1008,10 @@ def rank_program(g, core, T, topo):
     lin2(s("CW2", C, CWD), s("ONES"), scale=col("t8"))
     terms(s("ZW", 160, 320), [(4, 15, 256), (5, 15, 1)])
     terms(M("BU22"), [(7, None, -2 ** 22)])
-    terms(M("BU"), [(7, None, 1)])
+    terms(M("BH"), [(7, None, -1), (6, None, 2)])
+    terms(M("BL"), [(7, None, 1), (6, None, -1)])
     terms(M("BDE"), [(2, 8, 2 ** 20), (3, 8, 4096), (2, 9, -2 ** 20), (3, 9, -4096)])
-    terms(M("NBO"), [(4, 8, -2 ** 20), (5, 8, -4096), (4, 9, 2 ** 20), (5, 9, 4096), (0, 0, 1), (6, 4, 4), (6, 6, 1)])
+    terms(M("NBO"), [(4, 8, -2 ** 20), (5, 8, -4096), (4, 9, 2 ** 20), (5, 9, 4096), (8, 0, 1), (6, 4, 4), (6, 6, 1)])
     terms(M("BO"), [(4, None, 256), (5, None, -1)])
     terms(M("MN"), [(4, 4, -1), (6, 4, 4), (5, 5, 1), (6, 6, 1)])
     terms(sm("SELW"), [(0, None, 1)])
@@ -737,8 +1031,6 @@ def rank_program(g, core, T, topo):
     iota(s("II", 64, 72), [[16, 2], [32, 4]], 0, 0, False)
     ts(s("ELX", 40, 48), s("II", 64, 72), col("i"), AL.add)
     sel(sm("G8B"), G8, [[0, 8]], AL.is_ge, 0.0, 0)
-    if EARLY:
-        lin2(M("BD22"), BD, scale=-2.0 ** 22)
     sel(s("RS1"), O128, [[0, 8], [1, 16]], AL.not_equal, 0.0, 0, 0)
     iota(s("JI"), [[1, 16], [16, 16]], 0, 0)
     iota(s("J1"), [[1, 256]], 1, 0)
@@ -781,7 +1073,7 @@ def rank_program(g, core, T, topo):
 
     def replica_digits():
         i = len(done["d"])
-        q = SINGLE[i]
+        q = DIG[i]
         for h in (2 * i, 2 * i + 1):
             b0 = 16384 + 1024 * (h % NS)
             for x in range(0, 64, MP):
@@ -792,16 +1084,16 @@ def rank_program(g, core, T, topo):
     def pair_list():
         nh = PN // 2
         o, c0 = s("P7", 0, nh), nh * len(done["x"])
-        mms([(o, s("IDF"), w_("VAF", c0, nh))], True, False)
-        mms([(o, s("IDF"), w_("VAF", PN + c0, nh))], False, False)
-        mms([(o, M("N2304"), w_("PR", c0, nh)), (o, M("N48"), w_("PR", PN + c0, nh))], False)
-        ts(w_("PIX", c0, nh), o, 129.0 * 2352, AL.add)
+        mms([(o, M("I48"), w_("PR", c0, nh)), (o, ID, w_("PR", PN + c0, nh))])
+        ts(w_("PIX", c0, nh), o, -129.0 * 49, AL.add)
 
     def pair_mask():
         nh = PN // 2
         o, c0 = s("P7", 0, nh), nh * len(done["m"])
-        mms([(o, M("I64"), w_("PR", c0, nh)), (o, ID, w_("PR", PN + c0, nh))])
-        ts(w_("MIX", c0, nh), o, -129.0 * 65, AL.add)
+        mms([(o, s("IDF"), w_("VAF", c0, nh))], True, False)
+        mms([(o, s("IDF"), w_("VAF", PN + c0, nh))], False, False)
+        mms([(o, M("N4096"), w_("PR", c0, nh)), (o, M("N64"), w_("PR", PN + c0, nh))], False)
+        ts(w_("MIX", c0, nh), o, 129.0 * 4160, AL.add)
         for x in range(c0, c0 + nh, MP):
             nodes[lin2(w_("MASK", 16 * x, 16 * MP), ind(s("TBM"), w_("MIX", x, MP)))]["push"] = PUSHM
 
@@ -815,106 +1107,141 @@ def rank_program(g, core, T, topo):
     def pair_tables():
         for j in range(2):
             vp = w_("VAP", 1024 * j, PN)
-            ts(w_("PR", PN * j, PN), vp, 1.0 / 48, AL.mult, 128.5 + 1.0 / 96, AL.add)
-            ts(w_("VAF", PN * j, PN), vp, 1.0 if j else 48.0, AL.mult)
-        lin2(M("I64"), ID, scale=64.0)
+            ts(w_("PR", PN * j, PN), vp, 1.0 / 64, AL.mult, 128.5 + 1.0 / 128, AL.add)
+            ts(w_("VAF", PN * j, PN), vp, 1.0 if j else 64.0, AL.mult)
+        lin2(M("N4096"), ID, scale=-4096.0)
+        lin2(M("N64"), ID, scale=-64.0)
         lin2(col("npar"), col("par"), 1.0, -1.0)
         lin2(col("c2"), col("par"), 1.0)
+        lin2(col("i0"), col("par"), 2.0 ** -8, -2.0 ** -9)
         B = lambda j: w_("BIN", 64 * j, 64)
-        iota(B(0), [[0, 8], [1, 8]], 0, 0)
-        iota(B(1), [[2, 8], [0, 8]], 0, 0)
-        ts(B(2), B(0), 0.0, AL.is_equal, 2.0 ** -8, AL.mult)
-        ts(B(3), B(0), 0.0, AL.is_gt, col("c2"), AL.mult)
-        scan(B(0), B(3), B(2), 0.0, AL.mult, AL.add)
+        iota(B(1), [[0, 8], [2, 8]], 0, 0)
+        ts(B(2), B(1), 0.0, AL.is_equal, col("c2"), AL.mult)
+        ts(B(3), B(2), 1.0, AL.max)
+        scan(B(0), B(3), s("ZERO", 0, 64), col("i0"), AL.mult, AL.add)
         ts(B(1), B(1), col("r2"), AL.is_equal, col("npar"), AL.max)
-        tt(s("TBM", 0, 64), B(0), B(1), AL.mult)
+        tt(B(2), B(0), B(1), AL.mult)
+        ts(s("TF", 144, 152), s("IO", 0, 16, 2), col("r2"), AL.is_equal, col("par"), AL.max)
+        for j in range(8):
+            lin2(w_("TBM", 64 * j, 64), B(2), scale=w_("TF", 144 + j, 1))
         for j, w in enumerate((1.0, 3.0, 15.0)):
             lin2(col("e%d" % j), col("npar"), 1.0, w)
-            lin2(s("TBM", 64 << j, 128 << j), s("TBM", 0, 64 << j), scale=col("e%d" % j))
-        ts(s("TF", 144, 152), s("IO", 0, 16, 2), col("r2"), AL.is_equal, col("par"), AL.max)
-        for j in range(7, -1, -1):
-            lin2(w_("TBM", 512 * j, 512), s("TBM", 0, 512), scale=w_("TF", 144 + j, 1))
+            for x in range(0, 512 << j, 512):
+                lin2(w_("TBM", (512 << j) + x, 512), w_("TBM", x, 512), scale=col("e%d" % j), e=TBE)
 
     def window_tables():
-        lin2(M("N2304"), ID, scale=-2304.0)
-        lin2(M("N48"), ID, scale=-48.0)
+        lin2(M("I48"), ID, scale=48.0)
         lin2(M("NI"), ID, scale=-1.0)
+        for d in range(3):
+            ts(M("BP%d" % d), s("GI"), col("pg%d" % d), AL.is_equal, -2.0 ** 22, AL.mult)
+        for e in range(8):
+            sel(col("bit"), col("bit") if e else col("par"), [[0, 1]], AL.is_gt, 2.0 ** (6 - e), 8 * e, -1)
+        iota(s("RW"), [[0, 24], [1, 8], [0, 2]], 0, 0)
+        ts(s("RW"), s("RW"), col("r8"), AL.not_equal, 2.0 ** 40, AL.mult)
+        sel(s("ZC", 0, 112), s("ZERO", 0, 112), [[1, 112]], AL.not_equal, 1.0, -95, 0)
+        sel(s("ZC", 112, 224), s("ONES", 0, 112), [[2, 56], [1000, 2]], AL.is_ge, 0.0, -1090, 0)
+        sel(s("ZC", 112, 224), s("ZC", 112, 224), [[-1, 112]], AL.is_ge, 0.0, 95, 0)
+        lin2(s("ZC"), s("ZC"), scale=col("bit"))
         ms(s("CUM", 0, 273, 272), 0.0)
-        c0 = sm("SELP", 16)[1][0][1]
+        c0 = sm("SELP", 32)[1][0][1]
         lin2(s("SM", c0, c0 + 16, 2), G8, scale=col("npar"))
         lin2(s("SM", c0 + 1, c0 + 16, 2), G8, scale=col("par"))
+        lin2(s("SM", c0 + 16, c0 + 32), s("SM", c0, c0 + 16), scale=-1.0)
+        for n, top in (("PAIRS", NP), ("PAIR0", NP0)):
+            sel(M(n), O128, [[0, 16], [-1, 8]], AL.is_gt, 0.0, top, 0)
+        if SG:
+            for j in range(SG):
+                col("nc%d" % j)
+            sel(M("LAST"), O128, [[1, 128]], AL.is_ge, 0.0, 16 * SG - 128, 0)
+            iota(col("half"), [[0, 1]], 1, 0)
+            sel(col("half"), col("half"), [[0, 1]], AL.is_gt, 0.5, 128 - 16 * SG, -1)
+        for k, w in enumerate((-256.0, -0.5, -2 * EPS)):
+            sel(M("LOW"), M("LOW") if k else Z128, [[0, 128]], AL.not_equal, w, -k)
         for x in range(0, EW, 480):
             n = min(480, EW - x)
             sel(w_("OHT", x, n), s("CODE", 0, n), [[2, n // 48], [0, 48]], AL.not_equal, 1.0, x // 24, -1)
             sel(w_("OHT", x, n), w_("OHT", x, n), [[0, n // 48], [2, 48]], AL.not_equal, 1.0, 1, -1)
-        sel(s("FT", 0, 112), s("ZERO", 0, 112), [[-1, 112]], AL.not_equal, 128.0, 1, 2)
-        sel(s("FT", 0, 112), s("FT", 0, 112), [[-1, 112]], AL.not_equal, 64.0, -95, 2)
+        sel(s("FT", 0, 112), s("ZERO", 0, 112), [[-2, 56], [1000, 2]], AL.not_equal, 128.0, -1000)
+        sel(s("FT", 0, 112), s("FT", 0, 112), [[-2, 56], [1000, 2]], AL.not_equal, 8.0, -1001)
         for j in range(1, 4):
-            lin2(w_("FT", 112 * j, 112), s("FT", 0, 112), scale=0.25 ** j)
-        terms(sm("S7"), [(7, None, 1)])
-        for t in range(8):
-            fill("LC", 320 * (t // 2) + 64 + 128 * (t & 1), 320 * (t // 2) + 128 + 128 * (t & 1))
+            lin2(w_("FT", 112 * j, 112), s("FT", 0, 112), scale=0.5 ** j)
 
     def lane_numbers():
         mmx([(w_("P1", 16 * i + 8 * h, 8), w_("SR", 128 * h, 128), sm(n)) for h in range(2) for i, n in enumerate(("SELS", "SELC"))])
         lin2(s("SCT"), s("P1", 0, 32))
 
-    for m in range(4):
+    def gather_lanes():
         for j in range(4):
             lin2(w_("GR", 1024 * j, 1024), ind(AW, w_("VARS", 64 * j, 64)))
+
+    for m in range(4):
+        if m - 1 not in QUICK:
+            gather_lanes()
         if m == 0:
-            dma("y", s("A", 0, V, p=row(2)), s("DEW", 0, V, p=row(4)), 49152)
-            dma("y", s("A", 0, V, p=row(3)), s("DEW", 0, V, p=row(5)), 49152)
-            lin2(s("SR"), ind(s("CW"), s("LN", 0, 16)))
+            lin2(s("SR"), ind(s("A", 0, CWD), s("LN", 0, 16)))
+            dma("y", s("A", 0, V, p=row(2)), s("DEW", 0, V, p=row(4)), 49152, rows=16)
+            dma("y", s("A", 0, V, p=row(3)), s("DEW", 0, V, p=row(5)), 49152, rows=16)
+        keys = ("P0", "P2" if LANES else "P0")
         for h in range(2):
-            mmx([(s("P0", 128 * h + k, 128 * h + 128, 16), s("GR", 2048 * h + k, 2048 * h + 2048, 16), s("MAT", mats["SELK"] * 128 + k, mats["SELK"] * 128 + 128, 16)) for k in range(16)])
+            mmx([(s(keys[h], 128 * h + k, 128 * h + 128, 16), s("GR", 2048 * h + k, 2048 * h + 2048, 16), s("MAT", mats["SELK"] * 128 + k, mats["SELK"] * 128 + 128, 16)) for k in range(16)])
         if m == 0:
             lane_numbers()
-        scan(s("M1"), s("RSB"), s("P0", 0, 256), 0.0, AL.add, AL.min)
-        tt(s("YY", 1, 256), s("M1", 0, 255), s("P0", 1, 256), AL.max)
-        cp(s("TI", 0, 16), s("M1", 15, 256, 16))
-        ts(s("OI"), s("TI", 0, 16), 4095, AL.bitwise_and)
-        tt(s("EXP", 0, 256), ind(s("OI"), s("ELX", 0, 16)), s("MASKR", 0, 256), AL.mult)
-        mmx([(w_("P1", 64 + 8 * h, 8), w_("EXP", 128 * h, 128), G8) for h in range(2)])
+        for x0, x1 in (((0, 8), (8, 16)) if LANES else ((0, 16),)):
+            b = keys[x0 // 8]
+            scan(s("M1", 16 * x0, 16 * x1), s("RSB", 16 * x0, 16 * x1), s(b, 16 * x0, 16 * x1), 0.0, AL.add, AL.min)
+            tt(s("YY", 16 * x0 + 1, 16 * x1), s("M1", 16 * x0, 16 * x1 - 1), s(b, 16 * x0 + 1, 16 * x1), AL.max)
+            cp(s("TI", x0, x1), s("M1", 16 * x0 + 15, 16 * x1, 16))
+            ts(s("OI", x0, x1), s("TI", x0, x1), 4095, AL.bitwise_and)
+            tt(s("EXP", 16 * x0, 16 * x1), ind(s("OI", x0, x1), s("ELX", 0, x1 - x0)), s("MASKR", 16 * x0, 16 * x1), AL.mult)
+            mmx([(w_("P1", 64 + 8 * h, 8), w_("EXP", 128 * h, 128), G8) for h in range(x0 // 8, x1 // 8)])
+            cp(s("L1", x0, x1), s("P1", 64 + x0, 64 + x1))
+            if LANES > 1:
+                lin2(s("BE", 16 * x0, 16 * x1), ind(s("BITS"), s("L1", x0, x1)))
+                lin2(s("BO", 16 * x0, 16 * x1), ind(s("BITS"), s("L1", x0, x1)), scale=col("od"))
         LIVE = s("TF", 16, 32)
         tt(LIVE, s("M1", 15, 256, 16), s("SCT", 0, 16), AL.is_lt)
-        cp(s("L1"), s("P1", 64, 80))
-        lin2(s("BE"), ind(s("BITS"), s("L1")), scale=col("ev"))
-        lin2(s("BO"), ind(s("BITS"), s("L1")), scale=col("od"))
+        if LANES < 2:
+            lin2(s("BE"), ind(s("BITS"), s("L1")))
+            lin2(s("BO"), ind(s("BITS"), s("L1")), scale=col("od"))
         if m == 0:
             first_replicas()
         lin2(s("GO"), ind(AW, s("L1")))
 
         def gram(gg, bank, c0, lo):
-            B, pp = ("BE", "BO")[gg & 1], slice(32 * (gg // 2), 32 * (gg // 2) + 32)
+            B, pp = ("BE", "BO")[gg & 1], slice(32 * (gg // 2), 32 * (gg // 2) + (32 if gg & 1 else 16))
             mm(w_(bank, c0, 256 - lo), s(B, lo, lo + 128, p=pp), s(B, lo, 256, p=pp), tile=gg // 2)
+        place = (lambda gg: gg) if BOG else (lambda gg: gg // 2 + 4 * (gg & 1))
         for gg in range(8):
-            gram(gg, "P%d" % (2 + gg // 2), 256 * (gg & 1), 0)
+            gram(gg, "P%d" % (2 + place(gg) // 2), 256 * (place(gg) & 1), 0)
         for gg in range(8):
-            gram(gg, "P0" if gg >= 4 else "P6", 128 * (gg % 4), 128)
+            gram(gg, "P0" if place(gg) >= 4 else "P6", 128 * (place(gg) % 4), 128)
         scan(s("M2"), s("YY"), s("RSB"), 0.0, AL.min, AL.max)
         ts(s("WL", 0, 16), LIVE, col("pow"), AL.mult)
         ts(s("WL", 16, 24), s("TF", 16, 24), 2.0 ** 62, AL.mult)
         tt(s("TI", 16, 32), s("M2", 15, 256, 16), s("SCT", 0, 16), AL.min)
         tt(s("DO"), s("OI"), s("JT", 16, 32), AL.subtract)
-        tt(s("TMP"), ind(s("DO"), s("ELX", 0, 16)), s("MASKR", 0, 256), AL.mult)
+        if not AD:
+            tt(s("TMP"), ind(s("DO"), s("ELX", 0, 16)), s("MASKR", 0, 256), AL.mult)
         ts(s("TI", 32, 48), s("TI", 16, 32), 16, AL.arith_shift_right)
         for j, b in enumerate((2, 3, 4, 5, 6, 0)):
             over(w_("TH", 512 * j, 512), s("P%d" % b), 11.0)
         cp(s("VT", 16, 272, 16), s("TI", 32, 48))
-        th = lambda gg: 256 * gg
-        for g0 in range(0, 8, 2):
-            mmx([(w_("P1", 96 + gg, 1), w_("TH", th(gg), 128), w_("WL", gg, 1)) for gg in (g0, g0 + 1)])
+        th = lambda gg: 256 * place(gg)
         for gg in range(8):
+            mm(w_("P1", 96 + gg, 1), w_("TH", th(gg), 128), w_("WL", gg, 1))
             o1 = w_("P1", 104 + gg, 1)
-            mms([(o1, w_("TH", th(gg) + 128, 128), w_("WL", 16 + gg, 1)), (o1, w_("TH", 2048 + 128 * gg, 128), w_("WL", 8 + gg, 1))])
+            mms([(o1, w_("TH", th(gg) + 128, 128), w_("WL", 16 + gg, 1)), (o1, w_("TH", 2048 + 128 * place(gg), 128), w_("WL", 8 + gg, 1))])
         PV = s("P2", 256, 512)
         mms([(PV, M("SV1"), s("GO")), (PV, M("SV2"), s("SR"))] + [(w_("P2", 256 + 128 * h, 128), w_("VT", 16 - i + 128 * h, 128), ID) for h in range(2) for i in range(2)])
         mm(s("P3", 0, 16), s("IDF"), s("BASEW", 0, 16), True, False)
         tt(s("ACT"), s("P1", 96, 112), s("WL", 0, 16), AL.is_lt)
         VAL = w_("VAL", 256 * m, 256)
         lin2(VAL, PV)
-        tt(s("EXP", 0, 256), ind(s("ACT"), s("ELX", 0, 16)), s("TMP"), AL.mult)
+        if AD:
+            tt(s("DO"), s("DO"), s("ACT"), AL.mult)
+            tt(s("EXP", 0, 256), ind(s("DO"), s("ELX", 0, 16)), s("MASKR", 0, 256), AL.mult)
+        else:
+            tt(s("EXP", 0, 256), ind(s("ACT"), s("ELX", 0, 16)), s("TMP"), AL.mult)
         mms([(w_("P3", 8 * h, 8), w_("EXP", 128 * h, 128), G8) for h in range(2)], False)
         if m < 3:
             mmx([(w_("P2", 8 * h, 8), w_("GO", 128 * h, 128), sm("SELE")) for h in range(2)])
@@ -943,14 +1270,18 @@ def rank_program(g, core, T, topo):
         mms([(s("P1", 160 + lo, 192), s("IDF"), s("BASEW", 16 + lo, 48))] + [(w_("P1", 160 + 8 * h, 8), w_("EXP", 128 * h, 128), G8) for h in range(lo // 8, 4)])
         cp(s("LN", 32 * (m + 1) + lo, 32 * (m + 2)), s("P1", 160 + lo, 192))
         if m < 3:
-            cp(VARS0, ind(s("VA"), w_("LN", 32 * (m + 1), 16)))
-            lin2(s("SR"), ind(s("CW"), w_("LN", 32 * (m + 1), 16)))
+            cp(VARS0, ind(s("VA", 0, C + 16), w_("LN", 32 * (m + 1), 16)))
+            lin2(s("SR"), ind(s("A", 0, CWD), w_("LN", 32 * (m + 1), 16)))
             lane_numbers()
         cp(ind(s("OW"), w_("LN", 32 * (m + 1) + 16, 16)), VAL)
         LA = lambda d: w_("LA", 192 * (m + 1) + S * d, S)
         mms([(w_("P4", S * d, S), M("PK%d" % d), LA(d)) for d in range(3)], False)
         mms([(w_("P5", S * d, S), M("PD%d" % d), LA(d)) for d in range(3)], False)
         TTm = w_("TT", 192 * m, 192)
+        if m in QUICK:
+            mmx([(w_("P6", S * d, S), M("PD%d" % d), LA(d)) for d in range(3)])
+            tt(AREP, s("P6", 0, 192), AREP, AL.max)
+            gather_lanes()
         ts(s("LS"), s("P4", 0, 192), 0.0, AL.is_gt)
         tt(TTm, s("P5", 0, 192), s("LS"), AL.mult)
         tt(AREP, s("P5", 256, 448), TTm, AL.add)
@@ -962,9 +1293,8 @@ def rank_program(g, core, T, topo):
                 x["push"] = PUSHT
             window_tables()
         gap_work(GAPS[m])
-    mmx([(w_("P7", 8 * d, 8), M("PI%d" % d), sm("G8B")) for d in range(3)])
-    lin2(sm("G8P", 24), s("P7", 0, 24))
     dma("y", s("CH1", 0, H), s("CH0", 0, H), 256 * H, after=[lands[3]])
+    dma("y", s("CW"), s("CH0", 0, CWD), 256 * CWD, after=[lands[3]])
     fill("CH1", H, VW)
     for j in range(6):
         b, o = s("P6" if j & 1 else "P7", 0, 480), w_("X", 480 * j, 480)
@@ -972,14 +1302,15 @@ def rank_program(g, core, T, topo):
         lin2(o, b)
 
     def changed_digits(lst, n):
-        b, o = lst[0][0], s("T192", 0, 192)
-        mms([(b, ID, s("CODE", H, V))] + lst)
+        b, o = s("P6", 0, 192), s("T192", 0, 192)
+        mms([(b, ID, s("CODE", H, V))] + lst[:3 * (len(lst) > 3)], True, False)
+        mms(lst[3 * (len(lst) > 3):], False)
         node({"s": (cost(o, [b], 1) + 0.02, lambda: g.scalar.activation(o[0], b[0], AF.Relu, accum_out=col(n)[0]))}, [o, col(n)], [b])
 
     def mask_test(c0, n, wc, src=None):
         ts(s("MT", 0, n), src or w_("MK", c0, n), col(wc), AL.subtract, float(0x555555), AL.add)
-        ts(w_("MT", 512, n), s("MT", 0, n), 0xAAAAAA, AL.bitwise_and)
-        ts(w_("MB", c0, n), w_("MT", 512, n), 0.0, AL.is_gt)
+        ts(w_("MT", 384, n), s("MT", 0, n), 0xAAAAAA, AL.bitwise_and)
+        ts(w_("MB", c0, n), w_("MT", 384, n), 0.0, AL.is_gt)
 
     def piece(win, q, slot, e):
         n = 128 // len(e)
@@ -987,20 +1318,37 @@ def rank_program(g, core, T, topo):
             lin2(w_("GR", 2048 * slot + 16 * x, 16 * n), ind(win, w_("VAP", 128 * q + x, n)), e={"b": "sv"}.get(eng, eng))
 
     P96 = slice(0, 96)
-    marks = lambda b: s("P1", 64 * (b % 4) + b // 4, 64 * (b % 4) + 64, 8, p=P96)
+    P64 = slice(0, 64)
+    EL = 45 * 48
 
-    def signs(lo, hi, step=1):
-        o, i = s("BIN", lo, hi, step, p=P96), s("P1", lo, hi, step, p=P96)
+    def pair_window(ch):
+        for h in range(2):
+            mmx([(s("P1", 64 * (r // 8) + r % 8, 64 * (r // 8) + 64, 8, p=P96), s(ch, r, V, 32), sm("G8B")) for r in range(16 * h, 16 * h + 16)])
+        o, i = s("BIN", p=P96), s("P1", 0, 256, p=P96)
         node({"s": act_(o, i, AF.Sign), "v": ts_(o, i, 0.0, AL.is_gt)}, [o], [i])
-
-    def pair_window(EB=EB):
         for h in range(2):
             mms([(s("P1", 256 + h, 384, 2, p=P96), s("FT", 112 * j + 1 - h, 112 * j + 97 - h, p=P96), s("BIN", 64 * j, 64 * j + 64, p=P96)) for j in range(4)])
         lin2(s("WT", p=P96), s("P1", 256, 384, p=P96))
-        for x in range(0, EW, 480):
-            n, b = min(480, EW - x), EB[x // 480]
-            mm(s(b, 0, n), s("WT", p=P96), s("OHT", x, x + n, p=P96))
-            nodes[lin2(w_("E", x, n), s(b, 0, n), e=EQ[x // 480])]["push"] = PUSHE
+        n = (EW if PE0 else EL) // len(EB) + 1
+        for j, x in enumerate(range(0, EW if PE0 else EL, n)):
+            y = min(n, (EW if PE0 else EL) - x)
+            mm(s(EB[j], 0, y), s("WT", p=P96), s("OHT", x, x + y, p=P96))
+            nodes[lin2(w_("E", x, y), s(EB[j], 0, y), e=EQ[j])]["push"] = PUSHE
+
+    def pair_patch(own, bm, b0, b1):
+        k0 = len(nodes)
+        act(s("BX", p=P64), s(bm, 0, 384, p=P64), AF.Sign, -1.0, -1.0)
+        for h in range(2):
+            mms([(s(bm, 384 + h, 512, 2, p=P96), s("ZC", 5 - 2 * d - h, 101 - 2 * d - h, p=P64), s("BX", 128 * d + h, 128 * d + 128, 2, p=P64)) for d in range(3)]
+                + [(s(bm, 384 + h, 512, 2, p=P96), s("ZC", 113 - h, 209 - h, p=P64), s("ONES", 0, 64, p=P64))])
+        lin2(s("WR", p=P96), s(bm, 384, 512, p=P96), e=EP[0])
+        cut = [(b0, 0, 144, EL, EW, 1), (b0, 144, 189, 45, EL, 48), (b1, 0, 45, 46, EL, 48), (b1, 45, 90, 47, EL, 48)]
+        for b, x0, x1, lo, hi, st in cut:
+            mms([(s(b, x0, x1), s(w, p=P96), s("OHT", lo, hi, st, p=P96)) for w in ("WT", "WR")[1 - own:]])
+        for n, (b, x0, x1, lo, hi, st) in enumerate(cut):
+            lin2(s("E", lo, hi, st), s(b, x0, x1), e=EP[1 + n])
+        for x in nodes[k0:]:
+            x["push"] = PUSHE
 
     def pair_gather(b, calls):
         n = 128 // calls
@@ -1008,62 +1356,77 @@ def rank_program(g, core, T, topo):
             k = tt(w_("GR", 2048 * (NS + b) + 16 * x, 16 * n), ind(s("E"), w_("PIX", 128 * b + x, n)), w_("MASK", 2048 * b + 16 * x, 16 * n), AL.mult)
             nodes[k]["push"] = PUSHP
 
-    def pair_flags(b, lst, last, ZB=ZB, **kw):
-        z, g0, r0 = s(ZB[b % len(ZB)], 0, 256), 2048 * (NS + b), 512 * (b & 1)
-        mmx([(s(z[1][0][0], k, 256, 16), s("GR", g0 + k, g0 + 2048, 16), sm("SELP", 16)) for k in range(16)])
-        lin2(w_("RR", r0, 256), z, 128.0 + EPS)
-        lin2(w_("RR", r0 + 256, 256), z, -128.5 - EPS, -1.0)
+    def add(sums, lst, **kw):
+        c = sum(max(min(64, l[3]), r[3]) for (o, l, r) in lst) * PECY
+        sums.append(node({"p": (c, [(o, l, r, False, False, None) for (o, l, r) in lst])}, [], [x[1] for x in lst] + [x[2] for x in lst],
+                         inc=len(lst), after=sums[:1], **kw))
+
+    def pair_flags(b, sums, last, ZB=ZB, **kw):
+        z, g0, r0 = ZB[b % len(ZB)], 2048 * (NS + b), 512 * (b & 1)
+        if RRC:
+            mms([(s(z, 0, 256), Z128, s("ONES")), (s(z, 256, 512), M("LOW"), s("ONES"))], True, False)
+            mms([(s(z, k, 512, 16), s("GR", g0 + k, g0 + 2048, 16), sm("SELP", 32)) for k in range(16)], False)
+            lin2(w_("RR", r0, 512), s(z), 128.0 + EPS)
+        else:
+            mmx([(s(z, k, 256, 16), s("GR", g0 + k, g0 + 2048, 16), w_("SM", sm("SELP", 32)[1][0][1], 16)) for k in range(16)])
+            lin2(w_("RR", r0, 256), s(z, 0, 256), 128.0 + EPS, e=RRE[0])
+            lin2(w_("RR", r0 + 256, 256), s(z, 0, 256), -128.5 - EPS, -1.0, e=RRE[1])
         o = s("P0", b, 128, 8)
         if last:
             c0 = 272 * (b & 1)
             scan(w_("CUM", c0 + 1, 256), w_("RR", r0, 256), w_("RR", r0 + 256, 256), 0.0, AL.add, AL.add)
-            lst = lst + [(o, ID, s("CUM", c0 + 16, c0 + 257, 16)), (o, M("NI"), s("CUM", c0, c0 + 256, 16))]
+            add(sums, [(o, ID, s("CUM", c0 + 16, c0 + 257, 16)), (o, M("NI"), s("CUM", c0, c0 + 256, 16))], **kw)
         else:
-            lst = lst + [(o, ID, s("RR", r0 + 256 * h + k, r0 + 256 * h + 256, 16)) for h in range(2) for k in range(16)]
-        mms([(o, M("ID16"), s("ONES", 0, 16))] + lst, **kw)
+            for h in range(2):
+                add(sums, [(o, ID, s("RR", r0 + 256 * h + k, r0 + 256 * h + 256, 16)) for k in range(16)], **kw)
 
     changed_digits([(s("P6", 0, 192), M("BU22"), w_("SQ", 192 * m, 192)) for m in range(4)], "wd")
-    mms([(s("P1", 0, 256, p=P96), s("ZERO", 0, 96), s("ZERO"))] + [(marks(30 + j), w_("SQ", 192 * m + 96 * j, 96), sm("S7")) for m in range(4) for j in range(2)])
-    signs(0, 256)
+    others = lambda b: mm(s(b, 0, 384, p=P64), s("ZW", 16, 80, p=P64), s("RW", p=P64), True, False)
+    others("P2")
+    for ms_ in ((0, 1, 2), (3,)):
+        mms([(s("P2", 128 * d, 128 * d + 128, p=P64), w_("SQ", 192 * m + S * d, S), M("BU22")) for m in ms_ for d in range(3)], False, 3 in ms_)
     if NP0 < NP:
         mms([(s("P3", 256, 448), M("SU"), w_("SQ", 192 * m, 192)) for m in range(4)])
         lin2(s("CH0", H, V), s("P3", 256, 448))
-    pair_window(("P2", "P3", "P1", "P2", "P3"))
-    for c0 in range(0, 128 * NS, 384):
-        mask_test(c0, min(384, 128 * NS - c0), "wd")
-    rest = [(b + 8 * h, (NS + b, NS - 1 - b + NP0)[h]) for b in range(NP0, NP) for h in range(2)]
+    pair_patch(0, "P2", "P1", "P4")
+    for c0 in range(0, 128 * ND, 384):
+        mask_test(c0, min(384, 128 * ND - c0), "wd")
+    rest = [(b + 8 * h, (NS + b, NS + NP1 + b - NP0 if NP1 < NP else NS - 1 - b + NP0)[h]) for b in range(NP0, NP1) for h in range(2)]
     for q, slot in rest:
         piece(s("CH0"), q, slot, "bb")
     if rest:
         lin2(s("CH0", H, V), s("ZERO", 0, 192))
     for b in range(NP0):
         pair_gather(b, 2)
-    first_term = lambda q: (s("P0", q, 128, 16), s("OW", q, C, 16), sm("SF"))
-    for i, q in enumerate(SINGLE):
-        mms([first_term(q), (s("P0", q, 128, 16), w_("MB", 128 * i, 128), sm("G8B"))])
-    for n in range(max(NP0, len(rest))):
-        if n < len(rest):
-            q, slot = rest[n]
-            mms([first_term(q)] + [(s("P0", q, 128, 16), s("GR", 2048 * slot + k, 2048 * slot + 2048, 16), sm("S8")) for k in range(16)])
-        if n < NP0:
-            pair_flags(n, [first_term(n), first_term(n + 8)], n == NP0 - 1, ("P1", "P2"))
+    sums = [mm(s("P0", 0, 128), M("ID16"), M("PAIR0"), True, False)]
+    for h in range(2):
+        add(sums, [(s("P0", q, 128, 16), s("OW", q, C, 16), sm("SF")) for q in range(8 * h, 8 * h + 8)])
+    for i0 in range(0, ND, 3):
+        add(sums, [(s("P0", DIG[i], 128, 16), w_("MB", 128 * i, 128), sm("G8B")) for i in range(i0, min(ND, i0 + 3))])
+    for q, slot in rest:
+        add(sums, [(s("P0", q, 128, 16), s("GR", 2048 * slot + k, 2048 * slot + 2048, 16), sm("S8")) for k in range(16)])
+    for n in range(NP0):
+        pair_flags(n, sums, n >= NP0 - SCAN0, ("P1", "P2"))
+    mms([(s("P0", 0, 16), Z128, s("ZERO", 0, 16))], False, True, after=sums)
     mms([(s("P4", 0, 128), slide(1, r), s("OW", r, C, 16)) for r in range(16)])
     ts(s("LO128"), s("P4", 0, 128), float(C), AL.add)
     for j in range(4):
         lin2(w_("GV", 512 * j, 512), ind(AW, w_("LO128", 32 * j, 32)))
         b, o = s("P4" if j & 1 else "P5"), w_("CW2", 512 * j, 512)
-        mms([(b, M("NBO"), w_("CW", 512 * j, 512)), (b, M("MO"), w_("OW", 512 * j, 512)), (b, M("BDE"), w_("GV", 512 * j, 512))])
+        mms([(b, M("NBO"), w_("A", 512 * j, 512)), (b, M("MO"), w_("OW", 512 * j, 512)), (b, M("BDE"), w_("GV", 512 * j, 512))])
         node({"s": act_(o, b, AF.Relu), "v": ts_(o, b, 0.0, AL.max)}, [o], [b])
     mms([(s("P7", 256, 384), slide(3, r), w_("CW2", 128 * r, 128)) for r in range(16)])
     ts(s("FF", 128, 256), s("P7", 256, 384), float(V), AL.add, float(V), AL.min)
     dma("y", ext(T.yo[:]), s("FF", 128, 256), 65536)
-    mm(s("P6", 256, 448), M("BU"), AREP)
-    for d in range(3):
-        ts(w_("T192", S * d, S), w_("P6", 256 + S * d, S), 1.0 if high[d] else 2.0, AL.is_equal)
-    ts(s("T192", 192, 384), s("P6", 256, 448), 0.0, AL.is_equal, STALE, AL.mult)
-    tt(s("T192", 0, 192), s("T192", 0, 192), s("DX"), AL.mult)
-    tt(s("T192", 0, 192), s("T192", 0, 192), s("XR0"), AL.add)
-    tt(XREP, s("T192", 0, 192), s("T192", 192, 384), AL.max)
+    mms([(w_("P6", S * d, S), M("BH" if high[d] else "BL"), w_("A", H + S * d, S)) for d in range(3)] + [(s("P6", 256, 448), M("STL"), AREP)],
+        after=writers(M("BH"), M("BL")))
+    o, i = s("NE"), s("P6", 0, 192)
+    node({"s": act_(o, i, AF.Relu), "v": ts_(o, i, 0.0, AL.max)}, [o], [i])
+    o, i = s("BX", 0, 192), s("P6", 256, 448)
+    node({"s": act_(o, i, AF.Relu), "v": ts_(o, i, 0.0, AL.max)}, [o], [i])
+    tt(s("NE"), s("NE"), s("DX"), AL.mult)
+    mms([(s("P6", 0, 192), ID, s(n, 0, 192)) for n in ("XR0", "NE", "BX")])
+    lin2(XREP, s("P6", 0, 192))
     lin2(s("GM"), s("LS"), 1.0, -1.0)
     GM = s("P2", 256, 448)
     mm(GM, ID, s("GM"))
@@ -1095,8 +1458,8 @@ def rank_program(g, core, T, topo):
         tt(SBA, AREP, GM, AL.mult)
 
     def take_w(base, w):
-        mmx([(w_("P7", 16 + S * d, S), M("PI%d" % d), w_("LP", base + w * d, S)) for d in range(3)])
-        tt(AREP, s("P7", 16, 208), SBA, AL.add)
+        mms([(w_("P7", 16 + S * d, S), ID, part(d, 1, 2)) for d in range(3)] + [(w_("P7", 16 + S * d, S), M("PI%d" % d), w_("LP", base + w * d, S)) for d in range(3)])
+        lin2(AREP, s("P7", 16, 208))
 
     for t in range(4):
         u = t & 1
@@ -1106,12 +1469,25 @@ def rank_program(g, core, T, topo):
         mm(s("P1", 0, 8), M("TRI%d" % t), s("IP", 15, 128, 16))
         lin2(s("CR"), ind(s("IP"), s("ELX", 32, 40)))
         mms([(s("P2", 0, 128), s("F"), M("PM4%d" % t)), (s("P2", 0, 128), s("IP"), M("PM%d" % t)), (s("P2", 0, 128), s("CR"), M("TRS%d" % t))])
+        if SG:
+            mm(s("P4", 256, 256 + SG), M("TRI%d" % t), s("IP", 143 - 16 * SG, 128, 16))
+            lin2(w_("CF", cols["nc0"], SG), s("P4", 256, 256 + SG), 0.5, -1.0, e="s")
+            mm(s("P3", 0, 32), M("LAST"), w_("RH", 32 * t, 32), True, False)
         for gg in range(8):
-            ts(w_("CMP", 256 * gg, 256), s("JI"), w_("P1", gg, 1), AL.is_ge)
+            if gg < 8 - SG:
+                ts(w_("CMP", 256 * gg, 256), s("JI"), w_("P1", gg, 1), AL.is_ge)
+            else:
+                act(w_("CMP", 256 * gg, 256), s("JI"), AF.Sign, col("nc%d" % (gg - 8 + SG)))
         lin2(s("POS", 0, 128), s("P2", 0, 128), -4096.0)
-        mmx([(s("P3", j, 32, 16), s("CMP", j, 2048, 16), s("RH", 32 * t + j, 32 * t + 32, 16)) for j in range(16)])
-        cp(s("LB"), s("P3", 0, 16))
-        lin2(s("BC"), s("P3", 16, 32), float(40 * t))
+        lst = [(s("P3", j, 32, 16), s("CMP", j, 2048, 16), s("RH", 32 * t + j, 32 * t + 32, 16)) for j in range(16)]
+        if SG:
+            mms(lst, False)
+            ts(s("LB"), s("P3", 0, 16), col("half"), AL.mult)
+            lin2(s("BC"), s("P3", 16, 32), float(40 * t), col("half"))
+        else:
+            mmx(lst)
+            cp(s("LB"), s("P3", 0, 16))
+            lin2(s("BC"), s("P3", 16, 32), float(40 * t))
         tt(s("OH"), ind(s("POS"), s("LB")), s("J1"), AL.is_equal)
         mms([(s("P1", 16, 32), slide(2, r), s("OH", r, 256, 16)) for r in range(16)] + [(s("P1", 16, 32), M("ID16"), s("BC"))])
         CL, LO, LOD, PS = s("CL"), s("LO", 0, 16), w_("LO", 16 + 16 * u, 16), s("P4", 0, 256)
@@ -1126,23 +1502,26 @@ def rank_program(g, core, T, topo):
         lin2(s("XO"), ind(XW_, LO), scale=1.0 / 256)
         for j, n in zip(XP[:-1], XP[1:]):
             lin2(s("GR", 16 * j, 16 * n), ind(XW_, s("VARS", c0 + j, c0 + n)))
-        for j in range(4):
-            mms([(w_("P4", 64 * j, 64), M("NID"), s("GR", 1024 * j + k, 1024 * j + 1024, 16)) for k in range(16)], j == 0, j == 3)
-            if j == 2:
-                mms([(s("P4", lo, hi), l, s(b, o + lo, o + hi)) for lo, hi in ((0, 192), (192, 256))
-                     for l, b, o in ((M("BNH"), "CG", c0), (M("IDS"), "KR", 0), (ID, "XO", 0))], False, False)
-        ts(s("FL"), PS, -0.498, AL.add)
-        tt(s("NX"), PS, s("FL"), AL.subtract)
-        GG, GS = s("GG"), s("GS")
-        node({"s": act_(GG, PS, AF.Relu, 640.0), "v": ts_(GG, PS, -640.0, AL.is_ge)}, [GG], [PS])
-        act(GS, PS, AF.Sign, 640.0)
+        GS = s("GS")
         mm(s("P2", 0, 256), ID, s("XO"))
-        tt(s("NEQ"), s("P2", 0, 256), s("NX"), AL.not_equal)
-        tt(ind(CH, LO), s("NEQ"), GG, AL.mult)
-        send([w_("CH%d" % u, H + S * d, S) for d in range(3)], "LC", 320 * t, S, gap=S)
+        for bank, x0, x1 in ((("P6", 0, 128), ("P4", 128, 256)) if HALVES else (("P4", 0, 256),)):
+            for x in range(x0, x1, 64):
+                if x == x1 - 64:
+                    mms([(s(bank, lo, hi), l, s(b, o + lo, o + hi)) for lo, hi in ((x0, x), (x, x1))
+                         for l, b, o in ((M("BNH"), "CG", c0), (M("IDS"), "KR", 0), (ID, "XO", 0))], False, False)
+                mms([(w_(bank, x, 64), M("NID"), s("GR", 16 * x + k, 16 * x + 1024, 16)) for k in range(16)], x == x0, x == x1 - 64)
+            PS, GG = s(bank, x0, x1), s("GG", x0, x1)
+            ts(s("FL", x0, x1), PS, -0.498, AL.add)
+            tt(s("NX", x0, x1), PS, s("FL", x0, x1), AL.subtract)
+            node({"s": act_(GG, PS, AF.Relu, 640.0), "v": ts_(GG, PS, -640.0, AL.is_ge)}, [GG], [PS])
+            act(s("GS", x0, x1), PS, AF.Sign, 640.0)
+            tt(s("NEQ", x0, x1), s("P2", x0, x1), s("NX", x0, x1), AL.not_equal)
+            tt(ind(CH, s("LO", x0 // 16, x1 // 16)), s("NEQ", x0, x1), GG, AL.mult)
+        send([w_("CH%d" % u, H + S * d, S) for d in range(3)], "LC", 192 * t, S)
         DOWN = ("OW", "CW")[u]
         cp(ind(s(DOWN), CL), GS)
-        mms([(s("P3", 48, 64), slide(3, r), s("CG", c0 + r, c0 + 256, 16)) for r in range(16)] + [(s("P3", 48, 64), slide(4, r), s("GS", r, 256, 16)) for r in range(16)])
+        mms([(s("P3", 48, 64), s("IDF"), s("TF", 0, 16))], True, False)
+        mms([(s("P3", 48, 64), slide(4, r), s("GS", r, 256, 16)) for r in range(16)], False)
         tt(s("TF", 48, 64), s("P3", 48, 64), s("BASEW", 64, 80), AL.min)
         if t:
             strengths(t - 1)
@@ -1155,37 +1534,42 @@ def rank_program(g, core, T, topo):
             send([part(d, 0, 1) for d in range(3)], "LP", 0, S, XW_X)
         nodes[sends[-1]]["push"] = PUSHX
         left = lambda j: (32 - j) * 0.5 * 1024 * GATHER * CY
+        pair_window("CH%d" % u)
+        k0 = len(nodes)
         for i in range(EARLY):
             piece(CH, SINGLE[i], i, SCALLS[i])
-        mmx([(marks(b), w_("CH%d" % u, 96 * b, 96), sm("G8B")) for b in range(30)])
-        signs(0, 256)
-        far = lambda d, c0: (w_("LC", 320 * t + c0, 96), w_("SM", sm("G8P", 24)[1][0][1] + 8 * d, 8))
-        mms([(marks(30), w_("CH%d" % u, H, 96), sm("G8B")), (marks(30), *far(0, 0)), (marks(30), *far(1, 64))])
-        mms([(marks(31), w_("CH%d" % u, H + 96, 96), sm("G8B")), (marks(31), *far(1, 160)), (marks(31), *far(2, 224))])
-        signs(135, 256, 8)
-        mmx([(w_("P6", S * d, S), M("PI%d" % d), w_("LC", 320 * t + 2 * S * d, S)) for d in range(3)])
-        tt(CHREP, s("P6", 0, 192), CHREP, AL.add)
-        pair_window()
-        if EARLY:
-            changed_digits([(s("P6", 0, 192), M("BD22"), CHREP)], "wd")
-            mask_test(0, 128 * EARLY, "wd")
+        for k in range(k0 + HOLD[0], len(nodes)):
+            nodes[k]["pred"].add(k0 - HOLD[1])
+        if PE0:
+            pair_gather(NP - 1, PCALLS[t == 3][NP - 1])
+        LC = lambda d: w_("LC", 192 * t + S * d, S)
+        others("P6")
+        mms([(s("P6", 128 * d, 128 * d + 128, p=P64), LC(d), M("BP%d" % d)) for d in range(3)], False)
+        pair_patch(1, "P6", "P3", "P4")
+        mms([(s("P2", 0, 192), ID, CHREP)] + [(w_("P2", S * d, S), M("PI%d" % d), LC(d)) for d in range(3)])
+        lin2(CHREP, s("P2", 0, 192))
+        if EARLY or PE0:
+            changed_digits([(w_("P6", S * d, S), M("BP%d" % d), LC(d)) for d in range(3)], "wd")
+            d0, d1 = ND - NS - 2 * PE0, ND - NS + EARLY
+            mask_test(128 * d0, 128 * (d1 - d0), "wd")
         for i in range(EARLY, NS):
             piece(CH, SINGLE[i], i, SCALLS[i])
-        for b in range(NP):
+        for b in range(NP - PE0):
             pair_gather(b, PCALLS[t == 3][b])
-        down = lambda q: (s("P0", q, 128, 16), s(DOWN, q, C, 16), sm("SN"))
+        sums = [mms([(s("P0", 0, 128), ID, s("F")), (s("P0", 0, 128), M("ID16"), M("PAIRS"))], True, False)]
+        for h in range(2):
+            add(sums, [(s("P0", q, 128, 16), s(DOWN, q, C, 16), sm("SN")) for q in range(8 * h, 8 * h + 8)])
+        add(sums, [(s("P0", DIG[i], 128, 16), w_("MB", 128 * i, 128), sm("G8B")) for i in range(d0, d1)])
         for n, (kind, i) in enumerate(zip(SUMS[::2], map(int, SUMS[1::2]))):
             extra = FX * left(32 * (n + 1) // (NS + NP))
             if kind == "p":
-                pair_flags(i, [(s("P0", i, 128, 8), ID, s("F", i, 128, 8)), down(i), down(i + 8)], i >= NP - SCANS, extra=extra)
+                pair_flags(i, sums, i >= NP - SCANS, extra=extra)
             else:
-                q = SINGLE[i]
-                o = s("P0", q, 128, 16)
-                mms([(o, ID, s("F", q, 128, 16)), down(q)] + ([(o, w_("MB", 128 * i, 128), sm("G8B"))] if i < EARLY else [])
-                    + [(o, s("GR", 2048 * i + k, 2048 * i + 2048, 16), sm("G8B")) for k in range(16)], extra=extra)
+                add(sums, [(s("P0", SINGLE[i], 128, 16), s("GR", 2048 * i + k, 2048 * i + 2048, 16), sm("G8B")) for k in range(16)], extra=extra)
+        mms([(s("P0", 0, 16), Z128, s("ZERO", 0, 16))], False, True, after=sums)
         wx = 128 if t else S
-        mmx([(w_("P6", S * d, S), M("PI%d" % d), w_("LP", 384 * t + wx * d, S)) for d in range(3)])
-        tt(XREP, s("P6", 0, 192), SBX, AL.add)
+        mms([(w_("P6", S * d, S), ID, part(d, 0, 1)) for d in range(3)] + [(w_("P6", S * d, S), M("PI%d" % d), w_("LP", 384 * t + wx * d, S)) for d in range(3)])
+        lin2(XREP, s("P6", 0, 192))
         if t:
             take_w(384 * t + S, 128)
         if t < 2:

from concourse.bass import DstId, RemoteDMATransfer
from concourse.mybir import AluOpType as AL, AxisListType as AX, ActivationFunctionType as AF

V, C, S, N = 3072, 2048, 64, 4
H = V - 3 * S
NV, DV0, VW, CWD = 3072, 3088, 3344, 2304
STALE = 65536.0
BIG = 3.0e7
ALL = (1 << 128) - 1
B16, F32, I32, U16 = "bfloat16", "float32", "int32", "uint16"
NP = 5
NP0 = 3
PN, EW = 128 * NP, 48 * 48
SINGLE = [q for q in range(16) if q % 8 >= NP]
NS = len(SINGLE)
NP1 = 4
DIG = [q for q in range(16) if NP1 <= q % 8 < NP] + SINGLE
PE0 = 0
ND = len(DIG)
LN2 = 0.6931471805599453
EPS = 2.0 ** -10
MP = 32
EARLY = 1
_sb = {
    "VA": (CWD, I32), "VAP": (C, U16), "A": (VW, B16), "X": (VW, B16), "KK": (CWD, B16), "CW": (CWD, B16), "CW2": (CWD, B16), "OW": (CWD, B16),
    "CH0": (VW, B16), "CH1": (VW, B16), "GR": (32768, B16), "GW": (4096, B16), "CODE": (V, B16), "MK": (128 * ND + 2 * PN, F32), "MB": (128 * ND, B16), "MT": (768, I32), "EQ": (256, B16),
    "IO": (256, F32), "ZERO": (256, B16), "GI": (128, F32), "JI": (256, B16), "J1": (256, F32), "II": (128, I32), "CF": (160, F32), "IC": (16, F32),
    "JW": (128, F32), "TMP": (256, F32), "TMP2": (256, F32), "MAT": (58 * 128, B16), "PIT": (160, B16), "SM": (128, B16), "ZW": (6 * 160, B16), "IDF": (128, F32), "G8": (8, F32),
    "MASKR": (512, F32), "RSB": (256, F32), "RS1": (128, B16), "ELX": (48, U16), "BASEW": (80, F32), "JT": (32, F32),
    "OVI": (128, I32), "OV2": (384, I32), "OVL": (128, U16), "OVB": (256, B16), "WI": (192, I32), "WB": (192, B16), "SI": (128, I32), "SBF": (128, B16), "NLI": (16, I32),
    "LN": (32 * 5, U16), "VARS": (512, U16), "SR": (256, B16), "M1": (256, F32), "YY": (256, F32), "M2": (256, F32),
    "TI": (64, I32), "OI": (16, I32), "TF": (256, F32), "SCT": (32, F32), "ACT": (16, F32), "NM": (32, F32), "DO": (16, F32), "EXP": (512, F32),
    "L1": (16, U16), "L2": (64, U16), "BE": (256, B16), "BO": (256, B16), "GO": (256, B16), "WL": (32, B16), "VT": (272, B16), "VAL": (1024, B16), "YW": (192, F32),
    "ONES": (256, B16), "LA": (192 * 5, B16), "LS": (192, B16), "TT": (192 * 4, B16), "SQ": (192 * 4, B16), "XR0": (192, B16), "DX": (192, B16), "NE": (192, B16), "GM": (192, B16),
    "T192": (384, F32), "LO128": (128, U16), "LC": (192 * 4, B16), "RW": (384, B16), "BX": (384, B16), "WR": (128, B16), "ZC": (224, B16), "LP": (384 * 5, B16),
    "F": (128, B16), "FF": (256, F32), "IP": (128, B16), "CR": (128, B16), "CMP": (2048, B16), "POS": (144, F32), "LB": (16, U16), "BC": (16, B16), "OH": (256, B16), "CL": (16, U16),
    "CG": (512, B16), "KR": (256, B16), "XO": (256, B16), "LO": (48, U16), "FL": (256, I32), "GG": (256, B16), "NX": (256, B16),
    "NEQ": (256, B16), "T1": (256, B16), "RH": (128, B16), "C256": (256, B16), "GS": (256, B16),
    "OHT": (EW, B16), "PIX": (PN, U16), "BIN": (256, B16), "FT": (4 * 112, B16), "WT": (128, B16), "RR": (1024, B16), "CUM": (544, B16), "MIX": (PN, U16),
}
SCRATCH = {k: ("sbuf", [128, w], d) for k, (w, d) in _sb.items()}
SCRATCH["SB"] = ("sbuf", [128, 3, 128], B16)
for _i in range(8):
    SCRATCH["P%d" % _i] = ("psum", [128, 512], F32)
SEMAPHORES = ["cv", "cs", "cp", "cg"] + ["d%d" % i for i in range(56)] + ["ar%d" % i for i in range(14)] + ["ls%d" % i for i in range(14)]
ALIAS = {"TH": ("GR", 4096, 3072), "DEW": ("GR", 8192, DV0 + C), "DVAL": ("GR", 13568, C), "GV": ("GR", C, C), "YB": ("CH0", 0, V),
         "BITS": ("CH1", 0, DV0), "MASK": ("GR", 32768 - 16 * PN, 16 * PN), "TBM": ("GR", 8192, 4096), "E": ("CODE", 0, EW),
         "PR": ("GW", 0, 2 * PN), "VAF": ("MK", 128 * ND, 2 * PN)}
CY, PECY, GATHER, SCATTER, FIX, WAKE = 0.00088, 0.00044, 1.2, 3.0, 0.05, 0.1
VPEN = (0.3, 0.5)
RATES = ((1.55, 3.6), (1.15, 5.0), (2.0, 2.5), (2.0, 5.5), (1.15, 2.0))
XW_X = 42.0
VAP_X = 50.0
FX = 0.8
ROUNDS = 3
WP = 32
DMA0, DMABW, ROWS = 1.5, 250e3, 0.4
REMOTE = 3.2
FIRST = 3.5
MARGIN = 3.0
GSLACK = 1.15
PUSHY = 5.0
DEAR = 1.5
W3 = "sv"
PUSH = 8.0
PUSHX = 14.0
CWDMA = 1
XP = (0, 32, 64, 96, 128, 160, 192, 224, 256)
SHAKE = 0.0
PLAN = []
SFIX = 0.015
POLISH = ((1.5, 3.6, 1.0, 1.6, 1.0, 0.62), (1.1, 2.5, 1.4, 2.2, 1.0, 0.62), (1.15, 4.5, 1.1, 1.4, 1.1, 0.62), (1.35, 3.0, 1.2, 2.6, 1.0, 0.62))
START = 0
TRIES, HEAT = 24000, 0.005
SWEEPS = ((60, 600), (60, 600), (100, 800), (160, 1000, 450), (100, 800)) * 2 + ((140, 600), (140, 600), (80, 500), (80, 500), (120, 600), (120, 600), (80, 400))
NEAR = 0.5
COOL = 7
LOG = []
DEBUG = []
MOVES = 12
OWN_X, PUSHO = 12.0, 6.0
VAW = 1024
EB = ("P3", "P4", "P1", "P3", "P4")
EQ = ("sv",) * 5
EP = ("sv",) * 5
ZB = ("P1", "P3", "P4")
GAPS = ("dmdd", "xddd", "dxdm", "")
SCAN0 = 1
TWO = (0, 1, 2, 3, 4, 5, 7, 9, 11)
BOG = 1
QUICK = (1, 2)
HALVES = 1
LANES = 0
AD, TBE = 0, "sv"
SG = 2
HOLD = (9, 1)
RRC, RRE = 1, ("sv", "sv")
SCANS = 2
PUSHE = 3.0
PUSHT, PUSHM, PUSHP = 10.0, 0.0, 0.0
SCALLS = ("ssss", "s", "s", "s", "ss", "bbbb")
PCALLS = ((1, 1, 1, 1, 2), (1, 1, 2, 2, 2))
SUMS = "s0s1s2p0s3p1p2s4p3p4s5"


def rank_program(g, core, T, topo):
    rank = T.rank_of(core)
    if rank is None:
        return
    Q = {"v": g.vector, "s": g.scalar, "p": g.tensor, "g": g, "y": g.sync}
    CS = {"v": "cv", "s": "cs", "p": "cp", "g": "cg"}
    nodes, rec, banks, nd = [], {}, {}, [0]

    def node(alt, outs, ins, sem=None, inc=1, lat=None, extra=0.0, after=(), whole=True):
        me = len(nodes)
        wr = [r for o in outs for r in o[1]]
        rd = [r for o in outs for r in o[2]] + [r for o in ins if isinstance(o, tuple) for r in o[1] + o[2]]
        pred = set(after)
        eng = "".join(alt) if len(alt) == 1 else me
        for b in {r[0] for r in wr + rd if r[0][0] == "P" and r[0][1:].isdigit()}:
            st = banks.setdefault(b, [None, [], [], []])
            if st[0] != eng:
                st[0], st[1], st[2] = eng, [], st[1]
            pred.update(st[2])
            if eng == "p":
                pred.update(st[3] if whole else st[1] + st[3])
                if not whole:
                    st[3] = [me]
            st[1].append(me)
        for regs, w in ((wr, True), (rd, False)):
            for (b, lo, hi, tg) in regs:
                for (l2, h2, t2, w2, k) in rec.get(b, ()):
                    if l2 < hi and lo < h2 and (w or w2) and tg & t2:
                        pred.add(k)
        for (b, lo, hi, tg) in wr:
            rec[b] = [e for e in rec.get(b, ()) if not (lo <= e[0] and e[1] <= hi and not e[2] & ~tg)]
        for regs, w in ((rd, False), (wr, True)):
            for (b, lo, hi, tg) in regs:
                rec.setdefault(b, []).append((lo, hi, tg, w, me))
        pred.discard(me)
        kind = 2 if any(o[5] == "ind" for o in outs) else 1 if any(isinstance(o, tuple) and o[5] == "ind" for o in ins) else 0
        nodes.append({"alt": alt, "pred": pred, "sem": sem, "inc": inc, "lat": lat, "extra": extra, "kind": kind, "name": (wr + rd + [("", 0)])[0][:2]})
        return me

    def writers(*xs):
        return [k for x in xs for (b, lo, hi, tg) in x[1] for (l2, h2, t2, w2, k) in rec.get(b, ()) if w2 and l2 < hi and lo < h2]

    def s(name, lo=0, hi=None, step=1, p=None):
        if name in ALIAS:
            b, o, w = ALIAS[name]
            name, lo, hi = b, o + lo, o + (w if hi is None else hi)
        t = T[name]
        hi = t.shape[1] if hi is None else hi
        ps = slice(0, 128) if p is None else p
        tg = ALL if p is None else sum(1 << x for x in range(128)[p])
        return (t[ps, lo:hi:step] if step > 1 else t[ps, lo:hi], [(name, lo, hi, tg)], [], len(range(lo, hi, step)), SCRATCH[name][2], SCRATCH[name][0])

    def w_(name, lo, n):
        return s(name, lo, lo + n)

    def ind(win, off):
        return (win[0].indirect(off[0]), win[1], off[1], 16 * off[3], win[4], "ind")

    def a(x):
        return x[0] if isinstance(x, tuple) else x

    def cost(o, ins, rate=None):
        full = [o] + [x for x in ins if isinstance(x, tuple)]
        n = max(x[3] for x in full)
        if o[5] == "ind":
            rate = SCATTER
        elif any(x[5] == "ind" for x in full):
            rate = GATHER
        elif rate is None:
            rate = 0.5 if all(x[4] in (B16, U16) for x in full if x[3] > 1) else 1
        return FIX + max(64, n * rate) * CY

    def cp_(o, i):
        return (cost(o, [i]), lambda: g.vector.tensor_copy(o[0], i[0]))

    def ts_(o, x, s1, f0, s2=None, f1=None):
        if f1 is None:
            return (cost(o, [x]), lambda: g.vector.tensor_scalar(o[0], x[0], a(s1), None, f0))
        return (cost(o, [x]), lambda: g.vector.tensor_scalar(o[0], x[0], a(s1), a(s2), f0, f1))

    def act_(o, i, f=AF.Copy, bias=0.0, scale=1.0):
        return (cost(o, [i], 1), lambda: g.scalar.activation(o[0], i[0], f, bias=a(bias), scale=a(scale)))

    def cp(o, i, **k):
        return node({"v": cp_(o, i)}, [o], [i], **k)

    def tt(o, x, y, f, **k):
        c = cost(o, [x, y], 1 if "psum" in (x[5], y[5]) else 2)
        return node({"v": (c, lambda: g.vector.tensor_tensor(o[0], x[0], y[0], f))}, [o], [x, y], **k)

    def ts(o, x, s1, f0, s2=None, f1=None):
        return node({"v": ts_(o, x, s1, f0, s2, f1)}, [o], [x, s1, s2])

    def ms(o, c, **k):
        return node({"v": (cost(o, []), lambda: g.vector.memset(o[0], c))}, [o], [], **k)

    def scan(o, d0, d1, init, f0, f1):
        return node({"v": (cost(o, [d0, d1]), lambda: g.vector.tensor_tensor_scan(o[0], d0[0], d1[0], a(init), f0, f1))}, [o], [d0, d1, init])

    def red(o, i):
        return node({"v": (cost(o, [i], 1), lambda: g.vector.tensor_reduce(o[0], i[0], AX.X, AL.add))}, [o], [i])

    def act(o, i, f=AF.Copy, bias=0.0, scale=1.0):
        return node({"s": act_(o, i, f, bias, scale)}, [o], [i, bias, scale])

    def lin2(o, i, bias=0.0, scale=1.0, e="sv", **k):
        plain = not isinstance(bias, tuple) and bias == 0.0
        one = not isinstance(scale, tuple) and scale == 1.0
        alt = {"s": act_(o, i, AF.Copy if plain else AF.Identity, bias, scale),
               "v": cp_(o, i) if plain and one else (ts_(o, i, scale, AL.mult) if plain else ts_(o, i, scale, AL.mult, bias, AL.add))}
        return node({q: alt[q] for q in e}, [o], [i, bias, scale], **k)

    def over(o, i, thr):
        return node({"s": act_(o, i, AF.Relu, -0.375 * thr, 0.375), "v": ts_(o, i, thr, AL.is_gt, 0.375, AL.mult)}, [o], [i])

    def mms(lst, st=True, sp=True, tile=None, **k):
        c = sum(max(min(64, l[3]), r[3]) * (4 if l[4] == F32 else 1) for (o, l, r) in lst) * PECY
        calls = [(o, l, r, st and n == 0, sp and n == len(lst) - 1, tile) for n, (o, l, r) in enumerate(lst)]
        return node({"p": (c, calls)}, [x[0] for x in lst], [x[1] for x in lst] + [x[2] for x in lst], inc=len(lst), whole=st and sp, **k)

    def mm(o, l, r, st=True, sp=True, tile=None):
        return mms([(o, l, r)], st, sp, tile)

    def mmx(lst):
        c = sum(max(min(64, l[3]), r[3]) * (4 if l[4] == F32 else 1) for (o, l, r) in lst) * PECY
        return node({"p": (c, [(o, l, r, True, True, None) for (o, l, r) in lst])}, [x[0] for x in lst], [x[1] for x in lst] + [x[2] for x in lst], inc=len(lst))

    def iota(o, pat, base, cm, flt=True):
        c = GSLACK * (0.13 + 2 * o[3] * CY)
        if flt:
            return node({"g": (c, lambda: g.iota(o[0], pat, base, cm, allow_small_or_imprecise_dtypes=True))}, [o], [])
        return node({"g": (c, lambda: g.iota(o[0], pat, base, cm))}, [o], [])

    def fill(name, lo, hi, val=0):
        for x in range(lo, hi, 512):
            iota(s(name, x, min(hi, x + 512)), [[0, min(hi, x + 512) - x]], val, 0)

    def sel(o, i, pat, cmp, fil, base, cm=1):
        return node({"g": (GSLACK * (0.17 + 2 * o[3] * CY), lambda: g.affine_select(o[0], i[0], pat, cmp, fil, base, cm))}, [o], [i])

    def dma(q, o, i, nbytes, rows=128, **k):
        sem = "d%d" % nd[0]
        nd[0] += 1
        c = ROWS * rows / 128 + nbytes / DMABW
        me = node({"d": (c, lambda: Q[q].dma_start(o[0], i[0]))}, [o], [i], sem=sem, inc=16, lat=DMA0 + c, **k)
        nodes[me]["by"] = q
        return me

    def ext(ap):
        return (ap, [], [], 1, None, "hbm")

    sends, lands = [], []
    en = [e for e in topo.engines(core, T.cores[rank ^ 1]) if all(e in topo.engines(core, T.cores[rank ^ d]) for d in (2, 3))]
    pool = {True: en[0::2], False: en[1::2]}
    lanes = []
    for d in (1, 2, 3):
        far_die = topo.die(core) != topo.die(T.cores[rank ^ d])
        side = far_die if len(pool[far_die]) >= len(en) // 4 else not far_die
        lanes.append(pool[side][:len(en) // 4])
        pool[side] = pool[side][len(en) // 4:]
    near = sorted(range(3), key=lambda d: topo.die(core) != topo.die(T.cores[rank ^ (d + 1)]))
    wide = [None] * 3
    wide[near[0]], wide[near[1]], wide[near[2]] = en[0::2], en[1::2], en
    ways = (([[0, 1, 2]], lanes), ([near[:2], near[2:]], wide))

    def send(srcs, land, base, w, extra=0.0, gap=0):
        m = len(sends)
        trs, tot = [], 0
        calls, lanes = ways[m in TWO]
        for d in (1, 2, 3):
            dst = T.cores[rank ^ d]
            rid, pid, _ = topo.addr(dst)
            k = len(lanes[d - 1])
            mask = sum(1 << e for e in lanes[d - 1])
            tot += k
            trs.append(RemoteDMATransfer(dst_ids=[DstId(rid=rid, pnc=pid)], dma_engine_mask=mask, remote_sem=T.sem["ar%d" % m],
                                         src=srcs[d - 1][0], dst=w_(land, base + (d - 1) * (w + gap), w)[0]))

        def go():
            for c in calls:
                g.remote_dma_fused([trs[d] for d in c], local_sem=T.sem["ls%d" % m])
        k = node({"g": (0.6 * len(calls) + (0 if m else FIRST), go)}, [], srcs, sem="ls%d" % m, inc=tot, lat=REMOTE - 0.2 * (m in TWO) + (MARGIN if extra and m < 12 else 0) + (0 if m else FIRST), after=sends[-1:], extra=extra)
        nodes[k]["order"] = set(sends[-1:])
        sends.append(k)
        return node({"-": (0.0, None)}, [w_(land, base + d * (w + gap), w) for d in range(3)], [], sem="ar%d" % m, inc=tot, lat=0.01, after=[k])

    def issue():
        n = len(nodes)
        succ = [[] for _ in range(n)]
        for k, x in enumerate(nodes):
            for j in x["pred"]:
                succ[j].append(k)

        def delay(j, c, k):
            x, y = nodes[j], nodes[k]
            if j in y.get("order", ()):
                return c
            return (x["lat"] or c) + (0.0 if "-" in y["alt"] or ("p" in x["alt"] and "p" in y["alt"]) else WAKE)

        def place(key, back, spare):
            busy, at = {q: [] for q in "vspgd-"}, [None] * n
            for k in sorted(range(n), key=lambda k: (-key[k], -k if back else k)):
                x, best = nodes[k], None
                for q, (c, _) in x["alt"].items():
                    if back:
                        t0 = max([at[j][1] + at[j][2] + delay(k, c, j) for j in succ[k]] + [x["lat"] or c]) - c
                    else:
                        t0 = max([at[j][1] + delay(j, at[j][2], k) for j in x["pred"]] + [0.0])
                    lane, i = busy[q], 0
                    while i < len(lane) and t0 + c > lane[i][0]:
                        t0 = max(t0, lane[i][1])
                        i += 1
                    fin = t0 + DEAR * c + (spare if q == "v" else 0.0)
                    if best is None or fin < best[0]:
                        best = (fin, q, t0, c, i)
                at[k] = best[1:4]
                if best[1] != "-":
                    busy[best[1]].insert(best[4], (best[2], best[2] + best[3]))
            return at

        def length(at, rate):
            free, t0, c = {}, [0.0] * n, [0.0] * n
            for k in sorted(range(n), key=lambda k: (at[k][1], k)):
                q = at[k][0]
                c[k] = FIX + (at[k][2] - FIX) * rate[nodes[k]["kind"]] if nodes[k]["kind"] else at[k][2]
                t0[k] = max([t0[j] + delay(j, c[j], k) for j in nodes[k]["pred"]] + [free.get(q, 0.0)])
                free[q] = t0[k] + c[k]
            return max(t0[k] + (nodes[k]["lat"] or c[k]) for k in range(n))

        def polish(at):
            edge = [[(j, None if j in y.get("order", ()) or not nodes[j]["lat"] else nodes[j]["lat"],
                      delay(j, 0.0, k) - (0.0 if j in y.get("order", ()) else nodes[j]["lat"] or 0.0)) for j in y["pred"]] for k, y in enumerate(nodes)]
            order = sorted(range(n), key=lambda k: (at[k][1], k))
            que = [x[0] for x in at]
            rates = [(0, ga / GATHER, sc / SCATTER) for ga, sc, slow, wake in POLISH]
            tail = [k for k in range(n) if not succ[k]]

            def times(k):
                c = nodes[k]["alt"][que[k]][0]
                return [FIX + (c - FIX) * r[nodes[k]["kind"]] if nodes[k]["kind"] else c for r in rates]
            cs = [list(z) for z in zip(*[times(k) for k in range(n)])]

            def run(c, old, p0):
                t0, free = old[:], {}
                for p in range(p0 - 1, -1, -1):
                    k = order[p]
                    if que[k] not in free:
                        free[que[k]] = t0[k] + c[k]
                        if len(free) == 6:
                            break
                for k in order[p0:]:
                    q = que[k]
                    t = free.get(q, 0.0) if q != "-" else 0.0
                    for j, lat, w in c[n][k]:
                        e = t0[j] + (lat or c[j]) + w
                        if e > t:
                            t = e
                    t0[k] = t
                    free[q] = t + c[k]
                return t0, max(t0[k] + (nodes[k]["lat"] or c[k]) for k in tail)

            for c, (ga, sc, slow, wake) in zip(cs, POLISH):
                c.append([[(j, lat and lat * slow, w * wake) for j, lat, w in e] for e in edge])
                c.append([[] for _ in range(n)])
                for k in range(n):
                    for j, lat, w in c[n][k]:
                        c[n + 1][j].append((k, lat, w))

            def tails(c):
                y, nxt = [0.0] * n, {}
                for k in reversed(order):
                    q = que[k]
                    t = c[k] + nxt.get(q, 0.0) if q != "-" else 0.0
                    for j, lat, w in c[n + 1][k]:
                        e = (lat or c[k]) + w + y[j]
                        if e > t:
                            t = e
                    y[k] = nxt[q] = max(t, nodes[k]["lat"] or c[k])
                return y

            def least(c, old, y, p0, p1):
                t0, free, top_ = {}, {}, 0.0
                part = order[p0:p1 + 1]
                need = {que[k] for k in part}
                for p in range(p0 - 1, -1, -1):
                    k = order[p]
                    if que[k] in need and que[k] not in free:
                        free[que[k]] = old[k] + c[k]
                        if len(free) == len(need):
                            break
                for k in part:
                    q = que[k]
                    t = free.get(q, 0.0) if q != "-" else 0.0
                    for j, lat, w in c[n][k]:
                        e = t0.get(j, old[j]) + (lat or c[j]) + w
                        if e > t:
                            t = e
                    t0[k] = t
                    free[q] = t + c[k]
                for k in part:
                    for j, lat, w in c[n + 1][k]:
                        if j not in t0:
                            e = t0[k] + (lat or c[k]) + w + y[j]
                            if e > top_:
                                top_ = e
                need.discard("-")
                for p in range(p1 + 1, n):
                    if not need:
                        break
                    k = order[p]
                    if que[k] in need:
                        need.discard(que[k])
                        top_ = max(top_, free[que[k]] + y[k])
                return top_

            def waits(c, t0):
                before, last, out = [None] * n, {}, []
                for k in order:
                    before[k], last[que[k]] = last.get(que[k]), k
                k = max(tail, key=lambda k: t0[k] + (nodes[k]["lat"] or c[k]))
                while t0[k] > 0.0:
                    on = [j for j, lat, w in c[n][k] if t0[j] + (lat or c[j]) + w >= t0[k] - 1e-9]
                    if not on:
                        out.append((before[k], k))
                    k = on[0] if on else before[k]
                return out
            now = [run(c, [0.0] * n, 0) for c in cs]
            norm = [1.0 / x[1] for x in now]
            score, seed, cand = float(len(rates)), 1, None
            best = (score, order[:], que[:], now[0][0])
            for it in range(TRIES):
                if cand is None:
                    cand = [e for c, x in zip(cs, now) for e in waits(c, x[0])]
                    rest = [tails(c) for c in cs]
                seed = (seed * 1103515245 + 12345) % 2147483648
                j, k = cand[(seed >> 8) % len(cand)]
                move, pj, pk = (seed >> 4) % 4, order.index(j), order.index(k)
                for hop in range((seed >> 20) % 4 if move < 2 else 0):
                    step = 1 if move else -1
                    p = (pk if move else pj) + step
                    while 0 <= p < n and que[order[p]] != que[k]:
                        p += step
                    if 0 <= p < n:
                        pj, pk = (pj, p) if move else (p, pk)
                        j, k = order[pj], order[pk]
                keep, moved = order[pj:pk + 1], None
                if move < 2:
                    grp = {k if move == 0 else j}
                    for z in (reversed(keep) if move == 0 else keep):
                        if z in grp:
                            grp.update(nodes[z]["pred"] if move == 0 else succ[z])
                    if (j if move == 0 else k) in grp:
                        continue
                    a0, a1 = [z for z in keep if z in grp], [z for z in keep if z not in grp]
                    order[pj:pk + 1] = a0 + a1 if move == 0 else a1 + a0
                else:
                    moved = (j, k)[move - 2]
                    other = [q for q in nodes[moved]["alt"] if q != que[moved]]
                    if not other:
                        continue
                    was, que[moved] = que[moved], other[0]
                    for c, x in zip(cs, times(moved)):
                        c[moved] = x
                bar = score + HEAT * (1.0 - it / TRIES) * ((seed >> 12) % 16) / 16
                got = sum(least(c, x[0], y, pj, pk) * w for c, x, y, w in zip(cs, now, rest, norm))
                if got <= bar:
                    new = [run(c, x[0], pj) for c, x in zip(cs, now)]
                    got = sum(x[1] * w for x, w in zip(new, norm))
                if got <= bar:
                    score, now, cand = got, new, None
                    if got < best[0]:
                        best = (got, order[:], que[:], now[0][0])
                else:
                    order[pj:pk + 1] = keep
                    if moved is not None:
                        que[moved] = was
                        for c, x in zip(cs, times(moved)):
                            c[moved] = x
            out = [None] * n
            for p, k in enumerate(best[1]):
                out[k] = (best[2][k], best[3][k], nodes[k]["alt"][best[2][k]][0], p)
            return out
        def improve(at):
            order = sorted(range(n), key=lambda k: (at[k][1], k))
            que = [x[0] for x in at]
            ns = len(POLISH)

            def times(k):
                c, kind = nodes[k]["alt"][que[k]][0], nodes[k]["kind"]
                if que[k] == "p":
                    return [c * x[4] for x in POLISH]
                if que[k] in "vs" and not kind:
                    return [c * x[5] if c < FIX + 65 * CY else c for x in POLISH]
                more = SFIX if que[k] == "s" else 0.0
                return [FIX + more + (c - FIX) * (0, x[0] / GATHER, x[1] / SCATTER)[kind] if kind else c for x in POLISH]
            cs = [list(z) for z in zip(*[times(k) for k in range(n)])]
            ins, outs, last = [], [], []
            for ga, sc, slow, wake, pe, fix in POLISH:
                e = [[(j, None if j in y.get("order", ()) or not nodes[j]["lat"] else nodes[j]["lat"] * slow,
                       (delay(j, 0.0, k) - (0.0 if j in y.get("order", ()) else nodes[j]["lat"] or 0.0)) * wake) for j in y["pred"]] for k, y in enumerate(nodes)]
                o = [[] for _ in range(n)]
                for k in range(n):
                    for j, lat, w in e[k]:
                        o[j].append((k, lat, w))
                ins.append(e)
                outs.append(o)
            own = [x["lat"] or 0.0 for x in nodes]

            def heads(c, e, t0, part, rel, free):
                for k in part:
                    q = que[k]
                    t = rel[k]
                    if q != "-" and free[q] > t:
                        t = free[q]
                    for j, lat, w in e[k]:
                        x = t0[j] + (lat or c[j]) + w
                        if x > t:
                            t = x
                    t0[k] = t
                    free[q] = t + c[k]
                return t0

            def tails(c, o, y, part, oc, ol, nxt):
                for k in reversed(part):
                    q, ck = que[k], c[k]
                    t = ck + oc[k]
                    if q != "-" and ck + nxt[q] > t:
                        t = ck + nxt[q]
                    if ol[k] > t:
                        t = ol[k]
                    for j, lat, w in o[k]:
                        x = (lat or ck) + w + y[j]
                        if x > t:
                            t = x
                    y[k] = nxt[q] = t
                return y
            zero, seed = [0.0] * n, 1
            blank = lambda: dict.fromkeys("vspgd-", 0.0)
            for sweep, (width, tries, *upto) in enumerate(SWEEPS):
                ys = [tails(cs[r], outs[r], [0.0] * n, order, zero, own, blank()) for r in range(ns)]
                ts0 = [heads(cs[r], ins[r], [0.0] * n, order, zero, blank()) for r in range(ns)]
                norm = [1.0 / max(y) for y in ys]
                LOG.append([round(max(y), 1) for y in ys])
                for p0 in range(-(width // 4) * (sweep & 1), (upto + [n])[0], width // 2):
                    p0, p1 = max(p0, 0), min(n, p0 + width)
                    part = order[p0:p1]
                    m, inside = len(part), set(part)
                    sub = []
                    for r in range(ns):
                        c, t0, y, rel, oc, ol, qf, qt = cs[r], ts0[r], ys[r], {}, {}, {}, blank(), blank()
                        e, o = {}, {}
                        for k in part:
                            e[k] = [z for z in ins[r][k] if z[0] in inside]
                            o[k] = [z for z in outs[r][k] if z[0] in inside]
                            rel[k] = max([t0[j] + (lat or c[j]) + w for j, lat, w in ins[r][k] if j not in inside] + [0.0])
                            oc[k] = max([w + y[j] for j, lat, w in outs[r][k] if j not in inside and not lat] + [0.0])
                            ol[k] = max([lat + w + y[j] for j, lat, w in outs[r][k] if j not in inside and lat] + [own[k]])
                        for k in order[:p0]:
                            qf[que[k]] = t0[k] + c[k]
                        for k in reversed(order[p1:]):
                            qt[que[k]] = y[k]
                        sub.append((c, e, o, rel, oc, ol, qf, qt))

                    def full(pj, pk, now):
                        out, cand, total = [], [], 0.0
                        before, seen, nxt = {}, {}, {}
                        for k in part[:pj]:
                            before[k], seen[que[k]] = seen.get(que[k]), k
                        prev = dict(seen)
                        for k in part[pj:]:
                            before[k], seen[que[k]] = seen.get(que[k]), k
                        for k in part[:pk:-1]:
                            nxt[que[k]] = k
                        late, early = part[pj:], part[:pk + 1]
                        for (c, e, o, rel, oc, ol, qf, qt), (t0, y), w0 in zip(sub, now, norm):
                            t0 = heads(c, e, dict(t0), late, rel, {q: t0[prev[q]] + c[prev[q]] if q in prev else qf[q] for q in qf})
                            y = tails(c, o, dict(y), early, oc, ol, {q: y[nxt[q]] if q in nxt else qt[q] for q in qt})
                            thru = [t0[k] + y[k] for k in part]
                            top_ = max(thru)
                            total += top_ * w0
                            bar_ = top_ - NEAR
                            for k, x in zip(part, thru):
                                if x >= bar_:
                                    j = before[k]
                                    if j is not None and t0[j] + c[j] >= t0[k] - 1e-9 and que[k] != "-":
                                        cand.append((j, k))
                            out.append((t0, y))
                        return total, out, cand

                    def least(pj, pk):
                        seg, total = part[pj:pk + 1], 0.0
                        need = {que[k] for k in seg}
                        need.discard("-")
                        prev, nxt = {}, {}
                        for p in range(pj - 1, -1, -1):
                            q = que[part[p]]
                            if q in need and q not in prev:
                                prev[q] = part[p]
                                if len(prev) == len(need):
                                    break
                        for p in range(pk + 1, m):
                            q = que[part[p]]
                            if q in need and q not in nxt:
                                nxt[q] = part[p]
                                if len(nxt) == len(need):
                                    break
                        for (c, e, o, rel, oc, ol, qf, qt), (old, y), w0 in zip(sub, now, norm):
                            free = {q: old[prev[q]] + c[prev[q]] if q in prev else qf[q] for q in need}
                            free["-"] = 0.0
                            t0, top_ = {}, 0.0
                            for k in seg:
                                q = que[k]
                                t = rel[k]
                                if q != "-" and free[q] > t:
                                    t = free[q]
                                for j, lat, w in e[k]:
                                    x = (t0[j] if j in t0 else old[j]) + (lat or c[j]) + w
                                    if x > t:
                                        t = x
                                t0[k] = t
                                free[q] = t + c[k]
                            for k in seg:
                                ck = c[k]
                                x = max(ck + oc[k], ol[k])
                                for j, lat, w in o[k]:
                                    if j not in t0:
                                        z = (lat or ck) + w + y[j]
                                        if z > x:
                                            x = z
                                if t0[k] + x > top_:
                                    top_ = t0[k] + x
                            for q in need:
                                x = free[q] + (y[nxt[q]] if q in nxt else qt[q])
                                if x > top_:
                                    top_ = x
                            total += top_ * w0
                        return total
                    score, now, cand = full(0, m - 1, [({}, {})] * ns)
                    best = (score, part[:], [que[k] for k in part])
                    for it in range(tries if cand else 0):
                        seed = (seed * 1103515245 + 12345) % 2147483648
                        j, k = cand[(seed >> 8) % len(cand)]
                        move, pj, pk = (seed >> 4) % MOVES, part.index(j), part.index(k)
                        if move >= 4:
                            v = (j, k)[move & 1]
                            pv = part.index(v)
                            lo, hi = pv - 1, pv + 1
                            while lo >= 0 and part[lo] not in nodes[v]["pred"]:
                                lo -= 1
                            while hi < m and v not in nodes[part[hi]]["pred"]:
                                hi += 1
                            was, pick, ends = que[v], None, []
                            for (c, e, o, rel, oc, ol, qf, qt), (t0, y) in zip(sub, now):
                                ends.append((max([t0[z] + (lat or c[z]) + w for z, lat, w in e[v]] + [rel[v]]),
                                             max([w + y[z] for z, lat, w in o[v] if not lat] + [oc[v]]),
                                             max([lat + w + y[z] for z, lat, w in o[v] if lat] + [ol[v]])))
                            for q in nodes[v]["alt"]:
                                que[v] = q
                                cv = times(v)
                                p = lo
                                while p >= 0 and (que[part[p]] != q or p == pv):
                                    p -= 1
                                u = part[p] if p >= 0 else None
                                for p in range(lo + 1, m + 1):
                                    x = part[p] if p < m else None
                                    if p == pv or (x is not None and que[x] != q):
                                        continue
                                    if not (q == was and (u is None or part.index(u) < pv) and p > pv):
                                        est = 0.0
                                        for sb, (t0, y), en_, cc, w0 in zip(sub, now, ends, cv, norm):
                                            a_ = sb[6][q] if u is None else t0[u] + sb[0][u]
                                            b_ = sb[7][q] if x is None else y[x]
                                            est += w0 * (max(a_, en_[0]) + max(cc + max(b_, en_[1]), en_[2]))
                                        seed = (seed * 1103515245 + 12345) % 2147483648
                                        est += HEAT * ((seed >> 10) % 32) / 32
                                        if pick is None or est < pick[0]:
                                            pick = (est, q, min(p, hi))
                                    if p >= hi:
                                        break
                                    u = x
                            que[v] = was
                            if pick is None:
                                continue
                            p = pick[2]
                            pj, pk = min(p, pv), max(p - 1, pv)
                            keep, moved = part[pj:pk + 1], v
                            rest_ = [z for z in keep if z != v]
                            part[pj:pk + 1] = [v] + rest_ if p <= pv else rest_ + [v]
                            que[v] = pick[1]
                            for c, x in zip(cs, times(v)):
                                c[v] = x
                        for hop in range((seed >> 20) % 4 if move < 2 else 0):
                            step = 1 if move else -1
                            p = (pk if move else pj) + step
                            while 0 <= p < m and que[part[p]] != que[k]:
                                p += step
                            if 0 <= p < m:
                                pj, pk = (pj, p) if move else (p, pk)
                                j, k = part[pj], part[pk]
                        if move < 4:
                            keep, moved = part[pj:pk + 1], None
                        if move < 2:
                            grp = {k if move == 0 else j}
                            for z in (reversed(keep) if move == 0 else keep):
                                if z in grp:
                                    grp.update(nodes[z]["pred"] if move == 0 else succ[z])
                            if (j if move == 0 else k) in grp:
                                continue
                            a0, a1 = [z for z in keep if z in grp], [z for z in keep if z not in grp]
                            part[pj:pk + 1] = a0 + a1 if move == 0 else a1 + a0
                        elif move < 4:
                            moved = (j, k)[move - 2]
                            other = [q for q in nodes[moved]["alt"] if q != que[moved]]
                            if not other:
                                continue
                            was, que[moved] = que[moved], other[0]
                            for c, x in zip(cs, times(moved)):
                                c[moved] = x
                        bar = score + HEAT * (1.0 if sweep < len(SWEEPS) - COOL else 0.3) * (1.0 - it / tries) * ((seed >> 12) % 16) / 16
                        new = full(pj, pk, now) if least(pj, pk) <= bar else None
                        if new and new[0] <= bar and new[2]:
                            score, now, cand = new
                            part.sort(key=now[0][0].get)
                            if score < best[0]:
                                best = (score, part[:], [que[k] for k in part])
                        else:
                            part[pj:pk + 1] = keep
                            if moved is not None:
                                que[moved] = was
                                for c, x in zip(cs, times(moved)):
                                    c[moved] = x
                    part = order[p0:p1] = best[1]
                    for k, q in zip(part, best[2]):
                        if que[k] != q:
                            que[k] = q
                            for c, x in zip(cs, times(k)):
                                c[k] = x
                    for r, (c, e, o, rel, oc, ol, qf, qt) in enumerate(sub):
                        heads(c, e, ts0[r], part, rel, dict(qf))
            if DEBUG:
                for r in range(ns):
                    y = tails(cs[r], outs[r], [0.0] * n, order, zero, own, blank())
                    t0 = heads(cs[r], ins[r], [0.0] * n, order, zero, blank())
                    DEBUG.append([(round(t0[k], 2), que[k], round(cs[r][k], 2), nodes[k]["name"], round(max(y) - t0[k] - y[k], 2)) for k in order])
            out = [None] * n
            for p, k in enumerate(order):
                out[k] = (que[k], 0.0, nodes[k]["alt"][que[k]][0], p)
            return out
        top = []
        for spare in (() if PLAN else VPEN):
            far = [0.0] * n
            for k in range(n - 1, -1, -1):
                x = nodes[k]
                far[k] += (x["lat"] or min(c for c, _ in x["alt"].values())) + x["extra"]
                for j in x["pred"]:
                    far[j] = max(far[j], far[k] + WAKE)
            for rnd in range(ROUNDS):
                at = place(far, False, spare)
                score = sum(length(at, (0, ga / GATHER, sc / SCATTER)) / (1 + ga) for ga, sc in RATES)
                top.append((score, len(top), at))
                end = [0.0] * n
                for k, x in enumerate(nodes):
                    end[k] = max([at[k][1] + (x["lat"] or at[k][2])] + [end[j] + 1e-6 for j in x["pred"]])
                at = place(end, True, spare)
                far = [t0 + c + x.get("push", 0.0) for x, (q, t0, c) in zip(nodes, at)]
                for k in range(n - 1, -1, -1):
                    for j in nodes[k]["pred"]:
                        far[j] = max(far[j], far[k] + delay(j, at[j][2], k))
        if not PLAN:
            PLAN.append(improve(sorted(top)[START][2]))
        for x, at in zip(nodes, PLAN[0]):
            x["q"], x["t"] = at[0], max([at[3]] + [nodes[j]["t"] for j in x["pred"]])
        cnt, waited, tiles = {}, {}, {}

        def wait(q, sem, val):
            if waited.get((q, sem), 0) < val:
                Q[q].wait_ge(T.sem[sem], val)
                waited[(q, sem)] = val
        for k in sorted(range(n), key=lambda k: (nodes[k]["t"], k)):
            x = nodes[k]
            q = x["q"]
            own = x["sem"] or CS[q]
            cnt[own] = cnt.get(own, 0) + x["inc"]
            x["mark"] = (own, cnt[own])
            if q == "-":
                continue
            need = {}
            for j in x["pred"]:
                if j in x.get("order", ()) or q == nodes[j]["q"] == "p":
                    continue
                sem, val = nodes[j]["mark"]
                need[sem] = max(need.get(sem, 0), val)
            for sem, val in need.items():
                wait(x.get("by", q), sem, val)
            call = x["alt"][q][1]
            if q == "p":
                for i, (o, l, r, st, sp, tile) in enumerate(call):
                    bank = o[1][0][0]
                    if bank in tiles and tiles[bank][0] != tile:
                        wait("p", "cp", tiles[bank][1])
                    g.tensor.matmul(o[0], l[0], r[0], st, sp).then_inc(T.sem["cp"], 1)
                    tiles[bank] = (tile, cnt[own] - x["inc"] + i + 1)
            else:
                ins_ = call()
                if ins_ is not None:
                    ins_.then_inc(T.sem[own], x["inc"])
        for sem, val in cnt.items():
            wait("g", sem, val)

    high = [rank > (rank ^ d) for d in (1, 2, 3)]
    cols, mats, sms = {}, {}, {}

    def col(n):
        if n not in cols:
            cols[n] = len(cols)
        return w_("CF", cols[n], 1)

    def ic(i):
        return w_("IC", i, 1)

    def M(n):
        if n[:2] == "PI":
            return w_("PIT", 32 - 16 * int(n[2]), 128)
        if n not in mats:
            mats[n] = len(mats)
        return w_("MAT", mats[n] * 128, 128)

    def sm(n, w=8):
        if n not in sms:
            sms[n] = (sum(x[1] for x in sms.values()), w)
        return w_("SM", sms[n][0], sms[n][1])

    def shift(k):
        return s("ZW", 16 - k, 144 - k)

    def slide(z, r):
        return w_("ZW", 160 * z + 15 - r, 128)

    def lin(n, terms):
        for k, (i, w) in enumerate(terms):
            lin2(col(n if k == len(terms) - 1 else n + str(k)), ic(i), col(n + str(k - 1)) if k else 0.0, float(w))

    def terms(o, lst, first=True):
        n = o[3]
        for (i, j, w) in lst:
            pat = [[-16, 8]] if n == 8 else [[-16, n // 16], [0 if j is None else 256, 16]]
            sel(o, s("ZERO", 0, n) if first else o, pat, AL.not_equal, float(w), -i - 256 * (j or 0))
            first = False

    row = lambda i: slice(i, 128, 16)
    AREP, XREP = s("A", H, V), s("X", H, V)
    AW, XW_ = s("A"), s("X")
    ID, G8, BD = shift(0), s("G8"), M("BD")
    Z128, O128 = s("ZERO", 0, 128), s("ONES", 0, 128)

    first = [dma("y", s("WI"), ext(T.wv[:]), 98304), dma("y", s("OVI"), ext(T.ov[:]), 65536), dma("y", s("NLI"), ext(T.nl[:]), 8192)]
    ms(s("ZERO"), 0.0)
    ms(s("CODE", 0, 960), 0.0)
    for i in (4, 5):
        first.append(dma("y", s("DEW", 0, V, p=row(i)), s("CODE", 0, 768, p=slice(0, 32)), 49152, rows=32))
    first.append(dma("y", s("SI"), ext(T.sc[:]), 65536))
    dma("y", XREP, ext(T.xv[:, H:V]), 49152)
    for x in range(0, C, VAW):
        va_in = dma("y", w_("VA", x, VAW), ext(T.va[:, x:x + VAW]), 512 * VAW, after=first)
        nodes[va_in]["order"] = set(first)
        first = [va_in]
    iota(s("II", 0, 1), [[0, 1]], 0, 1, False)
    iota(s("IO"), [[1, 256]], 0, 0)
    iota(s("JW"), [[16, 128]], 0, 1)
    iota(s("II", 16, 48), [[1, 32]], 0, 0, False)
    iota(s("II", 48, 56), [[16, 8]], 15, 0, False)
    const = lambda o, c: lin2(o, s("ZERO", 0, o[3]), c)
    const(s("ONES"), 1.0)
    sel(s("ZW", 0, 160), s("ZERO", 0, 160), [[-1, 160]], AL.not_equal, 1.0, 16)
    iota(M("SELK"), [[0, 8], [4096, 16]], 2048, 0)
    sel(M("SELK"), M("SELK"), [[-16, 8], [0, 16]], AL.is_equal, 0.0, -6)
    terms(M("SELK"), [(0, None, 65536), (4, None, 256), (5, None, 1)], False)
    lin2(s("RSB"), s("ZERO"))
    lin2(s("RSB", 0, 256, 16), s("ONES", 0, 16), scale=BIG)
    sel(G8, s("ONES", 0, 8), [[-16, 8]], AL.is_ge, 0.0, 0)
    sel(G8, G8, [[16, 8]], AL.is_ge, 0.0, 15, -1)
    terms(sm("SELS"), [(8, None, 65536)])
    terms(sm("SELC"), [(4, None, 256), (5, None, 1)])
    lin2(s("IDF"), ID)
    for x in (960, 1920):
        dma("y", w_("CODE", x, 960), s("CODE", 0, 960), 245760, after=[va_in])
    const(s("TMP", 0, 8), 2.0)
    ts(s("II", 1, 2), s("II", 0, 1), 15, AL.bitwise_and)
    ts(s("II", 2, 3), s("II", 0, 1), 112, AL.bitwise_and)
    ts(s("II", 3, 4), s("II", 0, 1), 16, AL.bitwise_and)
    ts(s("II", 4, 5), s("II", 0, 1), 1, AL.bitwise_and)
    ts(s("II", 5, 6), s("II", 0, 1), 14, AL.bitwise_and)
    ts(s("II", 6, 7), s("II", 0, 1), 7, AL.bitwise_and)
    for n in ("p", "i", "g16", "odd", "par", "r2", "r8"):
        col(n)
    cp(s("CF", 0, 4), s("II", 0, 4))
    cp(s("CF", 4, 7), s("II", 4, 7))
    ms(s("VA", C, C + 16), NV)
    iota(s("VA", C + 16, CWD), [[0, CWD - C - 16]], NV, 0, False)
    ts(s("IC"), s("IO", 0, 16), col("i"), AL.is_equal)
    ts(s("BITS", 0, 1), col("i"), 12.0, AL.is_lt)
    for n in range(8):
        col("w5_%d" % n)
    for n in range(4):
        col("w4_%d" % n)
    lin("h5", [(5, 0.5)])
    lin("h4", [(4, 0.5)])
    ts(s("TF", 128, 144), s("IC"), -2.0, AL.mult, 1.0, AL.add)
    lin("cw", [(4, -8), (6, 1), (7, 1)])
    lin2(col("ca"), ic(0), col("cw"), 255.0)
    scan(w_("CF", cols["w5_0"], 8), s("TMP", 0, 8), s("ZERO", 0, 8), col("h5"), AL.mult, AL.add)
    scan(w_("CF", cols["w4_0"], 4), s("TMP", 0, 4), s("ZERO", 0, 4), col("h4"), AL.mult, AL.add)
    lin2(s("A", 0, 256), s("IO"), col("ca"), ic(5))
    for k in range(4):
        n = 256 << k
        w = min(n, VW - n)
        lin2(w_("A", n, w), s("A", 0, w), col("w4_%d" % k))
    for b in range(12):
        n = 1 << b
        w = min(n, DV0 - n)
        lin2(w_("BITS", n, w), s("BITS", 0, w), scale=w_("TF", 128 + b, 1))
    cp(s("WB"), s("WI"))
    lin2(s("DVAL", 0, 16), s("IO", 0, 16), col("cw0"), col("h4"))
    ts(s("JW"), s("JW"), col("g16"), AL.subtract)
    dma("y", s("A", 0, V, p=row(0)), s("WB"), 49152)
    lin2(s("MASKR", 0, 16), s("IC"))
    for k in range(5):
        lin2(w_("MASKR", 16 << k, 16 << k), s("MASKR", 0, 16 << k))
    for k in range(7):
        lin2(s("DVAL", 16 << k, 32 << k), s("DVAL", 0, 16 << k), col("w5_%d" % k))
    ts(s("TMP", 128, 256), s("OVI"), float(V), AL.is_ge)
    lin2(s("TMP2", 128, 256), s("JW"), 16.0)
    cp(s("SBF"), s("SI"))
    tt(s("TMP", 128, 256), s("TMP", 128, 256), s("TMP2", 128, 256), AL.mult)
    cp(s("LN", 0, 16), s("NLI"))
    tt(s("OV2", 0, 128), s("TMP", 128, 256), s("OVI"), AL.add)
    dma("y", s("A", 0, C, p=row(8)), s("SBF"), 32768)
    cp(s("OVL"), s("OV2", 0, 128))
    VARS0 = s("VARS", 0, 256)
    cp(VARS0, ind(s("VA", 0, C + 16), s("LN", 0, 16)))
    for j in range(8):
        nodes[cp(ind(s("DEW"), w_("OVL", 16 * j, 16)), w_("DVAL", 256 * j, 256), extra=OWN_X - j)]["push"] = PUSHO
    send([w_("X", H + S * d, S) for d in range(3)], "LA", 0, S)
    iota(s("JT", 0, 16), [[128, 2], [0, 8]], 0, 1)
    iota(s("JT", 16, 32), [[128, 2], [0, 8]], DV0, 1)
    lin2(s("VT"), s("CODE", 0, 272))
    sel(BD, O128, [[-16, 8], [0, 16]], AL.is_ge, 0.0, 0)
    sel(BD, BD, [[16, 8], [0, 16]], AL.is_ge, 0.0, 15, -1)
    terms(sm("SELE"), [(2, None, 256), (3, None, 1)])
    terms(M("SV1"), [(4, 4, 1), (5, 5, 1), (6, 6, 1), (6, 1, 1), (8, 8, 1)])
    terms(M("SV2"), [(4, 2, 1), (5, 3, 1)])
    sel(s("PIT"), s("ZERO", 0, 160), [[16, 10], [-1, 16]], AL.not_equal, 1.0, -48)
    sel(s("PIT"), s("PIT"), [[16, 10], [-1, 16]], AL.not_equal, 1.0, -48 - 128)
    sel(M("B7"), BD, [[0, 8], [1, 16]], AL.is_equal, 0.0, -7, 0)
    terms(M("K1"), [(0, 1, 1), (6, 1, 1), (6, 7, 1)])
    terms(M("K3"), [(2, 1, -1)])
    iota(s("II", 12, 15), [[16, 3]], 143 + 16, -1, False)
    iota(s("GI"), [[16, 8], [0, 16]], 0, 0)
    terms(M("SK"), [(1, None, -1)])
    sel(M("SD"), Z128, [[-1, 128]], AL.not_equal, -1.0, 0)
    sel(M("SD"), M("SD"), [[0, 8], [-1, 16]], AL.is_ge, 0.0, 3, 0)
    terms(M("SD"), [(7, 7, -1)], False)
    cp(s("ELX", 0, 40), s("II", 16, 56))
    lin2(col("od"), col("odd"), scale=1.0 / 16)
    ts(col("ev"), col("odd"), 1.0, AL.is_lt)
    const(s("TMP2", 0, 128), 0.5)
    lin2(s("YY", 0, 256, 128), s("ZERO", 0, 2))
    scan(s("T192", 0, 128), s("TMP2", 0, 128), Z128, 2.0 ** 61, AL.mult, AL.add)
    lin2(s("BASEW", 0, 16), s("JW", 0, 16), float(DV0))
    tt(s("T192", 0, 128), s("T192", 0, 128), s("IDF"), AL.mult)
    red(col("pow"), s("T192", 0, 128))
    lin2(w_("CODE", H, 16), s("IC"))
    for n, w in ((16, 16), (32, 32), (64, 64), (128, 64)):
        lin2(w_("CODE", H + n, w), w_("CODE", H, w), scale=4.0 ** (n // 16), extra=VAP_X)
    lin("kh", [(1, 1), (6, 0.5)])
    lin("kl", [(1, 1), (6, -0.5)])
    lin("r07", [(0, 1), (7, 1)])
    ts(s("II", 12, 15), s("II", 12, 15), 112, AL.bitwise_and)
    for n in range(3):
        col("pg%d" % n)
    cp(w_("CF", cols["pg0"], 3), s("II", 12, 15))
    lin2(s("BASEW", 32, 48), s("JW", 0, 16), float(C))
    const(s("BASEW", 16, 32), float(C))
    for d in range(3):
        lin2(M("PD%d" % d), M("PI%d" % d), scale=col("r07"))
        k = ts(M("PK%d" % d), s("GI"), col("pg%d" % d), AL.is_equal, col("kh" if high[d] else "kl"), AL.mult)
        nodes[k]["pred"].update(writers(col("kh"), col("kl")))
    dma("y", s("OW"), s("CODE", 0, CWD), 256 * CWD)
    ts(s("OV2", 128, 256), s("OVI"), 8, AL.arith_shift_right)
    ts(s("OV2", 256, 384), s("OVI"), 255, AL.bitwise_and)
    ts(s("OVB", 0, 128), s("OV2", 128, 256), -8.0, AL.add)
    cp(s("OVB", 128, 256), s("OV2", 256, 384))
    dma("y", s("OW", 0, C, p=row(4)), s("OVB", 0, 128), 32768)
    dma("y", s("OW", 0, C, p=row(5)), s("OVB", 128, 256), 32768)
    for q in range(16):
        cp(w_("VAP", 128 * q, 128), s("VA", q, C, 16), extra=VAP_X - 3 * q)
    fill("X", V, VW)
    terms(M("STL"), [(6, None, STALE), (7, None, -STALE)])
    terms(s("ZW", 800, 960), [(0, 15, 1)])
    fill("C256", 0, 256, 256)
    fill("KK", C, CWD)
    lin("t8", [(8, 4096)])
    lin2(s("CW2", C, CWD), s("ONES"), scale=col("t8"))
    terms(s("ZW", 160, 320), [(4, 15, 256), (5, 15, 1)])
    terms(M("BU22"), [(7, None, -2 ** 22)])
    terms(M("BH"), [(7, None, -1), (6, None, 2)])
    terms(M("BL"), [(7, None, 1), (6, None, -1)])
    terms(M("BDE"), [(2, 8, 2 ** 20), (3, 8, 4096), (2, 9, -2 ** 20), (3, 9, -4096)])
    terms(M("NBO"), [(4, 8, -2 ** 20), (5, 8, -4096), (4, 9, 2 ** 20), (5, 9, 4096), (8, 0, 1), (6, 4, 4), (6, 6, 1)])
    terms(M("BO"), [(4, None, 256), (5, None, -1)])
    terms(M("MN"), [(4, 4, -1), (6, 4, 4), (5, 5, 1), (6, 6, 1)])
    terms(sm("SELW"), [(0, None, 1)])
    terms(sm("SELD"), [(4, None, 256), (5, None, 1), (6, None, -1024)])
    terms(sm("SN"), [(13, None, -1)])
    terms(sm("SF"), [(6, None, 1)])
    if NP0 < NP:
        terms(sm("S8"), [(8, None, 1)])
        terms(M("SU"), [(7, 8, 1)])
    terms(M("MO"), [(4, 4, -1), (5, 5, 1)])
    terms(M("BNH"), [(8, None, 2), (9, None, 2)])
    terms(s("ZW", 480, 640), [(4, 15, -256), (5, 15, 1), (8, 15, 1), (9, 15, 1)])
    terms(s("ZW", 640, 800), [(0, 15, -4096)])
    for n, w in (("NID", -1.0 / 256), ("IDS", 1.0 / 256), ("ID16", 16.0)):
        sel(M(n), Z128, [[-1, 128]], AL.not_equal, w, 0)
    sel(M("PERM"), Z128, [[-1, 4], [-4, 32]], AL.not_equal, 1.0, 0)
    iota(s("II", 64, 72), [[16, 2], [32, 4]], 0, 0, False)
    ts(s("ELX", 40, 48), s("II", 64, 72), col("i"), AL.add)
    sel(sm("G8B"), G8, [[0, 8]], AL.is_ge, 0.0, 0)
    sel(s("RS1"), O128, [[0, 8], [1, 16]], AL.not_equal, 0.0, 0, 0)
    iota(s("JI"), [[1, 16], [16, 16]], 0, 0)
    iota(s("J1"), [[1, 256]], 1, 0)
    lin2(s("POS", 128, 144), s("JW", 0, 16), 1.0)
    lin2(s("BASEW", 48, 64), s("JW", 0, 16), float(DV0 - V))
    lin2(s("BASEW", 64, 80), s("JW", 0, 16), float(DV0 - V - 4096))
    lin2(col("g15"), col("g16"), 15.0)
    ts(s("ZW", 320, 480), s("IO", 0, 160), col("g15"), AL.is_equal, col("i"), AL.mult)
    for t in range(4):
        r = 40 * t
        for n, cmp in (("TRI", AL.is_ge), ("TRS", AL.is_gt)):
            o = M("%s%d" % (n, t))
            sel(o, O128, [[1, 128]], cmp, 0.0, r, -1)
            if t:
                c0 = o[1][0][1]
                sel(s("MAT", c0, c0 + 128, p=slice(0, r)), s("ONES", 0, 128, p=slice(0, r)), [[1, 128]], cmp, 0.0, r - 128, -1)
        for n, w in (("PM", 1.0), ("PM4", 4096.0)):
            o = M("%s%d" % (n, t))
            sel(o, Z128, [[1, 128]], AL.not_equal, w, r, -1)
            if t:
                sel(o, o, [[1, 128]], AL.not_equal, w, r - 128, -1)
        for h, last in ((0, 1), (1, 128 - (127 + r) % 128)):
            o = w_("RH", 32 * t + 16 * h, 16)
            iota(o, [[1, 16]], last, 0)
            sel(o, o, [[0, 16]], AL.is_equal, 1.0, -127)
            if h and t:
                sel(o, o, [[0, 16]], AL.not_equal, -127.0, r - 127)

    def first_replicas():
        mmx([(w_("P7", S * d, S), M("PI%d" % d), w_("LA", S * d, S)) for d in range(3)])
        tt(s("NE"), s("P7", 0, 192), XREP, AL.not_equal)
        tt(s("DX"), s("P7", 0, 192), XREP, AL.subtract)
        lin2(s("XR0"), XREP)
        mm(s("P7", 0, 192), M("K1"), AREP)
        mms([(s("P7", 256, 448), M("K3"), AREP)] + [(w_("P7", 256 + S * d, S), M("B7"), w_("NE", S * d, S)) for d in range(3) if high[d]],
            after=writers(M("B7"), s("NE")))
        ts(s("LS"), s("P7", 256, 448), 0.0, AL.is_gt)
        tt(s("LS"), s("P7", 0, 192), s("LS"), AL.mult)
        tt(AREP, AREP, s("LS"), AL.add)

    def replica_digits():
        i = len(done["d"])
        q = DIG[i]
        for h in (2 * i, 2 * i + 1):
            b0 = 16384 + 1024 * (h % NS)
            for x in range(0, 64, MP):
                lin2(w_("GR", b0 + 16 * x, 16 * MP), ind(s("CODE"), w_("VAP", 128 * q + 64 * (h & 1) + x, MP)))
            mms([(w_("P7", 384 + 64 * (h & 1), 64), ID, s("GR", b0 + k, b0 + 1024, 16)) for k in range(16)])
        lin2(w_("MK", 128 * i, 128), s("P7", 384, 512))

    def pair_list():
        nh = PN // 2
        o, c0 = s("P7", 0, nh), nh * len(done["x"])
        mms([(o, M("I48"), w_("PR", c0, nh)), (o, ID, w_("PR", PN + c0, nh))])
        ts(w_("PIX", c0, nh), o, -129.0 * 49, AL.add)

    def pair_mask():
        nh = PN // 2
        o, c0 = s("P7", 0, nh), nh * len(done["m"])
        mms([(o, s("IDF"), w_("VAF", c0, nh))], True, False)
        mms([(o, s("IDF"), w_("VAF", PN + c0, nh))], False, False)
        mms([(o, M("N4096"), w_("PR", c0, nh)), (o, M("N64"), w_("PR", PN + c0, nh))], False)
        ts(w_("MIX", c0, nh), o, 129.0 * 4160, AL.add)
        for x in range(c0, c0 + nh, MP):
            nodes[lin2(w_("MASK", 16 * x, 16 * MP), ind(s("TBM"), w_("MIX", x, MP)))]["push"] = PUSHM

    done = {"d": [], "x": [], "m": []}

    def gap_work(plan):
        for c in plan:
            {"d": replica_digits, "x": pair_list, "m": pair_mask}[c]()
            done[c].append(c)

    def pair_tables():
        for j in range(2):
            vp = w_("VAP", 1024 * j, PN)
            ts(w_("PR", PN * j, PN), vp, 1.0 / 64, AL.mult, 128.5 + 1.0 / 128, AL.add)
            ts(w_("VAF", PN * j, PN), vp, 1.0 if j else 64.0, AL.mult)
        lin2(M("N4096"), ID, scale=-4096.0)
        lin2(M("N64"), ID, scale=-64.0)
        lin2(col("npar"), col("par"), 1.0, -1.0)
        lin2(col("c2"), col("par"), 1.0)
        lin2(col("i0"), col("par"), 2.0 ** -8, -2.0 ** -9)
        B = lambda j: w_("BIN", 64 * j, 64)
        iota(B(1), [[0, 8], [2, 8]], 0, 0)
        ts(B(2), B(1), 0.0, AL.is_equal, col("c2"), AL.mult)
        ts(B(3), B(2), 1.0, AL.max)
        scan(B(0), B(3), s("ZERO", 0, 64), col("i0"), AL.mult, AL.add)
        ts(B(1), B(1), col("r2"), AL.is_equal, col("npar"), AL.max)
        tt(B(2), B(0), B(1), AL.mult)
        ts(s("TF", 144, 152), s("IO", 0, 16, 2), col("r2"), AL.is_equal, col("par"), AL.max)
        for j in range(8):
            lin2(w_("TBM", 64 * j, 64), B(2), scale=w_("TF", 144 + j, 1))
        for j, w in enumerate((1.0, 3.0, 15.0)):
            lin2(col("e%d" % j), col("npar"), 1.0, w)
            for x in range(0, 512 << j, 512):
                lin2(w_("TBM", (512 << j) + x, 512), w_("TBM", x, 512), scale=col("e%d" % j), e=TBE)

    def window_tables():
        lin2(M("I48"), ID, scale=48.0)
        lin2(M("NI"), ID, scale=-1.0)
        for d in range(3):
            ts(M("BP%d" % d), s("GI"), col("pg%d" % d), AL.is_equal, -2.0 ** 22, AL.mult)
        for e in range(8):
            sel(col("bit"), col("bit") if e else col("par"), [[0, 1]], AL.is_gt, 2.0 ** (6 - e), 8 * e, -1)
        iota(s("RW"), [[0, 24], [1, 8], [0, 2]], 0, 0)
        ts(s("RW"), s("RW"), col("r8"), AL.not_equal, 2.0 ** 40, AL.mult)
        sel(s("ZC", 0, 112), s("ZERO", 0, 112), [[1, 112]], AL.not_equal, 1.0, -95, 0)
        sel(s("ZC", 112, 224), s("ONES", 0, 112), [[2, 56], [1000, 2]], AL.is_ge, 0.0, -1090, 0)
        sel(s("ZC", 112, 224), s("ZC", 112, 224), [[-1, 112]], AL.is_ge, 0.0, 95, 0)
        lin2(s("ZC"), s("ZC"), scale=col("bit"))
        ms(s("CUM", 0, 273, 272), 0.0)
        c0 = sm("SELP", 32)[1][0][1]
        lin2(s("SM", c0, c0 + 16, 2), G8, scale=col("npar"))
        lin2(s("SM", c0 + 1, c0 + 16, 2), G8, scale=col("par"))
        lin2(s("SM", c0 + 16, c0 + 32), s("SM", c0, c0 + 16), scale=-1.0)
        for n, top in (("PAIRS", NP), ("PAIR0", NP0)):
            sel(M(n), O128, [[0, 16], [-1, 8]], AL.is_gt, 0.0, top, 0)
        if SG:
            for j in range(SG):
                col("nc%d" % j)
            sel(M("LAST"), O128, [[1, 128]], AL.is_ge, 0.0, 16 * SG - 128, 0)
            iota(col("half"), [[0, 1]], 1, 0)
            sel(col("half"), col("half"), [[0, 1]], AL.is_gt, 0.5, 128 - 16 * SG, -1)
        for k, w in enumerate((-256.0, -0.5, -2 * EPS)):
            sel(M("LOW"), M("LOW") if k else Z128, [[0, 128]], AL.not_equal, w, -k)
        for x in range(0, EW, 480):
            n = min(480, EW - x)
            sel(w_("OHT", x, n), s("CODE", 0, n), [[2, n // 48], [0, 48]], AL.not_equal, 1.0, x // 24, -1)
            sel(w_("OHT", x, n), w_("OHT", x, n), [[0, n // 48], [2, 48]], AL.not_equal, 1.0, 1, -1)
        sel(s("FT", 0, 112), s("ZERO", 0, 112), [[-2, 56], [1000, 2]], AL.not_equal, 128.0, -1000)
        sel(s("FT", 0, 112), s("FT", 0, 112), [[-2, 56], [1000, 2]], AL.not_equal, 8.0, -1001)
        for j in range(1, 4):
            lin2(w_("FT", 112 * j, 112), s("FT", 0, 112), scale=0.5 ** j)

    def lane_numbers():
        mmx([(w_("P1", 16 * i + 8 * h, 8), w_("SR", 128 * h, 128), sm(n)) for h in range(2) for i, n in enumerate(("SELS", "SELC"))])
        lin2(s("SCT"), s("P1", 0, 32))

    def gather_lanes():
        for j in range(4):
            lin2(w_("GR", 1024 * j, 1024), ind(AW, w_("VARS", 64 * j, 64)))

    for m in range(4):
        if m - 1 not in QUICK:
            gather_lanes()
        if m == 0:
            lin2(s("SR"), ind(s("A", 0, CWD), s("LN", 0, 16)))
            dma("y", s("A", 0, V, p=row(2)), s("DEW", 0, V, p=row(4)), 49152, rows=16)
            dma("y", s("A", 0, V, p=row(3)), s("DEW", 0, V, p=row(5)), 49152, rows=16)
        keys = ("P0", "P2" if LANES else "P0")
        for h in range(2):
            mmx([(s(keys[h], 128 * h + k, 128 * h + 128, 16), s("GR", 2048 * h + k, 2048 * h + 2048, 16), s("MAT", mats["SELK"] * 128 + k, mats["SELK"] * 128 + 128, 16)) for k in range(16)])
        if m == 0:
            lane_numbers()
        for x0, x1 in (((0, 8), (8, 16)) if LANES else ((0, 16),)):
            b = keys[x0 // 8]
            scan(s("M1", 16 * x0, 16 * x1), s("RSB", 16 * x0, 16 * x1), s(b, 16 * x0, 16 * x1), 0.0, AL.add, AL.min)
            tt(s("YY", 16 * x0 + 1, 16 * x1), s("M1", 16 * x0, 16 * x1 - 1), s(b, 16 * x0 + 1, 16 * x1), AL.max)
            cp(s("TI", x0, x1), s("M1", 16 * x0 + 15, 16 * x1, 16))
            ts(s("OI", x0, x1), s("TI", x0, x1), 4095, AL.bitwise_and)
            tt(s("EXP", 16 * x0, 16 * x1), ind(s("OI", x0, x1), s("ELX", 0, x1 - x0)), s("MASKR", 16 * x0, 16 * x1), AL.mult)
            mmx([(w_("P1", 64 + 8 * h, 8), w_("EXP", 128 * h, 128), G8) for h in range(x0 // 8, x1 // 8)])
            cp(s("L1", x0, x1), s("P1", 64 + x0, 64 + x1))
            if LANES > 1:
                lin2(s("BE", 16 * x0, 16 * x1), ind(s("BITS"), s("L1", x0, x1)))
                lin2(s("BO", 16 * x0, 16 * x1), ind(s("BITS"), s("L1", x0, x1)), scale=col("od"))
        LIVE = s("TF", 16, 32)
        tt(LIVE, s("M1", 15, 256, 16), s("SCT", 0, 16), AL.is_lt)
        if LANES < 2:
            lin2(s("BE"), ind(s("BITS"), s("L1")))
            lin2(s("BO"), ind(s("BITS"), s("L1")), scale=col("od"))
        if m == 0:
            first_replicas()
        lin2(s("GO"), ind(AW, s("L1")))

        def gram(gg, bank, c0, lo):
            B, pp = ("BE", "BO")[gg & 1], slice(32 * (gg // 2), 32 * (gg // 2) + (32 if gg & 1 else 16))
            mm(w_(bank, c0, 256 - lo), s(B, lo, lo + 128, p=pp), s(B, lo, 256, p=pp), tile=gg // 2)
        place = (lambda gg: gg) if BOG else (lambda gg: gg // 2 + 4 * (gg & 1))
        for gg in range(8):
            gram(gg, "P%d" % (2 + place(gg) // 2), 256 * (place(gg) & 1), 0)
        for gg in range(8):
            gram(gg, "P0" if place(gg) >= 4 else "P6", 128 * (place(gg) % 4), 128)
        scan(s("M2"), s("YY"), s("RSB"), 0.0, AL.min, AL.max)
        ts(s("WL", 0, 16), LIVE, col("pow"), AL.mult)
        ts(s("WL", 16, 24), s("TF", 16, 24), 2.0 ** 62, AL.mult)
        tt(s("TI", 16, 32), s("M2", 15, 256, 16), s("SCT", 0, 16), AL.min)
        tt(s("DO"), s("OI"), s("JT", 16, 32), AL.subtract)
        if not AD:
            tt(s("TMP"), ind(s("DO"), s("ELX", 0, 16)), s("MASKR", 0, 256), AL.mult)
        ts(s("TI", 32, 48), s("TI", 16, 32), 16, AL.arith_shift_right)
        for j, b in enumerate((2, 3, 4, 5, 6, 0)):
            over(w_("TH", 512 * j, 512), s("P%d" % b), 11.0)
        cp(s("VT", 16, 272, 16), s("TI", 32, 48))
        th = lambda gg: 256 * place(gg)
        for gg in range(8):
            mm(w_("P1", 96 + gg, 1), w_("TH", th(gg), 128), w_("WL", gg, 1))
            o1 = w_("P1", 104 + gg, 1)
            mms([(o1, w_("TH", th(gg) + 128, 128), w_("WL", 16 + gg, 1)), (o1, w_("TH", 2048 + 128 * place(gg), 128), w_("WL", 8 + gg, 1))])
        PV = s("P2", 256, 512)
        mms([(PV, M("SV1"), s("GO")), (PV, M("SV2"), s("SR"))] + [(w_("P2", 256 + 128 * h, 128), w_("VT", 16 - i + 128 * h, 128), ID) for h in range(2) for i in range(2)])
        mm(s("P3", 0, 16), s("IDF"), s("BASEW", 0, 16), True, False)
        tt(s("ACT"), s("P1", 96, 112), s("WL", 0, 16), AL.is_lt)
        VAL = w_("VAL", 256 * m, 256)
        lin2(VAL, PV)
        if AD:
            tt(s("DO"), s("DO"), s("ACT"), AL.mult)
            tt(s("EXP", 0, 256), ind(s("DO"), s("ELX", 0, 16)), s("MASKR", 0, 256), AL.mult)
        else:
            tt(s("EXP", 0, 256), ind(s("ACT"), s("ELX", 0, 16)), s("TMP"), AL.mult)
        mms([(w_("P3", 8 * h, 8), w_("EXP", 128 * h, 128), G8) for h in range(2)], False)
        if m < 3:
            mmx([(w_("P2", 8 * h, 8), w_("GO", 128 * h, 128), sm("SELE")) for h in range(2)])
        L2 = w_("L2", 16 * m, 16)
        cp(L2, s("P3", 0, 16))
        cp(ind(AW, L2), VAL)
        landed = send([w_("A", H + S * d, S) for d in range(3)], "LA", 192 * (m + 1), S)
        lands.append(landed)
        if m == 1:
            dma("y", s("X", 0, H), ext(T.xv[:, 0:H]), 737280, after=[landed])
        if m == 2:
            dma("y", s("KK", 0, C), ext(T.kc[:]), 524288, after=[landed])
            dma("y", s("CH0", 0, H), s("CODE", 0, H), 256 * H, after=[landed])
            fill("CH0", H, VW)
        tt(s("TF", 112, 128), s("SCT", 16, 32), s("JT", 0, 16), AL.subtract)
        tt(s("NM", 16, 32), s("TF", 112, 128), s("ACT"), AL.mult)
        lo = 0 if m < 3 else 16
        if m < 3:
            tt(s("TF", 80, 96), s("SCT", 16, 32), LIVE, AL.mult)
            tt(s("TF", 96, 112), s("P2", 0, 16), s("TF", 80, 96), AL.subtract)
            tt(s("TF", 96, 112), s("TF", 96, 112), s("ACT"), AL.mult)
            tt(s("NM", 0, 16), s("TF", 96, 112), s("TF", 80, 96), AL.add)
        tt(s("EXP", 16 * lo, 512), ind(s("NM"), s("ELX", lo, 32)), s("MASKR", 16 * lo, 512), AL.mult)
        mm(s("P4", 0, 192), M("SK"), AREP, True, False)
        mms([(s("P5", 0, 192), M("SD"), AREP), (s("P5", 256, 448), ID, AREP)], True, False)
        mms([(s("P1", 160 + lo, 192), s("IDF"), s("BASEW", 16 + lo, 48))] + [(w_("P1", 160 + 8 * h, 8), w_("EXP", 128 * h, 128), G8) for h in range(lo // 8, 4)])
        cp(s("LN", 32 * (m + 1) + lo, 32 * (m + 2)), s("P1", 160 + lo, 192))
        if m < 3:
            cp(VARS0, ind(s("VA", 0, C + 16), w_("LN", 32 * (m + 1), 16)))
            lin2(s("SR"), ind(s("A", 0, CWD), w_("LN", 32 * (m + 1), 16)))
            lane_numbers()
        cp(ind(s("OW"), w_("LN", 32 * (m + 1) + 16, 16)), VAL)
        LA = lambda d: w_("LA", 192 * (m + 1) + S * d, S)
        mms([(w_("P4", S * d, S), M("PK%d" % d), LA(d)) for d in range(3)], False)
        mms([(w_("P5", S * d, S), M("PD%d" % d), LA(d)) for d in range(3)], False)
        TTm = w_("TT", 192 * m, 192)
        if m in QUICK:
            mmx([(w_("P6", S * d, S), M("PD%d" % d), LA(d)) for d in range(3)])
            tt(AREP, s("P6", 0, 192), AREP, AL.max)
            gather_lanes()
        ts(s("LS"), s("P4", 0, 192), 0.0, AL.is_gt)
        tt(TTm, s("P5", 0, 192), s("LS"), AL.mult)
        tt(AREP, s("P5", 256, 448), TTm, AL.add)
        act(w_("SQ", 192 * m, 192), TTm, AF.Abs)
        if m == 0:
            k0 = len(nodes)
            pair_tables()
            for x in nodes[k0:]:
                x["push"] = PUSHT
            window_tables()
        gap_work(GAPS[m])
    dma("y", s("CH1", 0, H), s("CH0", 0, H), 256 * H, after=[lands[3]])
    dma("y", s("CW"), s("CH0", 0, CWD), 256 * CWD, after=[lands[3]])
    fill("CH1", H, VW)
    for j in range(6):
        b, o = s("P6" if j & 1 else "P7", 0, 480), w_("X", 480 * j, 480)
        mms([(b, ID, o), (b, M("STL"), w_("A", 480 * j, 480))])
        lin2(o, b)

    def changed_digits(lst, n):
        b, o = s("P6", 0, 192), s("T192", 0, 192)
        mms([(b, ID, s("CODE", H, V))] + lst[:3 * (len(lst) > 3)], True, False)
        mms(lst[3 * (len(lst) > 3):], False)
        node({"s": (cost(o, [b], 1) + 0.02, lambda: g.scalar.activation(o[0], b[0], AF.Relu, accum_out=col(n)[0]))}, [o, col(n)], [b])

    def mask_test(c0, n, wc, src=None):
        ts(s("MT", 0, n), src or w_("MK", c0, n), col(wc), AL.subtract, float(0x555555), AL.add)
        ts(w_("MT", 384, n), s("MT", 0, n), 0xAAAAAA, AL.bitwise_and)
        ts(w_("MB", c0, n), w_("MT", 384, n), 0.0, AL.is_gt)

    def piece(win, q, slot, e):
        n = 128 // len(e)
        for x, eng in zip(range(0, 128, n), e):
            lin2(w_("GR", 2048 * slot + 16 * x, 16 * n), ind(win, w_("VAP", 128 * q + x, n)), e={"b": "sv"}.get(eng, eng))

    P96 = slice(0, 96)
    P64 = slice(0, 64)
    EL = 45 * 48

    def pair_window(ch):
        for h in range(2):
            mmx([(s("P1", 64 * (r // 8) + r % 8, 64 * (r // 8) + 64, 8, p=P96), s(ch, r, V, 32), sm("G8B")) for r in range(16 * h, 16 * h + 16)])
        o, i = s("BIN", p=P96), s("P1", 0, 256, p=P96)
        node({"s": act_(o, i, AF.Sign), "v": ts_(o, i, 0.0, AL.is_gt)}, [o], [i])
        for h in range(2):
            mms([(s("P1", 256 + h, 384, 2, p=P96), s("FT", 112 * j + 1 - h, 112 * j + 97 - h, p=P96), s("BIN", 64 * j, 64 * j + 64, p=P96)) for j in range(4)])
        lin2(s("WT", p=P96), s("P1", 256, 384, p=P96))
        n = (EW if PE0 else EL) // len(EB) + 1
        for j, x in enumerate(range(0, EW if PE0 else EL, n)):
            y = min(n, (EW if PE0 else EL) - x)
            mm(s(EB[j], 0, y), s("WT", p=P96), s("OHT", x, x + y, p=P96))
            nodes[lin2(w_("E", x, y), s(EB[j], 0, y), e=EQ[j])]["push"] = PUSHE

    def pair_patch(own, bm, b0, b1):
        k0 = len(nodes)
        act(s("BX", p=P64), s(bm, 0, 384, p=P64), AF.Sign, -1.0, -1.0)
        for h in range(2):
            mms([(s(bm, 384 + h, 512, 2, p=P96), s("ZC", 5 - 2 * d - h, 101 - 2 * d - h, p=P64), s("BX", 128 * d + h, 128 * d + 128, 2, p=P64)) for d in range(3)]
                + [(s(bm, 384 + h, 512, 2, p=P96), s("ZC", 113 - h, 209 - h, p=P64), s("ONES", 0, 64, p=P64))])
        lin2(s("WR", p=P96), s(bm, 384, 512, p=P96), e=EP[0])
        cut = [(b0, 0, 144, EL, EW, 1), (b0, 144, 189, 45, EL, 48), (b1, 0, 45, 46, EL, 48), (b1, 45, 90, 47, EL, 48)]
        for b, x0, x1, lo, hi, st in cut:
            mms([(s(b, x0, x1), s(w, p=P96), s("OHT", lo, hi, st, p=P96)) for w in ("WT", "WR")[1 - own:]])
        for n, (b, x0, x1, lo, hi, st) in enumerate(cut):
            lin2(s("E", lo, hi, st), s(b, x0, x1), e=EP[1 + n])
        for x in nodes[k0:]:
            x["push"] = PUSHE

    def pair_gather(b, calls):
        n = 128 // calls
        for x in range(0, 128, n):
            k = tt(w_("GR", 2048 * (NS + b) + 16 * x, 16 * n), ind(s("E"), w_("PIX", 128 * b + x, n)), w_("MASK", 2048 * b + 16 * x, 16 * n), AL.mult)
            nodes[k]["push"] = PUSHP

    def add(sums, lst, **kw):
        c = sum(max(min(64, l[3]), r[3]) for (o, l, r) in lst) * PECY
        sums.append(node({"p": (c, [(o, l, r, False, False, None) for (o, l, r) in lst])}, [], [x[1] for x in lst] + [x[2] for x in lst],
                         inc=len(lst), after=sums[:1], **kw))

    def pair_flags(b, sums, last, ZB=ZB, **kw):
        z, g0, r0 = ZB[b % len(ZB)], 2048 * (NS + b), 512 * (b & 1)
        if RRC:
            mms([(s(z, 0, 256), Z128, s("ONES")), (s(z, 256, 512), M("LOW"), s("ONES"))], True, False)
            mms([(s(z, k, 512, 16), s("GR", g0 + k, g0 + 2048, 16), sm("SELP", 32)) for k in range(16)], False)
            lin2(w_("RR", r0, 512), s(z), 128.0 + EPS)
        else:
            mmx([(s(z, k, 256, 16), s("GR", g0 + k, g0 + 2048, 16), w_("SM", sm("SELP", 32)[1][0][1], 16)) for k in range(16)])
            lin2(w_("RR", r0, 256), s(z, 0, 256), 128.0 + EPS, e=RRE[0])
            lin2(w_("RR", r0 + 256, 256), s(z, 0, 256), -128.5 - EPS, -1.0, e=RRE[1])
        o = s("P0", b, 128, 8)
        if last:
            c0 = 272 * (b & 1)
            scan(w_("CUM", c0 + 1, 256), w_("RR", r0, 256), w_("RR", r0 + 256, 256), 0.0, AL.add, AL.add)
            add(sums, [(o, ID, s("CUM", c0 + 16, c0 + 257, 16)), (o, M("NI"), s("CUM", c0, c0 + 256, 16))], **kw)
        else:
            for h in range(2):
                add(sums, [(o, ID, s("RR", r0 + 256 * h + k, r0 + 256 * h + 256, 16)) for k in range(16)], **kw)

    changed_digits([(s("P6", 0, 192), M("BU22"), w_("SQ", 192 * m, 192)) for m in range(4)], "wd")
    others = lambda b: mm(s(b, 0, 384, p=P64), s("ZW", 16, 80, p=P64), s("RW", p=P64), True, False)
    others("P2")
    for ms_ in ((0, 1, 2), (3,)):
        mms([(s("P2", 128 * d, 128 * d + 128, p=P64), w_("SQ", 192 * m + S * d, S), M("BU22")) for m in ms_ for d in range(3)], False, 3 in ms_)
    if NP0 < NP:
        mms([(s("P3", 256, 448), M("SU"), w_("SQ", 192 * m, 192)) for m in range(4)])
        lin2(s("CH0", H, V), s("P3", 256, 448))
    pair_patch(0, "P2", "P1", "P4")
    for c0 in range(0, 128 * ND, 384):
        mask_test(c0, min(384, 128 * ND - c0), "wd")
    rest = [(b + 8 * h, (NS + b, NS + NP1 + b - NP0 if NP1 < NP else NS - 1 - b + NP0)[h]) for b in range(NP0, NP1) for h in range(2)]
    for q, slot in rest:
        piece(s("CH0"), q, slot, "bb")
    if rest:
        lin2(s("CH0", H, V), s("ZERO", 0, 192))
    for b in range(NP0):
        pair_gather(b, 2)
    sums = [mm(s("P0", 0, 128), M("ID16"), M("PAIR0"), True, False)]
    for h in range(2):
        add(sums, [(s("P0", q, 128, 16), s("OW", q, C, 16), sm("SF")) for q in range(8 * h, 8 * h + 8)])
    for i0 in range(0, ND, 3):
        add(sums, [(s("P0", DIG[i], 128, 16), w_("MB", 128 * i, 128), sm("G8B")) for i in range(i0, min(ND, i0 + 3))])
    for q, slot in rest:
        add(sums, [(s("P0", q, 128, 16), s("GR", 2048 * slot + k, 2048 * slot + 2048, 16), sm("S8")) for k in range(16)])
    for n in range(NP0):
        pair_flags(n, sums, n >= NP0 - SCAN0, ("P1", "P2"))
    mms([(s("P0", 0, 16), Z128, s("ZERO", 0, 16))], False, True, after=sums)
    mms([(s("P4", 0, 128), slide(1, r), s("OW", r, C, 16)) for r in range(16)])
    ts(s("LO128"), s("P4", 0, 128), float(C), AL.add)
    for j in range(4):
        lin2(w_("GV", 512 * j, 512), ind(AW, w_("LO128", 32 * j, 32)))
        b, o = s("P4" if j & 1 else "P5"), w_("CW2", 512 * j, 512)
        mms([(b, M("NBO"), w_("A", 512 * j, 512)), (b, M("MO"), w_("OW", 512 * j, 512)), (b, M("BDE"), w_("GV", 512 * j, 512))])
        node({"s": act_(o, b, AF.Relu), "v": ts_(o, b, 0.0, AL.max)}, [o], [b])
    mms([(s("P7", 256, 384), slide(3, r), w_("CW2", 128 * r, 128)) for r in range(16)])
    ts(s("FF", 128, 256), s("P7", 256, 384), float(V), AL.add, float(V), AL.min)
    dma("y", ext(T.yo[:]), s("FF", 128, 256), 65536)
    mms([(w_("P6", S * d, S), M("BH" if high[d] else "BL"), w_("A", H + S * d, S)) for d in range(3)] + [(s("P6", 256, 448), M("STL"), AREP)],
        after=writers(M("BH"), M("BL")))
    o, i = s("NE"), s("P6", 0, 192)
    node({"s": act_(o, i, AF.Relu), "v": ts_(o, i, 0.0, AL.max)}, [o], [i])
    o, i = s("BX", 0, 192), s("P6", 256, 448)
    node({"s": act_(o, i, AF.Relu), "v": ts_(o, i, 0.0, AL.max)}, [o], [i])
    tt(s("NE"), s("NE"), s("DX"), AL.mult)
    mms([(s("P6", 0, 192), ID, s(n, 0, 192)) for n in ("XR0", "NE", "BX")])
    lin2(XREP, s("P6", 0, 192))
    lin2(s("GM"), s("LS"), 1.0, -1.0)
    GM = s("P2", 256, 448)
    mm(GM, ID, s("GM"))

    SBX = (T.SB[:, :, 0:S], [("SB", 0, 1, ALL)], [], 192, B16, "sbuf")
    SBA = (T.SB[:, :, S:2 * S], [("SB", 1, 2, ALL)], [], 192, B16, "sbuf")

    def part(d, lo, hi):
        return (T.SB[:, d, S * lo:S * hi], [("SB", lo, hi, ALL)], [], S * (hi - lo), B16, "sbuf")

    def strengths(t):
        u = t & 1
        CG, LOD = w_("CG", 256 * u, 256), w_("LO", 16 + 16 * u, 16)
        mmx([(w_("P7", 8 * h, 8), w_("CG", 256 * u + 128 * h, 128), sm("SELW")) for h in range(2)])
        for j in range(0, 256, WP):
            lin2(w_("GW", 16 * j, 16 * WP), ind(AW, w_("VARS", 256 * u + j, WP)), e=W3 if t == 3 else "sv")

        def turn(c0, h, n):
            return [(s("P5", c0 + 128 * h + k, c0 + 128 * h + 128, 16), s("GW", 2048 * h + k, 2048 * h + 2048, 16), sm(n)) for k in range(16)]
        for h in range(2):
            mms([(w_("P5", 256 + 128 * h, 128), w_("CG", 256 * u + 128 * h, 128), M("BO"))] + turn(256, h, "SELD"))
        ts(s("EQ"), s("P5", 256, 512), 0.0, AL.is_equal, 256.0, AL.mult)
        mms([(s("P5", 0, 256), ID, s("EQ"))] + turn(0, 0, "SELW") + turn(0, 1, "SELW"))
        scan(s("M1"), s("RSB"), s("P5", 0, 256), 0.0, AL.add, AL.min)
        tt(s("VT", 16, 272, 16), s("M1", 15, 256, 16), s("P7", 0, 16), AL.min)
        mms([(s("P7", 256, 512), M("MN"), CG)] + [(w_("P7", 256 + 128 * h, 128), w_("VT", 16 + 128 * h, 128), ID) for h in range(2)])
        lin2(s("T1"), s("P7", 256, 512))
        cp(ind(AW, LOD), s("T1"))
        tt(SBA, AREP, GM, AL.mult)

    def take_w(base, w):
        mms([(w_("P7", 16 + S * d, S), ID, part(d, 1, 2)) for d in range(3)] + [(w_("P7", 16 + S * d, S), M("PI%d" % d), w_("LP", base + w * d, S)) for d in range(3)])
        lin2(AREP, s("P7", 16, 208))

    for t in range(4):
        u = t & 1
        CH, CHREP = s("CH%d" % u), s("CH%d" % u, H, V)
        ts(s("F"), s("P0", 0, 128), 0.0, AL.is_gt)
        scan(s("IP"), s("RS1"), s("F"), 0.0, AL.mult, AL.add)
        mm(s("P1", 0, 8), M("TRI%d" % t), s("IP", 15, 128, 16))
        lin2(s("CR"), ind(s("IP"), s("ELX", 32, 40)))
        mms([(s("P2", 0, 128), s("F"), M("PM4%d" % t)), (s("P2", 0, 128), s("IP"), M("PM%d" % t)), (s("P2", 0, 128), s("CR"), M("TRS%d" % t))])
        if SG:
            mm(s("P4", 256, 256 + SG), M("TRI%d" % t), s("IP", 143 - 16 * SG, 128, 16))
            lin2(w_("CF", cols["nc0"], SG), s("P4", 256, 256 + SG), 0.5, -1.0, e="s")
            mm(s("P3", 0, 32), M("LAST"), w_("RH", 32 * t, 32), True, False)
        for gg in range(8):
            if gg < 8 - SG:
                ts(w_("CMP", 256 * gg, 256), s("JI"), w_("P1", gg, 1), AL.is_ge)
            else:
                act(w_("CMP", 256 * gg, 256), s("JI"), AF.Sign, col("nc%d" % (gg - 8 + SG)))
        lin2(s("POS", 0, 128), s("P2", 0, 128), -4096.0)
        lst = [(s("P3", j, 32, 16), s("CMP", j, 2048, 16), s("RH", 32 * t + j, 32 * t + 32, 16)) for j in range(16)]
        if SG:
            mms(lst, False)
            ts(s("LB"), s("P3", 0, 16), col("half"), AL.mult)
            lin2(s("BC"), s("P3", 16, 32), float(40 * t), col("half"))
        else:
            mmx(lst)
            cp(s("LB"), s("P3", 0, 16))
            lin2(s("BC"), s("P3", 16, 32), float(40 * t))
        tt(s("OH"), ind(s("POS"), s("LB")), s("J1"), AL.is_equal)
        mms([(s("P1", 16, 32), slide(2, r), s("OH", r, 256, 16)) for r in range(16)] + [(s("P1", 16, 32), M("ID16"), s("BC"))])
        CL, LO, LOD, PS = s("CL"), s("LO", 0, 16), w_("LO", 16 + 16 * u, 16), s("P4", 0, 256)
        CG, c0 = w_("CG", 256 * u, 256), 256 * u
        cp(CL, s("P1", 16, 32))
        cp(w_("VARS", c0, 256), ind(s("VA"), CL))
        lin2(CG, ind(s("CW2"), CL))
        lin2(s("KR"), ind(s("KK"), CL))
        mms([(s("P3", 32, 48), slide(3, r), s("CG", c0 + r, c0 + 256, 16)) for r in range(16)])
        tt(s("TF", 0, 16), s("P3", 32, 48), s("BASEW", 48, 64), AL.min)
        ts(LO, s("TF", 0, 16), float(V), AL.add)
        lin2(s("XO"), ind(XW_, LO), scale=1.0 / 256)
        for j, n in zip(XP[:-1], XP[1:]):
            lin2(s("GR", 16 * j, 16 * n), ind(XW_, s("VARS", c0 + j, c0 + n)))
        GS = s("GS")
        mm(s("P2", 0, 256), ID, s("XO"))
        for bank, x0, x1 in ((("P6", 0, 128), ("P4", 128, 256)) if HALVES else (("P4", 0, 256),)):
            for x in range(x0, x1, 64):
                if x == x1 - 64:
                    mms([(s(bank, lo, hi), l, s(b, o + lo, o + hi)) for lo, hi in ((x0, x), (x, x1))
                         for l, b, o in ((M("BNH"), "CG", c0), (M("IDS"), "KR", 0), (ID, "XO", 0))], False, False)
                mms([(w_(bank, x, 64), M("NID"), s("GR", 16 * x + k, 16 * x + 1024, 16)) for k in range(16)], x == x0, x == x1 - 64)
            PS, GG = s(bank, x0, x1), s("GG", x0, x1)
            ts(s("FL", x0, x1), PS, -0.498, AL.add)
            tt(s("NX", x0, x1), PS, s("FL", x0, x1), AL.subtract)
            node({"s": act_(GG, PS, AF.Relu, 640.0), "v": ts_(GG, PS, -640.0, AL.is_ge)}, [GG], [PS])
            act(s("GS", x0, x1), PS, AF.Sign, 640.0)
            tt(s("NEQ", x0, x1), s("P2", x0, x1), s("NX", x0, x1), AL.not_equal)
            tt(ind(CH, s("LO", x0 // 16, x1 // 16)), s("NEQ", x0, x1), GG, AL.mult)
        send([w_("CH%d" % u, H + S * d, S) for d in range(3)], "LC", 192 * t, S)
        DOWN = ("OW", "CW")[u]
        cp(ind(s(DOWN), CL), GS)
        mms([(s("P3", 48, 64), s("IDF"), s("TF", 0, 16))], True, False)
        mms([(s("P3", 48, 64), slide(4, r), s("GS", r, 256, 16)) for r in range(16)], False)
        tt(s("TF", 48, 64), s("P3", 48, 64), s("BASEW", 64, 80), AL.min)
        if t:
            strengths(t - 1)
        ts(LOD, s("TF", 48, 64), float(V + 4096), AL.add)
        tt(ind(XW_, LOD), s("NX"), s("C256"), AL.mult)
        tt(SBX, XREP, GM, AL.mult)
        if t:
            send([part(d, 0, 2) for d in range(3)], "LP", 384 * t, 128, XW_X)
        else:
            send([part(d, 0, 1) for d in range(3)], "LP", 0, S, XW_X)
        nodes[sends[-1]]["push"] = PUSHX
        left = lambda j: (32 - j) * 0.5 * 1024 * GATHER * CY
        pair_window("CH%d" % u)
        k0 = len(nodes)
        for i in range(EARLY):
            piece(CH, SINGLE[i], i, SCALLS[i])
        for k in range(k0 + HOLD[0], len(nodes)):
            nodes[k]["pred"].add(k0 - HOLD[1])
        if PE0:
            pair_gather(NP - 1, PCALLS[t == 3][NP - 1])
        LC = lambda d: w_("LC", 192 * t + S * d, S)
        others("P6")
        mms([(s("P6", 128 * d, 128 * d + 128, p=P64), LC(d), M("BP%d" % d)) for d in range(3)], False)
        pair_patch(1, "P6", "P3", "P4")
        mms([(s("P2", 0, 192), ID, CHREP)] + [(w_("P2", S * d, S), M("PI%d" % d), LC(d)) for d in range(3)])
        lin2(CHREP, s("P2", 0, 192))
        if EARLY or PE0:
            changed_digits([(w_("P6", S * d, S), M("BP%d" % d), LC(d)) for d in range(3)], "wd")
            d0, d1 = ND - NS - 2 * PE0, ND - NS + EARLY
            mask_test(128 * d0, 128 * (d1 - d0), "wd")
        for i in range(EARLY, NS):
            piece(CH, SINGLE[i], i, SCALLS[i])
        for b in range(NP - PE0):
            pair_gather(b, PCALLS[t == 3][b])
        sums = [mms([(s("P0", 0, 128), ID, s("F")), (s("P0", 0, 128), M("ID16"), M("PAIRS"))], True, False)]
        for h in range(2):
            add(sums, [(s("P0", q, 128, 16), s(DOWN, q, C, 16), sm("SN")) for q in range(8 * h, 8 * h + 8)])
        add(sums, [(s("P0", DIG[i], 128, 16), w_("MB", 128 * i, 128), sm("G8B")) for i in range(d0, d1)])
        for n, (kind, i) in enumerate(zip(SUMS[::2], map(int, SUMS[1::2]))):
            extra = FX * left(32 * (n + 1) // (NS + NP))
            if kind == "p":
                pair_flags(i, sums, i >= NP - SCANS, extra=extra)
            else:
                add(sums, [(s("P0", SINGLE[i], 128, 16), s("GR", 2048 * i + k, 2048 * i + 2048, 16), sm("G8B")) for k in range(16)], extra=extra)
        mms([(s("P0", 0, 16), Z128, s("ZERO", 0, 16))], False, True, after=sums)
        wx = 128 if t else S
        mms([(w_("P6", S * d, S), ID, part(d, 0, 1)) for d in range(3)] + [(w_("P6", S * d, S), M("PI%d" % d), w_("LP", 384 * t + wx * d, S)) for d in range(3)])
        lin2(XREP, s("P6", 0, 192))
        if t:
            take_w(384 * t + S, 128)
        if t < 2:
            fill("CH%d" % u, 0, VW)
            fill(DOWN, 0, C)
    strengths(3)
    send([part(d, 1, 2) for d in range(3)], "LP", 384 * 4, S)
    nodes[sends[-1]]["push"] = PUSH
    take_w(384 * 4, S)
    for r0 in range(0, 15, 5):
        mms([(s("P5", 0, 192), slide(5, r), w_("A", 192 * r, 192)) for r in range(r0, r0 + 5)], r0 == 0, False)
    mm(s("P5", 0, 192), slide(5, 15), AREP, False, True)
    lin2(s("YW"), s("P5", 0, 192))
    nodes[dma("y", ext(T.yw[:]), s("YW"), 98304)]["push"] = PUSHY
    for lo, hi in ((0, 960), (960, 1920), (1920, H), (H, V)):
        ts(s("YB", lo, hi), s("X", lo, hi), 256.0, AL.min)
    nodes[dma("y", ext(T.y[:]), s("YB"), 786432)]["push"] = PUSHY
    ts(s("F"), s("P0", 0, 128), 0.0, AL.is_gt)
    mm(s("P1", 0, 128), s("F"), M("PERM"))
    o, i = s("POS", 0, 128), s("P1", 0, 128)
    node({"v": (cost(o, [i]), lambda: g.vector.transpose(o[0], i[0]))}, [o], [i])
    lin2(s("FF", 0, 128), ind(s("POS", 0, 128), s("ELX", 40, 48)))
    for h in range(2):
        dma("ys"[h], ext(T.yf[h:8:2, :]), w_("FF", 64 * h, 64), 32768)
    issue()
